import numpy as np, ml_dtypes
CORES = [2,6,10,14,18,22,26,30]
N = 8
import mx_ref
BF = ml_dtypes.bfloat16
def gentries(a):
    return np.ascontiguousarray(a.reshape(8, 16, -1).transpose(0, 2, 1)).reshape(8, -1)
def gtable(e):
    e = np.asarray(e); return np.ascontiguousarray(e.reshape(8, -1, 16).transpose(0, 2, 1)).reshape(128, -1).astype(np.int32)
def gcols(t, e):
    v = np.concatenate([t.reshape(8, 16, -1, 4), np.zeros((8, 16, 1, 4), BF)], axis=2)
    return np.ascontiguousarray(np.stack([v[g][:, e[g]] for g in range(8)])).reshape(128, -1)
def pick(q, e):
    c = np.concatenate([q[0].reshape(128, -1, 4), np.zeros((128, 1, 4), np.uint8)], axis=1); s = np.concatenate([q[1], np.ones((16, 1), np.uint8)], axis=1)
    return (np.ascontiguousarray(c[:, e].reshape(128, -1)), np.ascontiguousarray(s[:, e]))
def join(*qs):
    return (np.concatenate([q[0] for q in qs], axis=1), np.concatenate([q[1] for q in qs], axis=1))
def put(q, e, v):
    c, s = q[0].reshape(128, -1, 4).copy(), q[1].copy(); c[:, e] = v[0].reshape(128, -1, 4); s[:, e] = v[1]
    return (c.reshape(128, -1), s)
def pk(c, s):
    return (np.ascontiguousarray(c), mx_ref.live(s))
def emit(q):
    return q[0], q[1]
def packed(v, rng):
    q = [mx_ref.quantize(np.ascontiguousarray(v[r])) for r in range(N)]
    return np.stack([a for a, b in q]), np.stack([mx_ref.plane(b, rng) for a, b in q])
def values_of_codes():
    e, c = np.zeros((128, 128, 4), np.float32), np.zeros((128, 2, 4), np.uint8)
    e[np.arange(128), np.arange(128), 0] = 1
    c[:127, :, 0] = np.arange(256).reshape(2, 128).T[:127]
    return mx_ref.matmul(mx_ref.quantize(e.reshape(128, 512).astype(BF)), (c.reshape(128, 8), np.full((16, 2), 127, np.uint8))).T.reshape(-1).astype(np.float64)
CODE_VALUE, SCALE_VALUE = values_of_codes(), 2.0 ** (np.arange(256) - 127.0)
def decode(q):
    return (CODE_VALUE[q[0]].reshape(16, 8, -1, 4) * SCALE_VALUE[q[1]][:, None, :, None] + 0.0).reshape(128, -1).astype(np.float32)
def f(rng, *shape):
    return mx_ref.flush((rng.standard_normal(shape, dtype=np.float32) * np.exp2(rng.integers(-2, 3, shape[:-1] + (1,)))).astype(BF))
def wide(rng, *shape, cols=0):
    v = rng.standard_normal(shape, dtype=np.float32) * np.exp2(rng.integers(-12, 13, shape)).astype(np.float32)
    if cols: v *= np.repeat(np.exp2(rng.integers(-cols, cols + 1, shape[:-2] + (1, shape[-1] // 4))) * (rng.random(shape[:-2] + (1, shape[-1] // 4)) > 0.0625), 4, axis=-1).astype(np.float32)
    return mx_ref.flush(v.astype(BF))
C, M, R = 256, 128, 3
def numbers_of(rng):
    return {"x": np.array(f(rng, N, 128, 4 * C)), "u": np.array(f(rng, N, 128, 512)), "v": np.array(f(rng, N, 128, 512))}
def shuffled(rng):
    return np.argsort(rng.random((N, 8, C)), axis=2)
def stored(t):
    return {"cf": np.stack([gtable(t[r]) for r in range(N)])}
def weights(rng, w):
    c, p = packed(np.ascontiguousarray(w).reshape(N, 128, 2048), rng)
    return {"wc": c, "ws": p}
def layers(rng, still=[]):
    w = np.array(f(rng, N, 128, 2048)).reshape(N, 8, 16, 4, 8, 16, 4)
    for i in still:
        w[:, :, i] = 0
        w[:, :, :, :, :, i] = 0
    return weights(rng, w)
def setup_inputs(rng):
    return {**numbers_of(rng), **stored(shuffled(rng)), **layers(rng)}
def setup_inputs_ties(rng):
    d = numbers_of(rng)
    x = d["x"].reshape(N, 8, 16, C, 4)
    x[:, :, :2] = 0
    x[:, :, 0, :, 0] = rng.integers(0, 4, (N, 8, C)).astype(np.float32).astype(BF)
    x[:, :, 1, :, 0] = rng.integers(0, 3, (N, 8, C)).astype(np.float32).astype(BF)
    u = d["u"].reshape(N, 128, 128, 4)
    u[:, :, ::16] = 0
    u[:, :, 1] = 0
    o = rng.permutation(N)
    for r in range(N):
        s = 0.0 if r == o[0] else -1.0 if r == o[1] else 1.0
        for h in range(0, 128, 16): u[r, h, h, 0] = s
        u[r, 1, 1, 0] = s
    return {"x": x.reshape(N, 128, 4 * C), "u": u.reshape(N, 128, 512), "v": d["v"], **stored(shuffled(rng)), **layers(rng, [0, 1])}
def setup_inputs_near(rng):
    d = numbers_of(rng)
    o = rng.permutation(N) % 4
    c = np.where(o % 2 == 0, 1.0, -1.0)
    x = d["x"].astype(np.float32).reshape(N, 8, 16, C, 4)
    x[:, :, 0] = 0
    x[:, :, 8:] = 0
    x[:, :, 0, :, 0] = c[:, None, None]
    s = rng.integers(0, 16, (N, 8, C))
    x[:, :, 8] = ((s[:, :, :, None] >> np.arange(4)) & 1) * np.exp2(np.arange(4) - 23.0)
    x[:, :, 11, :, 0] = 2.0 ** -10
    u = d["u"].reshape(N, 128, 128, 4)
    u[:, :, ::16] = 0
    u[:, :, 1] = 0
    for r in range(N):
        for g in 1 + rng.permutation(7)[:4]: x[r, g, 0, rng.integers(C), 0] = c[r] * 2.0 ** 29
        if o[r] == 1: x[r, 0, 0, rng.integers(C), 0] = -2.0 ** 29
        if o[r] == 3:
            i = rng.integers(0, 2, (8, C))
            x[r, :, 8:] = 0
            x[r, :, 10, :, 0] = (1.0 + 0.125 * i) * 2.0 ** -30
            x[r, :, 12, :, 0] = (1.125 - 0.125 * i) * 2.0 ** -30
        k = 2.0 ** -30 if o[r] == 2 else 1.0
        for a, h in [(0, 1)] + [(h, h) for h in range(0, 128, 16)]:
            if o[r] == 3:
                u[r, a + 10, h, 0] = 1.125 * 2.0 ** -30
                u[r, a + 12, h, 0] = 2.0 ** -30
            else:
                u[r, a, h, 0] = k
                u[r, a + 8, h] = k
                u[r, a + 11, h, 0] = k
    return {"x": x.reshape(N, 128, 4 * C).astype(BF), "u": u.reshape(N, 128, 512), "v": d["v"], **stored(shuffled(rng)), **layers(rng, [0] + [8, 9, 10, 11, 12, 13, 14, 15])}
def swings(rng):
    h, j, a = np.zeros(C, int), 0, 200
    while j < C:
        i = np.arange(min(int(rng.integers(10, 25)), C - j))
        n = np.where((i > 8) & (rng.random(len(i)) < 0.25), rng.integers(2, np.maximum(i, 3)), i)
        h[j:j + len(i)] = (1 - 2 * (i % 2)) * (a - 8 * n)
        j, a = j + len(i), a + 1
    return h
def setup_inputs_deep(rng):
    d = numbers_of(rng)
    x = d["x"].reshape(N, 8, 16, C, 4)
    o = rng.permutation(N)
    t = np.arange(C) - C // 2
    small = (1.0 + (2 * rng.integers(0, 64, (N, 8, 8, C, 4)) + 1) * 2.0 ** -7) * np.exp2(-rng.integers(8, 15, (N, 8, 8, C, 4)).astype(np.float64))
    small = small * rng.choice([-1.0, 1.0], small.shape)
    small[:, :, 0, :, 0] = np.where(rng.random((N, 8, C)) < 0.5, 1.875, 1.96875)
    x[:, :, 8:] = small.astype(np.float32).astype(BF)
    x[:, 0, 0] = 0
    u = d["u"].reshape(N, 128, 128, 4)
    u[:, :, 1] = 0
    u[:, 0, 1, 0] = 16
    u[:, 0, 1, 1] = 1
    for r in range(N):
        h = t if r == o[0] else -t if r == o[1] else swings(rng)
        x[r, 0, 0, :, 0] = (np.sign(h) * (np.abs(h) // 16)).astype(np.float32).astype(BF)
        x[r, 0, 0, :, 1] = (np.sign(h) * (np.abs(h) % 16)).astype(np.float32).astype(BF)
    return {"x": x.reshape(N, 128, 4 * C), "u": u.reshape(N, 128, 512), "v": d["v"], **stored(shuffled(rng)), **layers(rng)}
def setup_inputs_ends(rng):
    d = numbers_of(rng)
    o = (np.arange(N) + int(rng.integers(N))) % 4
    x = np.zeros((N, 8, 16, C, 4))
    u = d["u"].reshape(N, 128, 128, 4)
    u[:, :, ::16] = 0
    t = shuffled(rng)
    w = np.zeros((N, 128, 4, 128, 4), np.float32)
    i = np.arange(128)
    for r in range(N):
        sign = rng.permutation(8) % 2 * 2.0 - 1.0
        wave = 2.0 ** 30 * (0.9 + 0.1 * rng.random((128, 8, 4)))
        u[r, :, 1] = 2.0 ** -30 if o[r] == 3 else 2.0 ** 30
        if o[r] == 0:
            x[r] = -2.0 ** 30 * (0.9 + 0.1 * rng.random((8, 16, C, 4)))
            u[r, :, ::16] = wave.astype(np.float32).astype(BF)
            t[r] = np.arange(C)
        if o[r] == 1:
            x[r] = 2.0 ** 30 * np.where(rng.random((8, 16, C, 4)) < 0.125, 0.8125, 0.875) * (rng.permutation(C) % 2 * 2.0 - 1.0)[:, None]
            u[r, :, ::16] = (wave * sign[:, None]).astype(np.float32).astype(BF)
            for b in range(4): w[r, i, b, i, b] = rng.choice([-1.0, 1.0], 128)
        if o[r] == 2:
            x[r] = 2.0 ** 30
            x[r, rng.permutation(8)[:4]] *= np.where(rng.random((4, 1, C, 1)) < 0.5, 0.875, 1.0)
            t[r] = np.arange(C)[::-1]
            for g in range(8): u[r, 16 * g:16 * g + 16, 16 * g] = sign[g] * 2.0 ** 30
        if o[r] == 3:
            x[r] = 2.0 ** -30 * (1.0 + 0.125 * rng.integers(0, 8, (8, 16, C, 4)))
            t[r, ::2] = np.arange(C)
            t[r, 1::2] = np.arange(C)[::-1]
            for g in range(8): u[r, 16 * g:16 * g + 16, 16 * g] = 2.0 ** -30
    d["v"] = (np.where(d["v"] < 0, -1.0, 1.0) * np.where(rng.permutation(N) % 2, 2.0 ** -30, 2.0 ** 30)[:, None, None]).astype(np.float32).astype(BF)
    return {"x": x.astype(np.float32).reshape(N, 128, 4 * C).astype(BF), "u": u.reshape(N, 128, 512), "v": d["v"], **stored(t), **weights(rng, w.astype(BF))}
def setup_inputs_spread(rng):
    d = setup_inputs(rng)
    d["x"] = wide(rng, N, 128, 4 * C, cols=6)
    return d
def check_inputs(d):
    b = []
    for k in ("x", "u", "v"):
        a = np.abs(d[k].astype(np.float32))
        if not (np.isfinite(a).all() and ((a == 0) | (a >= 2.0 ** -30) & (a <= 2.0 ** 30)).all()): b.append("a value of " + k)
    none, least, most = [emit(mx_ref.quantize(np.full((128, 16), k, np.float32).astype(BF)))[1][0, 0] for k in (0.0, 2.0 ** -30, 2.0 ** 30)]
    for r in range(N):
        if (np.sort(gentries(d["cf"][r]), axis=1) != np.arange(C)).any(): b.append("cf: a group hasn't every column once")
        if ((d["wc"][r] == 0x7F) | (d["wc"][r] == 0xFF)).any(): b.append("wc: a code that is no number")
        s = mx_ref.live(d["ws"][r])
        if ((s != none) & ((s < least) | (s > most))).any(): b.append("ws: a scale out of range")
    return b
def turning(h):
    t = np.arange(C)
    e, found = np.zeros(C, np.int64), []
    for i in range(7):
        inside = (t >= e[:, None]) & (t <= t[:, None])
        s = np.where(inside, h if i % 2 == 0 else -h, np.float32(-np.inf))
        e = C - 1 - np.argmax(s[:, ::-1], axis=1)
        found.append(e)
    found = np.stack(found + [t])
    return found, np.argmax(found == t, axis=0)
def reference(x, u, v, cf, wc, ws):
    qu = [mx_ref.quantize(u[r]) for r in range(N)]
    lay = [pk(wc[r], ws[r]) for r in range(N)]
    now = [x[r] for r in range(N)]
    reads = [gentries(cf[r]) for r in range(N)]
    for t in range(R):
        blend, low, sent = [], [], []
        for r in range(N):
            q = mx_ref.quantize(now[r])
            own = decode(q).astype(BF)
            s = mx_ref.matmul(qu[r], q) + np.float32(0.0)
            e, depth = turning(s[1])
            at = np.take_along_axis(e, np.maximum(depth - np.arange(9)[:, None], 0), axis=0)
            a = np.take_along_axis(reads[r], at[:8], axis=1)
            b = np.take_along_axis(reads[r], at[1:], axis=1)
            z = ((gcols(own, a).astype(np.float32) + gcols(own, b).astype(np.float32)) * np.float32(0.5)).astype(BF)
            o = np.argsort(-s[::16], axis=1, kind="stable")
            l, d = o[:, :M], o[:, C - M:]
            sent.append(mx_ref.quantize(gcols(z, l)))
            other = np.tile(np.arange(C), (8, 1))
            np.put_along_axis(other, l, d, axis=1)
            np.put_along_axis(other, d, l, axis=1)
            reads[r] = np.take_along_axis(other, reads[r], axis=1)
            blend.append(z)
            low.append(d)
        for r in range(N):
            came = sent[(r - 1) % N]
            made = np.stack([mx_ref.matmul(pick(lay[r], np.arange(128 * b, 128 * b + 128)), came) * np.float32(0.03125) for b in range(4)], axis=2).reshape(8, 16, M, 4)
            z = blend[r].astype(np.float32).reshape(8, 16, C, 4)
            for g in range(8): z[g][:, low[r][g]] = made[g] + z[g][:, low[r][g]]
            now[r] = z.reshape(128, 4 * C).astype(BF)
    y, op = np.zeros((N, 128, C), np.float32), np.zeros((N, 8, C), np.float32)
    oc, osc = np.zeros((N, 128, 4 * C), np.uint8), np.zeros((N, 16, C), np.uint8)
    for r in range(N):
        q = mx_ref.quantize(now[r])
        y[r] = mx_ref.matmul(mx_ref.quantize(v[r]), q)
        op[r] = reads[r]
        oc[r], osc[r] = emit(q)
    return {"y": y, "op": op, "oc": oc, "osc": osc}

@@ -1,0 +1,409 @@
+from concourse.mybir import dt, AluOpType as A, ActivationFunctionType as AF
+
+ROUNDS = 3
+ZC = 384
+WIN = 400
+XS = (0, 1)
+SPLIT, L1, L2 = 4, 3, 5
+
+SCRATCH = {}
+PSUM = ["p%d" % i for i in range(8)]
+for _n in PSUM:
+    SCRATCH[_n] = ("psum", [128, 512], "float32")
+for _n, _c in [("u", 128), ("v", 128), ("w", 512), ("us", 384), ("x", 256), ("eb", 512), ("sa", 128), ("k", 128), ("hs", 128), ("h", 256),
+               ("w0", 256), ("w1", 256), ("w2", 256), ("w3", 256), ("eq", 256), ("kt1", 256), ("kt2", 256),
+               ("e0", 128), ("e1", 128), ("e2", 128), ("l0", 128), ("l1", 128), ("l2", 128)]:
+    SCRATCH["q" + _n] = ("sbuf", [128, _c], "float8_e4m3fn_x4")
+    SCRATCH["z" + _n] = ("sbuf", [128, _c], "uint8")
+for _d, _l in [("bfloat16", [("ut", 512), ("vt", 512), ("xt", 1024), ("xn", 1024), ("ebt", 528), ("half", 528), ("sat", 512), ("kt", 512), ("hst", 512),
+                             ("ht", 1024), ("eqt", 1024), ("w0t", 1024), ("w1t", 1024), ("w2t", 1024), ("w3t", 1024), ("kt1t", 1024), ("kt2t", 1024),
+                             ("rho", 256), ("st0", 256), ("st1", 256), ("f", 1024), ("fh", 1024), ("rk", WIN), ("orow", WIN), ("cw", WIN), ("sg", WIN),
+                             ("vr", 512), ("vo", 512), ("vf", 512), ("vc", 512), ("tr", 512), ("to", 512), ("tf", 512), ("tc", 512),
+                             ("r1", 256), ("r2", 128), ("r3", 64), ("nn", 256), ("mm", 256), ("cc", 256), ("irow", 256),
+                             ("ta", 1024), ("et", 512), ("lt", 512), ("l32", 512), ("v32", 1024)]),
+               ("float32", [("owna", 256), ("ownb", 256), ("crow", 256), ("ys", 256), ("fc", 16), ("nl", 16), ("nf", 16),
+                            ("rl", 16), ("ol", 16), ("cl", 16), ("da", 32), ("db", 32)]),
+               ("int32", [("ci", 32), ("cfi", 16), ("uli", 24)]),
+               ("uint16", [("ul", 24), ("dn", 32), ("od", 32), ("cd", 32), ("cu", 16), ("rku", 16), ("lab", 32)])]:
+    for _n, _c in _l:
+        SCRATCH[_n] = ("sbuf", [128, _c], _d)
+
+SEMAPHORES = ["cv", "cs", "ct", "cg", "left"] + ["ar%d" % t for t in range(ROUNDS)] + ["d%d" % i for i in range(20)]
+
+
+def rank_program(g, core, T, topo):
+    rank = T.rank_of(core)
+    if rank is None:
+        return
+    nxt = T.cores[(rank + 1) % len(T.cores)]
+    prv = T.cores[(rank - 1) % len(T.cores)]
+    Q = {"v": g.vector, "s": g.scalar, "t": g.tensor, "g": g, "y": g.sync}
+    SEM = {"v": "cv", "s": "cs", "t": "ct", "g": "cg"}
+    total = {}
+    know = {q: {} for q in Q}
+    acc = {}
+    dmas = [0]
+
+    def V(name, lo=0, hi=None, st=1, p0=0, p1=128):
+        return (name, lo, SCRATCH[name][1][1] if hi is None else hi, st, p0, p1)
+
+    def ap(v):
+        name, lo, hi, st, p0, p1 = v
+        c = slice(lo, hi) if st == 1 else slice(lo, hi, st)
+        return T[name][:, c] if (p0, p1) == (0, 128) else T[name][p0:p1, c]
+
+    def meet(a, b):
+        if a[4] >= b[5] or b[4] >= a[5] or a[1] >= b[2] or b[1] >= a[2]:
+            return False
+        return not (a[3] == b[3] and (a[1] - b[1]) % a[3])
+
+    def learn(k, more):
+        for s, n in more.items():
+            if k.get(s, 0) < n:
+                k[s] = n
+
+    def order(q, reads, writes):
+        for v, w in [(r, False) for r in reads] + [(r, True) for r in writes]:
+            for (o, ow, oq, sem, n, kn) in acc.get(v[0], []):
+                if v[0] in PSUM:
+                    if not (w or ow or oq != q):
+                        continue
+                elif not (w or ow) or not meet(v, o):
+                    continue
+                if know[q].get(sem, 0) < n:
+                    Q[q].wait_ge(T.sem[sem], n)
+                    learn(know[q], {sem: n})
+                    learn(know[q], kn)
+
+    def note(q, reads, writes, sem, n):
+        kn = dict(know[q])
+        for v, w in [(r, False) for r in reads] + [(r, True) for r in writes]:
+            L = acc.setdefault(v[0], [])
+            if w:
+                L[:] = [e for e in L if not (e[0][1] >= v[1] and e[0][2] <= v[2] and e[0][4] >= v[4] and e[0][5] <= v[5]
+                                             and (v[3] == 1 or (v[3] == e[0][3] and (v[1] - e[0][1]) % v[3] == 0)))]
+            L.append((v, w, q, sem, n, kn))
+
+    def run(q, call, reads, writes, first=True):
+        order(q, reads, writes if first else [])
+        sem = SEM[q]
+        if q == "g" and know[q].get(sem, 0) < total.get(sem, 0):
+            g.wait_ge(T.sem[sem], total[sem])
+            know[q][sem] = total[sem]
+        call().then_inc(T.sem[sem], 1)
+        total[sem] = total.get(sem, 0) + 1
+        note(q, reads, writes, sem, total[sem])
+
+    def dma(q, out, in_, reads, writes):
+        order(q, reads, writes)
+        sem = "d%d" % dmas[0]
+        dmas[0] += 1
+        Q[q].dma_start(out, in_).then_inc(T.sem[sem], 16)
+        total[sem] = 16
+        note(q, reads, writes, sem, 16)
+
+    def ind(v, lst):
+        return ap(v) if lst is None else ap(v).indirect(ap(lst))
+
+    def some(*v):
+        return [x for x in v if isinstance(x, tuple)]
+
+    def col(s):
+        return ap(s) if isinstance(s, tuple) else s
+
+    def fill(v, c):
+        run("v", lambda: g.vector.memset(ap(v), c), [], [v])
+
+    def ts(out, in0, s1, s2, op0, op1=None, lst=None):
+        a = [ap(out), ind(in0, lst), col(s1), col(s2), op0] + ([] if op1 is None else [op1])
+        run("v", lambda: g.vector.tensor_scalar(*a), some(in0, s1, s2, lst), [out])
+
+    def tt(out, in0, in1, op, lst=None):
+        run("v", lambda: g.vector.tensor_tensor(ap(out), ind(in0, lst), ap(in1), op), some(in0, in1, lst), [out])
+
+    def scan(out, d0, d1, op0, op1):
+        run("v", lambda: g.vector.tensor_tensor_scan(ap(out), ap(d0), ap(d1), 0.0, op0, op1), [d0, d1], [out])
+
+    def copy(out, in_):
+        run("v", lambda: g.vector.tensor_copy(ap(out), ap(in_)), [in_], [out])
+
+    def act(out, in_, scale=1.0, lst=None, func=AF.Copy, bias=None):
+        k = {} if scale == 1.0 else {"scale": scale}
+        if bias is not None:
+            k["bias"] = ap(bias)
+        run("s", lambda: g.scalar.activation(ap(out), ind(in_, lst), func, **k), some(in_, lst, bias), [out])
+
+    def turn(out, in_):
+        run("v", lambda: g.vector.transpose(ap(out), ap(in_)), [in_], [out])
+
+    def quant(n, tile, lo=0, hi=None):
+        c, z = V("q" + n, lo, hi), V("z" + n, lo, hi)
+        run("v", lambda: g.vector.quantize_mx(ap(c), ap(z), ap(tile)), [tile], [c, z])
+
+    def mm(bank, cols, L, R, start=True, stop=True):
+        lc, lz = V("q" + L[0], L[1], L[1] + 128), V("z" + L[0], L[1], L[1] + 128)
+        rc, rz = V("q" + R[0], R[1], R[1] + cols), V("z" + R[0], R[1], R[1] + cols)
+        out = V(bank, 0, cols)
+        run("t", lambda: g.tensor.matmul_mx(ap(out), ap(lc), ap(lz), ap(rc), ap(rz), start, stop), [lc, lz, rc, rz], [out], start)
+
+    def add_halves(out, turned):
+        tt(out, V(turned, 0, 512, 32), V(turned, 16, 512, 32), A.add)
+
+    def holes(out, lst):
+        ts(V(out, 0, 32, 2), lst, V("fc", 5, 6), V("fc", 6, 7), A.mult, A.add)
+        ts(V(out, 1, 32, 2), lst, V("fc", 9, 10), V("fc", 7, 8), A.mult, A.add)
+
+    def quarter(n, b):
+        return V(n, 256 * b, 256 * b + 256)
+
+    def I(i):
+        return V("ci", i, i + 1)
+
+    def fc(i):
+        return V("fc", i, i + 1)
+
+    dma("y", T["ut"][:, :], T.u[:, :], [], [V("ut")])
+    dma("s", T["xt"][:, 0:512], T.x[:, 0:512], [], [V("xt", 0, 512)])
+    dma("y", T["xt"][:, 512:1024], T.x[:, 512:1024], [], [V("xt", 512, 1024)])
+    dma("y", T["cfi"][:, :], T.cf[:, :], [], [V("cfi")])
+    dma("y", T["qw"][:, :].bitcast(dt.uint8), T.wc[:, :], [V("ut"), V("xt")], [V("qw")])
+    dma("y", T["zw"][:, :], T.ws[:, :], [], [V("zw")])
+    dma("y", T["vt"][:, :], T.v[:, :], [], [V("vt")])
+
+    def iota(out, pattern, base, cm):
+        run("g", lambda: g.iota(ap(out), pattern, base, cm), [], [out])
+
+    iota(V("uli", 0, 8), [[32, 4], [0, 2]], 0, 0)
+    iota(V("uli", 8, 16), [[32, 4], [0, 2]], 16, 0)
+    iota(V("uli", 16, 24), [[0, 8]], 1, 0)
+    iota(I(16), [[0, 1]], 0, 1)
+    iota(I(17), [[0, 1]], 8, 1)
+    run("g", lambda: g.iota(T["nf"][:, :], [[16, 16]], 0, 0, allow_small_or_imprecise_dtypes=True), [], [V("nf")])
+    fill(V("half"), 0.5)
+    fill(V("sat"), 0.0)
+    run("g", lambda: g.affine_select(T["ebt"][:, :], T["half"][:, :], [[1, 528]], A.is_equal, 0.0, -4, -4), [V("half")], [V("ebt")])
+    for a in range(4):
+        for h in (0, 1):
+            c = 128 * a + 64 * h
+            o, i = V("sat", c, c + 64, 1, 32 * a, 32 * a + 32), V("half", c, c + 64, 1, 32 * a, 32 * a + 32)
+            run("g", lambda: g.affine_select(ap(o), ap(i), [[0, 16], [1, 2], [0, 2]], A.is_equal, 0.0, -h, 0), [i], [o])
+    run("g", lambda: g.iota(T["irow"][:, :], [[1, 256]], 0, 0, allow_small_or_imprecise_dtypes=True), [], [V("irow")])
+    fill(V("hst"), 1.0 / 256)
+    for b in (0, 1):
+        act(V("kt", b, 512, 2), V("hst", b, 512, 2), (-2.0, 2.0)[b])
+    fill(V("ht", 2, 1024, 4), 0.0)
+    fill(V("ht", 3, 1024, 4), 0.0)
+    fill(V("eqt", 1, 1024, 2), 0.0)
+    copy(V("ul"), V("uli"))
+    quant("hs", V("hst"))
+    for n, c in (("rk", 0.0), ("orow", float(ZC)), ("cw", 0.0), ("sg", float(ZC))):
+        fill(V(n, 256, WIN), c)
+    fill(V("kt2t", 3, 1024, 4), 0.0)
+    quant("u", V("ut"))
+    run("v", lambda: g.vector.tensor_copy(T["qus"][:, 0:384].bitcast(dt.uint32), T["qu"][:, 0:128].bitcast(dt.uint32).indirect(T["ul"][:, 0:24])), [V("qu"), V("ul")], [V("qus")])
+    run("s", lambda: g.scalar.activation(T["zus"][:, 0:384], T["zu"][:, 0:128].indirect(T["ul"][:, 0:24]), AF.Copy), [V("zu"), V("ul")], [V("zus")])
+
+    def constants():
+        quant("sa", V("sat"))
+        quant("k", V("kt"))
+        for b in range(4):
+            quant("eb", V("ebt", 4 - b, 516 - b), 128 * b, 128 * b + 128)
+        ts(fc(5), I(21), -1.0, 1.0, A.mult, A.add)
+        copy(V("fc", 8, 10), V("ci", 20, 22))
+        ts(fc(1), I(19), -4.0, None, A.add)
+        copy(fc(0), I(18))
+        ts(fc(3), I(18), fc(1), None, A.add)
+        copy(V("cu"), V("cfi"))
+
+    def lists():
+        act(fc(7), fc(5), float(ZC))
+        act(fc(6), fc(9), float(ZC))
+        act(V("nl"), V("nf"), func=AF.Identity, bias=fc(8))
+        holes("dn", V("nl"))
+        holes("cd", V("cfi"))
+
+    for t in range(ROUNDS):
+        last = t == ROUNDS - 1
+        quant("x", V("xt") if t == 0 else V("xn"))
+        for bank, c in (("p0", 0), ("p1", 128), ("p3", 0), ("p4", 128)):
+            mm(bank, 256, ("us", c), ("x", 0))
+        mm("p7", 128, ("x", 0), ("u", 0))
+        mm("p6", 128, ("x", 128), ("u", 0))
+        mm("p2", 256, ("us", 256), ("x", 0))
+        if t == 0:
+            ts(I(18), I(16), 7, None, A.bitwise_and)
+            ts(I(19), I(17), 4, None, A.arith_shift_right)
+            ts(I(20), I(16), 15, None, A.bitwise_and)
+            ts(I(21), I(16), 4, 1, A.arith_shift_right, A.bitwise_and)
+        else:
+            copy(V("cd"), V("tc", 0, 512, 16))
+            ts(V("cu"), V("cl"), -float(ZC), None, A.add)
+        turn(V("owna"), V("p0", 0, 256))
+        turn(V("ownb"), V("p1", 0, 256))
+        tt(V("eqt", 0, 1024, 4), V("p0", 0, 256), V("owna"), A.is_equal)
+        tt(V("eqt", 2, 1024, 4), V("p1", 0, 256), V("ownb"), A.is_equal)
+        for b in range(2):
+            for a in range(4):
+                v = V("eqt", 2 * b, 1024, 4, 32 * a, 32 * a + 32)
+                run("g", lambda: g.affine_select(ap(v), ap(v), [[0, 8], [1, 32]], A.is_gt, 0.0, 0, -1), [v], [v])
+        ts(V("ht", 0, 1024, 4), V("p2", 0, 256), V("p7", 1, 2), None, A.is_gt)
+        ts(V("ht", 1, 1024, 4), V("p2", 0, 256), V("p6", 1, 2), None, A.is_gt)
+        quant("h", V("ht"))
+        mm("p2", 256, ("hs", 0), ("h", 0))
+        if t == 0:
+            constants()
+        for b in (0, 1):
+            mm(("p5", "p6")[b], 256, ("eb", 128 * b), ("x", 0))
+
+        def level(m):
+            S, flags = V("st%d" % (m % 2)), V("kt%dt" % (1 + m // 4), m % 4, 1024, 4)
+            if m == 0:
+                scan(S, V("rho"), V("rho"), A.max, A.max)
+            else:
+                ops = (A.max, A.min) if m % 2 else (A.min, A.max)
+                scan(S, V("kt%dt" % (1 + (m - 1) // 4), (m - 1) % 4, 1024, 4), V("rho"), ops[0], ops[1])
+            yield
+            tt(flags, V("p2", 0, 256), S, A.not_equal if m % 2 else A.is_equal)
+            yield
+            if m in (3, 6):
+                n = "kt%d" % (1 + m // 4)
+                quant(n, V(n + "t"))
+                mm("p0", 256, ("k", 0), (n, 0), m == 3, m == 6)
+
+        def levels(a, z):
+            for m in range(a, z):
+                for _ in level(m):
+                    yield
+
+        def rest(it):
+            for _ in it:
+                pass
+        ahead = levels(0, L1)
+        for b in list(range(SPLIT, 8)) + list(range(SPLIT)):
+            i = b // 2
+            tile = "w%dt" % i
+            for h in (0, 1):
+                own, e, c = V(("owna", "ownb")[h], 32 * b, 32 * b + 1), 32 * b + 32, b % 2 + 2 * h
+                left = V(tile, c, 4 * e, 4)
+                if b < SPLIT:
+                    ts(left, V(("p0", "p1")[h], 0, e), own, None, A.is_lt)
+                else:
+                    act(left, V(("p3", "p4")[h], 0, e), -1.0, None, AF.Relu, own)
+                if b < 7:
+                    ts(V(tile, 4 * e + c, 1024, 4), V(("p0", "p1")[h], e, 256), own, None, A.is_le)
+                if b < SPLIT:
+                    next(ahead, None)
+            if b % 2:
+                if b == SPLIT + 1:
+                    act(V("rho"), V("p2", 0, 256))
+                if b >= SPLIT:
+                    w = V(tile, 0, 4 * e)
+                    act(w, w, func=AF.Sign)
+                else:
+                    quant("w%d" % i, V(tile))
+                    mm("p7", 256, ("sa", 0), ("w%d" % i, 0), i == 0, False)
+        rest(ahead)
+        if t == 0:
+            lists()
+        for b, bank in enumerate(("p5", "p6")):
+            act(quarter("f", b), V(bank, 0, 256))
+        for b in range(SPLIT // 2, 4):
+            quant("w%d" % b, V("w%dt" % b))
+            mm("p7", 256, ("sa", 0), ("w%d" % b, 0), False, False)
+        quant("eq", V("eqt"))
+        mm("p7", 256, ("sa", 0), ("eq", 0), False, True)
+        act(V("rk", 0, 256), V("p7", 0, 256), 2.0)
+        act(V("vr"), V("rk"), lst=V("dn"))
+        for b, bank in ((2, "p3"), (3, "p4")):
+            mm(bank, 256, ("eb", 128 * b), ("x", 0))
+            act(quarter("f", b), V(bank, 0, 256))
+        for b in range(4):
+            act(quarter("fh", b), quarter("f", b), lst=V("cu"))
+        rest(levels(L1, L2))
+        more = levels(L2, 7)
+        next(more)
+        turn(V("tr"), V("vr"))
+        next(more)
+        add_halves(V("rl"), "tr")
+        next(more)
+        copy(V("rku"), V("rl"))
+        rest(more)
+        run("v", lambda: g.vector.tensor_copy(T["orow"][:, 0:256].indirect(T["rku"][:, :]), T["irow"][:, :]), [V("irow"), V("rku")], [V("orow", 0, 256)])
+        act(V("vo"), V("orow"), lst=V("dn"))
+        act(V("orow", 256, 384), V("orow", 0, 128))
+        act(V("sg", 0, 256), V("orow", 128, 384), lst=V("rku"))
+        k = V("p0", 0, 256)
+        ts(V("nn"), k, 4.0, fc(0), A.add, A.is_gt)
+        ts(V("mm"), k, fc(1), fc(3), A.max, A.is_equal)
+        scan(V("cc"), V("nn"), V("nn"), A.mult, A.add)
+        turn(V("to"), V("vo"))
+        tt(V("cw", 0, 256), V("cc"), V("mm"), A.mult)
+        copy(V("od"), V("to", 0, 512, 16))
+        for half in (0, 1):
+            act(V("vf", 256 * half, 256 * half + 256), V("cw"), lst=V("od", 16 * half, 16 * half + 16))
+        if last:
+            act(V("crow"), V("sg", 0, 256), lst=V("cu"))
+            dma("y", T.op[:, :], T["crow"][0:128:16, :], [V("crow")], [])
+        else:
+            act(V("vc"), V("sg"), lst=V("cd"))
+        add_halves(V("ol"), "to")
+        for half in (0, 1):
+            a, z = 256 * half, 256 * half + 256
+            if half == 0:
+                turn(V("tf", a, z), V("vf", a, z))
+            for o, i in (("r1", "tf"), ("r2", "r1"), ("r3", "r2")):
+                tt(V(o, a // 2, z // 2), V(i, a, z, 2), V(i, a + 1, z, 2), A.add)
+                a, z = a // 2, z // 2
+            p = 8 * half
+            for s in (0, 1):
+                tt(V("da", 16 * s + p, 16 * s + p + 8), V("r3", a + s, z, 4), V("r3", a + s + 2, z, 4), A.add)
+            for s in (0, 16):
+                tt(V("db", s + p, s + p + 8), V("ol", p, p + 8), V("da", s + p, s + p + 8), A.subtract)
+            for s in (0, 16):
+                ts(V("lab", s + p, s + p + 8), V("db", s + p, s + p + 8), -float(ZC), None, A.add)
+            if half == 0:
+                turn(V("tf", 256, 512), V("vf", 256, 512))
+            for b in range(4):
+                tmp = V("ta", 512 * half + 128 * b, 512 * half + 128 * b + 128)
+                act(tmp, quarter("fh", b), lst=V("lab", p, p + 8))
+                tt(V("et", b, 512, 4) if half == 0 else V("lt", 128 * b, 128 * b + 128), quarter("fh", b), tmp, A.add, lst=V("lab", 16 + p, 24 + p))
+            if half == 0:
+                e = "e%d" % t
+                quant(e, V("et"))
+                order("g", [V("q" + e), V("z" + e)], [])
+                rid, pid = topo.addr(nxt)[:2]
+                m = topo.mask(core, nxt)
+                g.remote_dma(T["ql%d" % t][:, 0:128].bitcast(dt.uint8), T["q" + e][:, 0:128].bitcast(dt.uint8), T.sem["ar%d" % t], T.sem["left"], pid, rid, m)
+                g.remote_dma(T["zl%d" % t][:, 0:128], T["z" + e][:, 0:128], T.sem["ar%d" % t], T.sem["left"], pid, rid, m)
+                total["left"] = total.get("left", 0) + 2 * len(topo.engines(core, nxt))
+        ts(V("l32"), V("lt"), 32.0, None, A.mult)
+        for b in range(4):
+            act(V("v32", 256 * b, 256 * b + 128), V("et", b, 512, 4), 32.0)
+        if last:
+            quant("v", V("vt"))
+        else:
+            turn(V("tc"), V("vc"))
+            add_halves(V("cl"), "tc")
+        n = 2 * len(topo.engines(prv, core))
+        total["ar%d" % t] = n
+        for z in ("ql%d" % t, "zl%d" % t):
+            acc.setdefault(z, []).append((V(z), True, "r", "ar%d" % t, n, {}))
+        for b, bank in enumerate(("p0", "p1", "p7", "p3")):
+            mm(bank, 128, ("w", 128 * b), ("l%d" % t, 0))
+            tt(V("v32", 256 * b + 128, 256 * b + 256), V(bank, 0, 128), V("l32", 128 * b, 128 * b + 128), A.add)
+        for b in range(4):
+            out, win, lst = V("xn", b, 1024, 4), quarter("v32", b), V("rku")
+            if b in XS:
+                act(out, win, scale=0.03125, lst=lst)
+            else:
+                ts(out, win, 0.03125, None, A.mult, lst=lst)
+
+    quant("x", V("xn"))
+    mm("p4", 256, ("v", 0), ("x", 0))
+    copy(V("ys"), V("p4", 0, 256))
+    dma("y", T.oc[:, :], T["qx"][:, :].bitcast(dt.uint8), [V("qx")], [])
+    for i in range(4):
+        dma("y" if i % 2 else "s", T.osc[4 * i:4 * i + 4, :], T["zx"][32 * i:32 * i + 4, :], [V("zx")], [])
+    dma("y", T.y[:, :], T["ys"][:, :], [V("ys")], [])
+    for sem, n in total.items():
+        g.wait_ge(T.sem[sem], n)

@@ -4,31 +4,109 @@ ROUNDS = 3
 ZC = 384
 WIN = 400
 XS = (0, 1)
-SPLIT, L1, L2 = 4, 3, 5
+SL, SR = 7, 3
+TINY = 2.0 ** -17
+HOP, FAR, LOAD = 200, 2200, 1800
+
+SLACK, PASSES = 150, 4
 
 SCRATCH = {}
 PSUM = ["p%d" % i for i in range(8)]
 for _n in PSUM:
     SCRATCH[_n] = ("psum", [128, 512], "float32")
-for _n, _c in [("u", 128), ("v", 128), ("w", 512), ("us", 384), ("x", 256), ("eb", 512), ("sa", 128), ("k", 128), ("hs", 128), ("h", 256),
-               ("w0", 256), ("w1", 256), ("w2", 256), ("w3", 256), ("eq", 256), ("kt1", 256), ("kt2", 256),
+for _n, _c in [("u", 128), ("v", 128), ("w", 512), ("us", 256), ("x", 256), ("eb", 512), ("k", 128), ("hs", 128), ("hn", 130), ("h", 256), ("al", 256),
                ("e0", 128), ("e1", 128), ("e2", 128), ("l0", 128), ("l1", 128), ("l2", 128)]:
     SCRATCH["q" + _n] = ("sbuf", [128, _c], "float8_e4m3fn_x4")
     SCRATCH["z" + _n] = ("sbuf", [128, _c], "uint8")
-for _d, _l in [("bfloat16", [("ut", 512), ("vt", 512), ("xt", 1024), ("xn", 1024), ("ebt", 528), ("half", 528), ("sat", 512), ("kt", 512), ("hst", 512),
-                             ("ht", 1024), ("eqt", 1024), ("w0t", 1024), ("w1t", 1024), ("w2t", 1024), ("w3t", 1024), ("kt1t", 1024), ("kt2t", 1024),
-                             ("rho", 256), ("st0", 256), ("st1", 256), ("f", 1024), ("fh", 1024), ("rk", WIN), ("orow", WIN), ("cw", WIN), ("sg", WIN),
-                             ("vr", 512), ("vo", 512), ("vf", 512), ("vc", 512), ("tr", 512), ("to", 512), ("tf", 512), ("tc", 512),
-                             ("r1", 256), ("r2", 128), ("r3", 64), ("nn", 256), ("mm", 256), ("cc", 256), ("irow", 256),
+for _d, _l in [("bfloat16", [("ut", 512), ("vt", 512), ("xt", 1024), ("xn", 1024), ("ebt", 528), ("half", 528), ("kt", 512), ("hst", 512), ("hnt", 520),
+                             ("ht", 1024), ("alt", 1024), ("rho", 256), ("gg", 512), ("ll", 512), ("nf", 384), ("lt1", 256), ("le1", 256),
+                             ("j16", 256), ("m16", 256), ("ka", 256), ("ke", 256), ("eye", 256), ("irow", 256), ("eq", 256), ("es", 256),
+                             ("cmp", 4096), ("cs", 4096), ("jk", 4096), ("f", 1024), ("orow", WIN), ("sg", WIN), ("crow", 272), ("dc", 256), ("up", 256),
+                             ("nn", 256), ("mm", 256), ("cc", 256), ("cw", 256), ("vf", 512), ("tf", 512), ("sm", 512), ("vc", 512), ("tc", 512),
                              ("ta", 1024), ("et", 512), ("lt", 512), ("l32", 512), ("v32", 1024)]),
-               ("float32", [("owna", 256), ("ownb", 256), ("crow", 256), ("ys", 256), ("fc", 16), ("nl", 16), ("nf", 16),
-                            ("rl", 16), ("ol", 16), ("cl", 16), ("da", 32), ("db", 32)]),
-               ("int32", [("ci", 32), ("cfi", 16), ("uli", 24)]),
-               ("uint16", [("ul", 24), ("dn", 32), ("od", 32), ("cd", 32), ("cu", 16), ("rku", 16), ("lab", 32)])]:
+               ("float32", [("sm16", 256), ("own", 256), ("key", 256), ("tiny", 256), ("cop", 256), ("ys", 256), ("fc", 32), ("hb", 8), ("neg", 16),
+                            ("kq", 16), ("acc", 16), ("ru", 16), ("rv", 16), ("cl", 16)]),
+               ("int32", [("ci", 16), ("cfi", 16), ("uli", 16), ("ri", 16), ("ra", 16), ("rp", 16)]),
+               ("uint16", [("ul", 16), ("cd", 32), ("cu", 16), ("rku", 16), ("pu", 16), ("lab", 32)])]:
     for _n, _c in _l:
         SCRATCH[_n] = ("sbuf", [128, _c], _d)
 
 SEMAPHORES = ["cv", "cs", "ct", "cg", "left"] + ["ar%d" % t for t in range(ROUNDS)] + ["d%d" % i for i in range(20)]
+
+
+def meet(a, b):
+    if a[4] >= b[5] or b[4] >= a[5] or a[1] >= b[2] or b[1] >= a[2]:
+        return False
+    return not (a[3] == b[3] and (a[1] - b[1]) % a[3])
+
+
+def covers(v, o):
+    return o[1] >= v[1] and o[2] <= v[2] and o[4] >= v[4] and o[5] <= v[5] and (v[3] == 1 or (v[3] == o[3] and (v[1] - o[1]) % v[3] == 0))
+
+
+def follows(seen, q, reads, writes):
+    for v, w in [(r, False) for r in reads] + [(r, True) for r in writes]:
+        for e in seen.get(v[0], []):
+            if (w or e[1] or e[2] != q) if v[0] in PSUM else ((w or e[1]) and meet(v, e[0])):
+                yield e
+
+
+def remember(seen, q, reads, writes, who):
+    for v, w in [(r, False) for r in reads] + [(r, True) for r in writes]:
+        L = seen.setdefault(v[0], [])
+        if w:
+            L[:] = [e for e in L if not covers(v, e[0])]
+        L.append((v, w, q, who))
+
+
+def arrange(calls):
+    seen, before = {}, []
+    for i, c in enumerate(calls):
+        before.append({e[3] for e in follows(seen, c["q"], c["reads"], c["writes"])} | set(c["after"]))
+        remember(seen, c["q"], c["reads"], c["writes"], i)
+    n = len(calls)
+    behind = [[] for _ in range(n)]
+    for i in range(n):
+        for j in before[i]:
+            behind[j].append(i)
+
+    def hop(j, i):
+        return 0 if calls[j]["q"] == calls[i]["q"] == "t" else HOP
+
+    def place(first, then, way):
+        left = [len(b) for b in first]
+        ready, done, free, placed, open_ = [0.0] * n, [0.0] * n, {}, [], {}
+        for i in range(n):
+            if not left[i]:
+                open_.setdefault(calls[i]["q"], []).append(i)
+        while len(placed) < n:
+            q = min((k for k in open_ if open_[k]), key=lambda k: max(free.get(k, 0), min(ready[i] for i in open_[k])))
+            now = max(free.get(q, 0), min(ready[i] for i in open_[q]))
+            i = max(open_[q], key=lambda i: way[i] - max(0, ready[i] - now))
+            if ready[i] > now:
+                fits = [j for j in open_[q] if ready[j] <= now and now + calls[j]["hold"] <= ready[i] + SLACK]
+                if not fits:
+                    free[q] = min(ready[j] for j in open_[q] if ready[j] > now)
+                    continue
+                i = max(fits, key=lambda j: way[j])
+            open_[q].remove(i)
+            free[q], done[i] = now + calls[i]["hold"], now + calls[i]["long"]
+            placed.append(i)
+            for j in then[i]:
+                ready[j] = max(ready[j], done[i] + hop(i, j))
+                left[j] -= 1
+                if not left[j]:
+                    open_.setdefault(calls[j]["q"], []).append(j)
+        return placed, done
+    way = [0.0] * n
+    for i in reversed(range(n)):
+        way[i] = calls[i]["long"] + max([hop(i, j) + way[j] for j in behind[i]], default=0)
+    tries = []
+    for _ in range(PASSES):
+        placed, done = place(before, behind, way)
+        tries.append((max(done), placed))
+        way = place(behind, before, done)[1]
+    return min(tries)[1]
 
 
 def rank_program(g, core, T, topo):
@@ -38,11 +116,7 @@ def rank_program(g, core, T, topo):
     nxt = T.cores[(rank + 1) % len(T.cores)]
     prv = T.cores[(rank - 1) % len(T.cores)]
     Q = {"v": g.vector, "s": g.scalar, "t": g.tensor, "g": g, "y": g.sync}
-    SEM = {"v": "cv", "s": "cs", "t": "ct", "g": "cg"}
-    total = {}
-    know = {q: {} for q in Q}
-    acc = {}
-    dmas = [0]
+    calls = []
 
     def V(name, lo=0, hi=None, st=1, p0=0, p1=128):
         return (name, lo, SCRATCH[name][1][1] if hi is None else hi, st, p0, p1)
@@ -52,55 +126,17 @@ def rank_program(g, core, T, topo):
         c = slice(lo, hi) if st == 1 else slice(lo, hi, st)
         return T[name][:, c] if (p0, p1) == (0, 128) else T[name][p0:p1, c]
 
-    def meet(a, b):
-        if a[4] >= b[5] or b[4] >= a[5] or a[1] >= b[2] or b[1] >= a[2]:
-            return False
-        return not (a[3] == b[3] and (a[1] - b[1]) % a[3])
+    def size(v):
+        return len(range(v[1], v[2], v[3]))
 
-    def learn(k, more):
-        for s, n in more.items():
-            if k.get(s, 0) < n:
-                k[s] = n
+    def quarter(n, b):
+        return V(n, 256 * b, 256 * b + 256)
 
-    def order(q, reads, writes):
-        for v, w in [(r, False) for r in reads] + [(r, True) for r in writes]:
-            for (o, ow, oq, sem, n, kn) in acc.get(v[0], []):
-                if v[0] in PSUM:
-                    if not (w or ow or oq != q):
-                        continue
-                elif not (w or ow) or not meet(v, o):
-                    continue
-                if know[q].get(sem, 0) < n:
-                    Q[q].wait_ge(T.sem[sem], n)
-                    learn(know[q], {sem: n})
-                    learn(know[q], kn)
+    def one(n, i):
+        return V(n, i, i + 1)
 
-    def note(q, reads, writes, sem, n):
-        kn = dict(know[q])
-        for v, w in [(r, False) for r in reads] + [(r, True) for r in writes]:
-            L = acc.setdefault(v[0], [])
-            if w:
-                L[:] = [e for e in L if not (e[0][1] >= v[1] and e[0][2] <= v[2] and e[0][4] >= v[4] and e[0][5] <= v[5]
-                                             and (v[3] == 1 or (v[3] == e[0][3] and (v[1] - e[0][1]) % v[3] == 0)))]
-            L.append((v, w, q, sem, n, kn))
-
-    def run(q, call, reads, writes, first=True):
-        order(q, reads, writes if first else [])
-        sem = SEM[q]
-        if q == "g" and know[q].get(sem, 0) < total.get(sem, 0):
-            g.wait_ge(T.sem[sem], total[sem])
-            know[q][sem] = total[sem]
-        call().then_inc(T.sem[sem], 1)
-        total[sem] = total.get(sem, 0) + 1
-        note(q, reads, writes, sem, total[sem])
-
-    def dma(q, out, in_, reads, writes):
-        order(q, reads, writes)
-        sem = "d%d" % dmas[0]
-        dmas[0] += 1
-        Q[q].dma_start(out, in_).then_inc(T.sem[sem], 16)
-        total[sem] = 16
-        note(q, reads, writes, sem, 16)
+    def row(bank, a=0, z=256):
+        return V(bank, a, z)
 
     def ind(v, lst):
         return ap(v) if lst is None else ap(v).indirect(ap(lst))
@@ -111,283 +147,252 @@ def rank_program(g, core, T, topo):
     def col(s):
         return ap(s) if isinstance(s, tuple) else s
 
+    def put(q, call, reads, writes, ns, kind="call", hold=None, after=()):
+        calls.append({"q": q, "call": call, "reads": reads, "writes": writes, "long": ns, "hold": ns if hold is None else hold, "kind": kind, "after": after})
+        return len(calls) - 1
+
+    def cycles(n, each, lst=None):
+        return 60 + 1.25 * n if lst is not None else 0.83 * max(64, n * each)
+
+    def narrow(*v):
+        return 0.5 if all(SCRATCH[x[0]][2] in ("bfloat16", "uint16") for x in v) else 1
+
+    def dma(q, out, in_, reads, writes):
+        put(q, lambda: Q[q].dma_start(out, in_), reads, writes, LOAD, "dma", 60)
+
     def fill(v, c):
-        run("v", lambda: g.vector.memset(ap(v), c), [], [v])
+        put("v", lambda: g.vector.memset(ap(v), c), [], [v], cycles(size(v), narrow(v)))
 
     def ts(out, in0, s1, s2, op0, op1=None, lst=None):
-        a = [ap(out), ind(in0, lst), col(s1), col(s2), op0] + ([] if op1 is None else [op1])
-        run("v", lambda: g.vector.tensor_scalar(*a), some(in0, s1, s2, lst), [out])
+        a = [col(s1), col(s2), op0] + ([] if op1 is None else [op1])
+        put("v", lambda: g.vector.tensor_scalar(ap(out), ind(in0, lst), *a), some(in0, s1, s2, lst), [out], cycles(size(out), narrow(out, in0), lst))
 
     def tt(out, in0, in1, op, lst=None):
-        run("v", lambda: g.vector.tensor_tensor(ap(out), ind(in0, lst), ap(in1), op), some(in0, in1, lst), [out])
+        put("v", lambda: g.vector.tensor_tensor(ap(out), ind(in0, lst), ap(in1), op), some(in0, in1, lst), [out],
+            cycles(size(out), 1 if in0[0] in PSUM else 2, lst))
 
-    def scan(out, d0, d1, op0, op1):
-        run("v", lambda: g.vector.tensor_tensor_scan(ap(out), ap(d0), ap(d1), 0.0, op0, op1), [d0, d1], [out])
+    def scan(out, d0, d1, op0, op1, init=0.0):
+        put("v", lambda: g.vector.tensor_tensor_scan(ap(out), ap(d0), ap(d1), col(init), op0, op1), some(d0, d1, init), [out],
+            cycles(size(out), narrow(out, d0, d1)))
 
     def copy(out, in_):
-        run("v", lambda: g.vector.tensor_copy(ap(out), ap(in_)), [in_], [out])
+        put("v", lambda: g.vector.tensor_copy(ap(out), ap(in_)), [in_], [out], cycles(size(out), narrow(out, in_)))
 
-    def act(out, in_, scale=1.0, lst=None, func=AF.Copy, bias=None):
-        k = {} if scale == 1.0 else {"scale": scale}
+    def scatter(win, lst, in_):
+        put("v", lambda: g.vector.tensor_copy(ind(win, lst), ap(in_)), [in_, lst], [win], 50 + 3 * size(in_))
+
+    def act(out, in_, scale=1.0, lst=None, func=AF.Copy, bias=None, total_to=None):
+        k = {} if scale == 1.0 else {"scale": col(scale)}
         if bias is not None:
-            k["bias"] = ap(bias)
-        run("s", lambda: g.scalar.activation(ap(out), ind(in_, lst), func, **k), some(in_, lst, bias), [out])
+            k["bias"] = col(bias)
+        if total_to is not None:
+            k["accum_out"] = ap(total_to)
+        put("s", lambda: g.scalar.activation(ap(out), ind(in_, lst), func, **k), some(in_, lst, bias, scale), some(out, total_to), cycles(size(out), 1, lst))
 
     def turn(out, in_):
-        run("v", lambda: g.vector.transpose(ap(out), ap(in_)), [in_], [out])
+        put("v", lambda: g.vector.transpose(ap(out), ap(in_)), [in_], [out], cycles(size(out), narrow(out)))
 
     def quant(n, tile, lo=0, hi=None):
         c, z = V("q" + n, lo, hi), V("z" + n, lo, hi)
-        run("v", lambda: g.vector.quantize_mx(ap(c), ap(z), ap(tile)), [tile], [c, z])
+        put("v", lambda: g.vector.quantize_mx(ap(c), ap(z), ap(tile)), [tile], [c, z], 12 + 0.22 * size(tile))
 
     def mm(bank, cols, L, R, start=True, stop=True):
         lc, lz = V("q" + L[0], L[1], L[1] + 128), V("z" + L[0], L[1], L[1] + 128)
         rc, rz = V("q" + R[0], R[1], R[1] + cols), V("z" + R[0], R[1], R[1] + cols)
         out = V(bank, 0, cols)
-        run("t", lambda: g.tensor.matmul_mx(ap(out), ap(lc), ap(lz), ap(rc), ap(rz), start, stop), [lc, lz, rc, rz], [out], start)
+        put("t", lambda: g.tensor.matmul_mx(ap(out), ap(lc), ap(lz), ap(rc), ap(rz), start, stop), [lc, lz, rc, rz], [out], 0.83 * (cols + 16),
+            "call" if start else "adds")
 
-    def add_halves(out, turned):
-        tt(out, V(turned, 0, 512, 32), V(turned, 16, 512, 32), A.add)
+    def iota(out, pattern, base, cm, small=False):
+        k = {"allow_small_or_imprecise_dtypes": True} if small else {}
+        put("g", lambda: g.iota(ap(out), pattern, base, cm, **k), [], [out], 130 + 1.66 * size(out))
 
-    def holes(out, lst):
-        ts(V(out, 0, 32, 2), lst, V("fc", 5, 6), V("fc", 6, 7), A.mult, A.add)
-        ts(V(out, 1, 32, 2), lst, V("fc", 9, 10), V("fc", 7, 8), A.mult, A.add)
+    def send(t):
+        e = "e%d" % t
+        rid, pid = topo.addr(nxt)[:2]
+        m = topo.mask(core, nxt)
 
-    def quarter(n, b):
-        return V(n, 256 * b, 256 * b + 256)
+        def call():
+            g.remote_dma(T["ql%d" % t][:, 0:128].bitcast(dt.uint8), T["q" + e][:, 0:128].bitcast(dt.uint8), T.sem["ar%d" % t], T.sem["left"], pid, rid, m)
+            g.remote_dma(T["zl%d" % t][:, 0:128], T["z" + e][:, 0:128], T.sem["ar%d" % t], T.sem["left"], pid, rid, m)
+        sent = put("g", call, [V("q" + e), V("z" + e)], [], FAR, "send", 200)
+        put("r", "ar%d" % t, [], [V("ql%d" % t), V("zl%d" % t)], 0, "arrives", after=[sent])
 
-    def I(i):
-        return V("ci", i, i + 1)
-
-    def fc(i):
-        return V("fc", i, i + 1)
+    I = {n: one("ci", i) for i, n in enumerate(("p", "r", "m", "s", "g", "h"))}
+    F = {n: one("fc", i) for i, n in enumerate(("r", "m", "s", "g", "h", "p", "gs", "m7", "thr", "val", "lo", "csg", "h16", "lw",
+                                                "zl", "zu", "k0", "k1", "t0", "t1", "t2", "nine"))}
 
     dma("y", T["ut"][:, :], T.u[:, :], [], [V("ut")])
     dma("s", T["xt"][:, 0:512], T.x[:, 0:512], [], [V("xt", 0, 512)])
     dma("y", T["xt"][:, 512:1024], T.x[:, 512:1024], [], [V("xt", 512, 1024)])
     dma("y", T["cfi"][:, :], T.cf[:, :], [], [V("cfi")])
     dma("y", T["qw"][:, :].bitcast(dt.uint8), T.wc[:, :], [V("ut"), V("xt")], [V("qw")])
-    dma("y", T["zw"][:, :], T.ws[:, :], [], [V("zw")])
-    dma("y", T["vt"][:, :], T.v[:, :], [], [V("vt")])
+    dma("y", T["zw"][:, :], T.ws[:, :], [V("ut"), V("xt")], [V("zw")])
+    dma("y", T["vt"][:, :], T.v[:, :], [V("ut"), V("xt")], [V("vt")])
 
-    def iota(out, pattern, base, cm):
-        run("g", lambda: g.iota(ap(out), pattern, base, cm), [], [out])
-
-    iota(V("uli", 0, 8), [[32, 4], [0, 2]], 0, 0)
-    iota(V("uli", 8, 16), [[32, 4], [0, 2]], 16, 0)
-    iota(V("uli", 16, 24), [[0, 8]], 1, 0)
-    iota(I(16), [[0, 1]], 0, 1)
-    iota(I(17), [[0, 1]], 8, 1)
-    run("g", lambda: g.iota(T["nf"][:, :], [[16, 16]], 0, 0, allow_small_or_imprecise_dtypes=True), [], [V("nf")])
+    iota(V("uli", 0, 8), [[16, 8]], 0, 0)
+    iota(V("uli", 8, 16), [[0, 8]], 1, 0)
+    iota(I["p"], [[0, 1]], 0, 1)
+    iota(V("j16"), [[0, 16], [1, 16]], 0, 0, True)
+    iota(V("irow"), [[1, 256]], 0, 0, True)
+    iota(V("kq"), [[16, 16]], 16, 0, True)
     fill(V("half"), 0.5)
-    fill(V("sat"), 0.0)
-    run("g", lambda: g.affine_select(T["ebt"][:, :], T["half"][:, :], [[1, 528]], A.is_equal, 0.0, -4, -4), [V("half")], [V("ebt")])
-    for a in range(4):
-        for h in (0, 1):
-            c = 128 * a + 64 * h
-            o, i = V("sat", c, c + 64, 1, 32 * a, 32 * a + 32), V("half", c, c + 64, 1, 32 * a, 32 * a + 32)
-            run("g", lambda: g.affine_select(ap(o), ap(i), [[0, 16], [1, 2], [0, 2]], A.is_equal, 0.0, -h, 0), [i], [o])
-    run("g", lambda: g.iota(T["irow"][:, :], [[1, 256]], 0, 0, allow_small_or_imprecise_dtypes=True), [], [V("irow")])
-    fill(V("hst"), 1.0 / 256)
-    for b in (0, 1):
-        act(V("kt", b, 512, 2), V("hst", b, 512, 2), (-2.0, 2.0)[b])
-    fill(V("ht", 2, 1024, 4), 0.0)
-    fill(V("ht", 3, 1024, 4), 0.0)
-    fill(V("eqt", 1, 1024, 2), 0.0)
-    copy(V("ul"), V("uli"))
+    put("g", lambda: g.affine_select(T["ebt"][:, :], T["half"][:, :], [[1, 528]], A.is_equal, 0.0, -4, -4), [V("half")], [V("ebt")], 1050)
+    for b in range(4):
+        quant("eb", V("ebt", 4 - b, 516 - b), 128 * b, 128 * b + 128)
+    fill(V("hst"), 1.0 / 512)
     quant("hs", V("hst"))
-    for n, c in (("rk", 0.0), ("orow", float(ZC)), ("cw", 0.0), ("sg", float(ZC))):
-        fill(V(n, 256, WIN), c)
-    fill(V("kt2t", 3, 1024, 4), 0.0)
+    fill(V("hnt"), 0.0)
+    fill(V("hnt", 8, 12), -1.0 / 512)
+    quant("hn", V("hnt"))
+    fill(V("kt"), 2.0)
+    fill(V("kt", 2, 512, 4), 1.0 / 128)
+    fill(V("kt", 3, 512, 4), 0.0)
+    quant("k", V("kt"))
+    for v in (V("ht", 2, 1024, 4), V("ht", 3, 1024, 4), V("alt"), V("acc"), one("cs", 4095), V("kq", 0, SL), V("crow", 0, 16), V("vf")):
+        fill(v, 0.0)
+    fill(V("orow", 256, WIN), float(ZC))
+    fill(V("sg", 256, WIN), float(ZC))
+    fill(F["nine"], 9.0)
+    copy(V("ul"), V("uli"))
+    ts(I["r"], I["p"], 15, None, A.bitwise_and)
+    ts(I["m"], I["p"], 1, 7, A.arith_shift_right, A.bitwise_and)
+    ts(I["s"], I["p"], 1, None, A.bitwise_and)
+    ts(I["g"], I["p"], 4, None, A.arith_shift_right)
+    ts(I["h"], I["p"], 4, 1, A.arith_shift_right, A.bitwise_and)
+    copy(F["r"], I["r"])
+    copy(F["p"], I["p"])
+    copy(V("fc", 1, 5), V("ci", 2, 6))
+    ts(V("m16"), V("j16"), F["r"], None, A.is_equal)
+    ts(V("ka"), V("j16"), 0.0, None, A.is_gt)
+    ts(V("ke"), V("j16"), F["r"], None, A.is_gt)
+    ts(V("eye"), V("irow"), F["p"], None, A.is_equal)
+    act(V("tiny"), V("irow"), TINY)
+    ts(F["k0"], F["p"], -TINY, -TINY / 2, A.mult, A.add)
+    ts(F["k1"], F["p"], -TINY, -TINY * 128.5, A.mult, A.add)
+    ts(F["gs"], F["g"], F["s"], 7.0, A.add, A.min)
+    ts(F["m7"], F["m"], 7.0, None, A.is_equal)
+    ts(F["t0"], F["m"], -1.0, 7.0, A.mult, A.add)
+    ts(F["t1"], F["m7"], -100.0, 7.0, A.mult, A.add)
+    ts(F["t2"], F["m7"], 7.0, F["m"], A.mult, A.subtract)
+    ts(F["thr"], F["m7"], 100.0, F["t0"], A.mult, A.add)
+    ts(F["lo"], F["t1"], F["gs"], None, A.subtract)
+    ts(F["val"], F["lo"], F["t2"], None, A.add)
+    ts(F["csg"], F["m7"], -2.0, 1.0, A.mult, A.add)
+    ts(F["lw"], F["h"], -1.0, 1.0, A.mult, A.add)
+    ts(F["h16"], F["h"], 16.0, None, A.mult)
+    ts(F["zl"], F["lw"], float(ZC), None, A.mult)
+    ts(F["zu"], F["h"], float(ZC), None, A.mult)
     quant("u", V("ut"))
-    run("v", lambda: g.vector.tensor_copy(T["qus"][:, 0:384].bitcast(dt.uint32), T["qu"][:, 0:128].bitcast(dt.uint32).indirect(T["ul"][:, 0:24])), [V("qu"), V("ul")], [V("qus")])
-    run("s", lambda: g.scalar.activation(T["zus"][:, 0:384], T["zu"][:, 0:128].indirect(T["ul"][:, 0:24]), AF.Copy), [V("zu"), V("ul")], [V("zus")])
-
-    def constants():
-        quant("sa", V("sat"))
-        quant("k", V("kt"))
-        for b in range(4):
-            quant("eb", V("ebt", 4 - b, 516 - b), 128 * b, 128 * b + 128)
-        ts(fc(5), I(21), -1.0, 1.0, A.mult, A.add)
-        copy(V("fc", 8, 10), V("ci", 20, 22))
-        ts(fc(1), I(19), -4.0, None, A.add)
-        copy(fc(0), I(18))
-        ts(fc(3), I(18), fc(1), None, A.add)
-        copy(V("cu"), V("cfi"))
-
-    def lists():
-        act(fc(7), fc(5), float(ZC))
-        act(fc(6), fc(9), float(ZC))
-        act(V("nl"), V("nf"), func=AF.Identity, bias=fc(8))
-        holes("dn", V("nl"))
-        holes("cd", V("cfi"))
+    quant("v", V("vt"))
+    put("v", lambda: g.vector.tensor_copy(T["qus"][:, :].bitcast(dt.uint32), T["qu"][:, 0:128].bitcast(dt.uint32).indirect(T["ul"][:, :])),
+        [V("qu"), V("ul")], [V("qus")], 380)
+    put("s", lambda: g.scalar.activation(T["zus"][:, :], T["zu"][:, 0:128].indirect(T["ul"][:, :]), AF.Copy), [V("zu"), V("ul")], [V("zus")], 380)
+    copy(V("cu"), V("cfi"))
+    ts(V("cd", 0, 32, 2), V("cfi"), F["lw"], F["zu"], A.mult, A.add)
+    ts(V("cd", 1, 32, 2), V("cfi"), F["h"], F["zl"], A.mult, A.add)
+    act(V("crow", 16, 272), V("irow"), F["csg"], V("cu"))
 
     for t in range(ROUNDS):
         last = t == ROUNDS - 1
+        tt(V("dc"), V("crow", 15, 271), V("crow", 16, 272), A.subtract)
         quant("x", V("xt") if t == 0 else V("xn"))
-        for bank, c in (("p0", 0), ("p1", 128), ("p3", 0), ("p4", 128)):
-            mm(bank, 256, ("us", c), ("x", 0))
-        mm("p7", 128, ("x", 0), ("u", 0))
-        mm("p6", 128, ("x", 128), ("u", 0))
-        mm("p2", 256, ("us", 256), ("x", 0))
-        if t == 0:
-            ts(I(18), I(16), 7, None, A.bitwise_and)
-            ts(I(19), I(17), 4, None, A.arith_shift_right)
-            ts(I(20), I(16), 15, None, A.bitwise_and)
-            ts(I(21), I(16), 4, 1, A.arith_shift_right, A.bitwise_and)
-        else:
-            copy(V("cd"), V("tc", 0, 512, 16))
-            ts(V("cu"), V("cl"), -float(ZC), None, A.add)
-        turn(V("owna"), V("p0", 0, 256))
-        turn(V("ownb"), V("p1", 0, 256))
-        tt(V("eqt", 0, 1024, 4), V("p0", 0, 256), V("owna"), A.is_equal)
-        tt(V("eqt", 2, 1024, 4), V("p1", 0, 256), V("ownb"), A.is_equal)
-        for b in range(2):
-            for a in range(4):
-                v = V("eqt", 2 * b, 1024, 4, 32 * a, 32 * a + 32)
-                run("g", lambda: g.affine_select(ap(v), ap(v), [[0, 8], [1, 32]], A.is_gt, 0.0, 0, -1), [v], [v])
-        ts(V("ht", 0, 1024, 4), V("p2", 0, 256), V("p7", 1, 2), None, A.is_gt)
-        ts(V("ht", 1, 1024, 4), V("p2", 0, 256), V("p6", 1, 2), None, A.is_gt)
+        mm("p0", 256, ("us", 0), ("x", 0))
+        mm("p1", 256, ("us", 0), ("x", 0))
+        mm("p3", 128, ("x", 0), ("u", 0))
+        mm("p4", 128, ("x", 128), ("u", 0))
+        mm("p2", 256, ("us", 128), ("x", 0))
+        for h, bank in enumerate(("p3", "p4")):
+            act(one("hb", h), one(bank, 1), -1.0)
+            act(V("ht", h, 1024, 4), row("p2"), func=AF.Sign, bias=one("hb", h))
         quant("h", V("ht"))
+        mm("p5", 256, ("hs", 0), ("h", 0))
+        mm("p3", 128, ("h", 0), ("hn", 2), True, False)
+        mm("p3", 128, ("h", 128), ("hn", 0), False, True)
         mm("p2", 256, ("hs", 0), ("h", 0))
-        if t == 0:
-            constants()
-        for b in (0, 1):
-            mm(("p5", "p6")[b], 256, ("eb", 128 * b), ("x", 0))
-
-        def level(m):
-            S, flags = V("st%d" % (m % 2)), V("kt%dt" % (1 + m // 4), m % 4, 1024, 4)
-            if m == 0:
-                scan(S, V("rho"), V("rho"), A.max, A.max)
-            else:
-                ops = (A.max, A.min) if m % 2 else (A.min, A.max)
-                scan(S, V("kt%dt" % (1 + (m - 1) // 4), (m - 1) % 4, 1024, 4), V("rho"), ops[0], ops[1])
-            yield
-            tt(flags, V("p2", 0, 256), S, A.not_equal if m % 2 else A.is_equal)
-            yield
-            if m in (3, 6):
-                n = "kt%d" % (1 + m // 4)
-                quant(n, V(n + "t"))
-                mm("p0", 256, ("k", 0), (n, 0), m == 3, m == 6)
-
-        def levels(a, z):
-            for m in range(a, z):
-                for _ in level(m):
-                    yield
-
-        def rest(it):
-            for _ in it:
-                pass
-        ahead = levels(0, L1)
-        for b in list(range(SPLIT, 8)) + list(range(SPLIT)):
-            i = b // 2
-            tile = "w%dt" % i
-            for h in (0, 1):
-                own, e, c = V(("owna", "ownb")[h], 32 * b, 32 * b + 1), 32 * b + 32, b % 2 + 2 * h
-                left = V(tile, c, 4 * e, 4)
-                if b < SPLIT:
-                    ts(left, V(("p0", "p1")[h], 0, e), own, None, A.is_lt)
-                else:
-                    act(left, V(("p3", "p4")[h], 0, e), -1.0, None, AF.Relu, own)
-                if b < 7:
-                    ts(V(tile, 4 * e + c, 1024, 4), V(("p0", "p1")[h], e, 256), own, None, A.is_le)
-                if b < SPLIT:
-                    next(ahead, None)
-            if b % 2:
-                if b == SPLIT + 1:
-                    act(V("rho"), V("p2", 0, 256))
-                if b >= SPLIT:
-                    w = V(tile, 0, 4 * e)
-                    act(w, w, func=AF.Sign)
-                else:
-                    quant("w%d" % i, V(tile))
-                    mm("p7", 256, ("sa", 0), ("w%d" % i, 0), i == 0, False)
-        rest(ahead)
-        if t == 0:
-            lists()
-        for b, bank in enumerate(("p5", "p6")):
-            act(quarter("f", b), V(bank, 0, 256))
-        for b in range(SPLIT // 2, 4):
-            quant("w%d" % b, V("w%dt" % b))
-            mm("p7", 256, ("sa", 0), ("w%d" % b, 0), False, False)
-        quant("eq", V("eqt"))
-        mm("p7", 256, ("sa", 0), ("eq", 0), False, True)
-        act(V("rk", 0, 256), V("p7", 0, 256), 2.0)
-        act(V("vr"), V("rk"), lst=V("dn"))
-        for b, bank in ((2, "p3"), (3, "p4")):
+        tt(V("key"), row("p5"), V("tiny"), A.add)
+        act(V("rho"), row("p2"))
+        for h in (0, 1):
+            act(one("hb", 2 + h), one("p3", 2 * h), func=AF.Identity, bias=F["k%d" % h])
+            act(quarter("gg", h), V("key"), func=AF.Sign, bias=one("hb", 2 + h))
+            scan(quarter("ll", h), quarter("gg", h), V("rho"), A.max, A.min, -0.75)
+        tt(V("nf", 0, 256), row("p5"), V("ll", 0, 256), A.not_equal)
+        tt(V("nf", 256, 384), row("p5", 128, 256), V("ll", 384, 512), A.not_equal)
+        scan(V("alt", 4, 1024, 4), V("eye", 1, 256), V("nf", 1, 256), A.max, A.min, one("eye", 0))
+        scan(V("alt", 513, 1024, 4), V("eye", 0, 128), V("nf", 256, 384), A.max, A.min)
+        tt(V("lt1", 1, 256), row("p5", 1, 256), V("rho", 0, 255), A.is_lt)
+        tt(V("le1", 1, 256), row("p5", 1, 256), V("rho", 0, 255), A.is_le)
+        scan(V("alt", 6, 1024, 4), V("le1", 1, 256), V("lt1", 1, 256), A.min, A.max)
+        quant("al", V("alt"))
+        mm("p2", 256, ("k", 0), ("al", 0))
+        act(V("up"), row("p2"), -1.0, func=AF.Relu, bias=F["nine"])
+        ts(V("nn"), V("up"), F["thr"], None, A.is_lt)
+        ts(V("mm"), V("up"), F["lo"], F["val"], A.min, A.is_equal)
+        scan(V("cc"), V("dc"), V("nn"), A.add, A.mult)
+        tt(V("cw"), V("cc"), V("mm"), A.mult)
+        for b, bank in enumerate(("p6", "p7", "p4", "p3")):
             mm(bank, 256, ("eb", 128 * b), ("x", 0))
-            act(quarter("f", b), V(bank, 0, 256))
-        for b in range(4):
-            act(quarter("fh", b), quarter("f", b), lst=V("cu"))
-        rest(levels(L1, L2))
-        more = levels(L2, 7)
-        next(more)
-        turn(V("tr"), V("vr"))
-        next(more)
-        add_halves(V("rl"), "tr")
-        next(more)
-        copy(V("rku"), V("rl"))
-        rest(more)
-        run("v", lambda: g.vector.tensor_copy(T["orow"][:, 0:256].indirect(T["rku"][:, :]), T["irow"][:, :]), [V("irow"), V("rku")], [V("orow", 0, 256)])
-        act(V("vo"), V("orow"), lst=V("dn"))
-        act(V("orow", 256, 384), V("orow", 0, 128))
-        act(V("sg", 0, 256), V("orow", 128, 384), lst=V("rku"))
-        k = V("p0", 0, 256)
-        ts(V("nn"), k, 4.0, fc(0), A.add, A.is_gt)
-        ts(V("mm"), k, fc(1), fc(3), A.max, A.is_equal)
-        scan(V("cc"), V("nn"), V("nn"), A.mult, A.add)
-        turn(V("to"), V("vo"))
-        tt(V("cw", 0, 256), V("cc"), V("mm"), A.mult)
-        copy(V("od"), V("to", 0, 512, 16))
+            act(quarter("f", b), row(bank))
+        tt(V("sm16"), row("p0"), V("m16"), A.mult)
+        scan(V("own"), V("ka"), V("sm16"), A.mult, A.add)
+        tt(V("eq"), row("p0"), V("own"), A.is_equal)
+        scan(V("es"), V("ke"), V("eq"), A.mult, A.add)
+        tt(V("ru"), V("kq"), V("es", 15, 256, 16), A.subtract)
+        if SR:
+            act(V("neg", 0, SR), V("own", 15, 16 * SR, 16), -1.0)
+        for q in range(16):
+            own, e, o = one("own", 16 * q + 15), 16 * q + 16, 256 * q
+            a, z = o if q < SL else o + e, o + 256 if q >= SR else o + e
+            if q < SL:
+                ts(V("cmp", o, o + e), row("p0", 0, e), own, None, A.is_ge)
+            else:
+                j = V("jk", o, o + e)
+                act(j, row("p1", 0, e), -1.0, func=AF.Relu, bias=own)
+                act(j, j, func=AF.Sign, total_to=one("acc", q))
+            if q < SR:
+                j = V("jk", o + e, o + 256)
+                act(j, row("p1", e, 256), func=AF.Relu, bias=one("neg", q))
+                act(j, j, -1.0, func=AF.Sign, total_to=one("acc", q))
+            elif q < 15:
+                ts(V("cmp", o + e, o + 256), row("p0", e, 256), own, None, A.is_gt)
+            if z > a:
+                scan(V("cs", o + 256 - (z - a), o + 256), V("cmp", a, z), V("cmp", a, z), A.add, A.max)
+        tt(V("rv"), V("ru"), V("cs", 255, 4096, 256), A.add)
+        tt(V("ri"), V("rv"), V("acc"), A.subtract)
+        ts(V("ra"), V("ri"), 240, None, A.bitwise_and)
+        tt(V("rp"), V("ri"), V("ra"), A.add)
+        ts(V("pu"), V("rp"), F["h16"], None, A.add)
+        copy(V("rku"), V("ri"))
+        scatter(V("vf"), V("pu"), V("cw"))
         for half in (0, 1):
-            act(V("vf", 256 * half, 256 * half + 256), V("cw"), lst=V("od", 16 * half, 16 * half + 16))
-        if last:
-            act(V("crow"), V("sg", 0, 256), lst=V("cu"))
-            dma("y", T.op[:, :], T["crow"][0:128:16, :], [V("crow")], [])
-        else:
-            act(V("vc"), V("sg"), lst=V("cd"))
-        add_halves(V("ol"), "to")
-        for half in (0, 1):
-            a, z = 256 * half, 256 * half + 256
-            if half == 0:
-                turn(V("tf", a, z), V("vf", a, z))
-            for o, i in (("r1", "tf"), ("r2", "r1"), ("r3", "r2")):
-                tt(V(o, a // 2, z // 2), V(i, a, z, 2), V(i, a + 1, z, 2), A.add)
-                a, z = a // 2, z // 2
-            p = 8 * half
+            a, p = 256 * half, 16 * half
+            turn(V("tf", a, a + 256), V("vf", a, a + 256))
             for s in (0, 1):
-                tt(V("da", 16 * s + p, 16 * s + p + 8), V("r3", a + s, z, 4), V("r3", a + s + 2, z, 4), A.add)
-            for s in (0, 16):
-                tt(V("db", s + p, s + p + 8), V("ol", p, p + 8), V("da", s + p, s + p + 8), A.subtract)
-            for s in (0, 16):
-                ts(V("lab", s + p, s + p + 8), V("db", s + p, s + p + 8), -float(ZC), None, A.add)
-            if half == 0:
-                turn(V("tf", 256, 512), V("vf", 256, 512))
+                scan(V("sm", a + 128 * s, a + 128 * s + 128), V("ka", 0, 128), V("tf", a + s, a + 256, 2), A.mult, A.add)
+            copy(V("lab", p, p + 16), V("sm", a + 15, a + 256, 16))
             for b in range(4):
                 tmp = V("ta", 512 * half + 128 * b, 512 * half + 128 * b + 128)
-                act(tmp, quarter("fh", b), lst=V("lab", p, p + 8))
-                tt(V("et", b, 512, 4) if half == 0 else V("lt", 128 * b, 128 * b + 128), quarter("fh", b), tmp, A.add, lst=V("lab", 16 + p, 24 + p))
+                act(tmp, quarter("f", b), lst=V("lab", p, p + 8))
+                tt(V("et", b, 512, 4) if half == 0 else V("lt", 128 * b, 128 * b + 128), quarter("f", b), tmp, A.add, lst=V("lab", p + 8, p + 16))
             if half == 0:
-                e = "e%d" % t
-                quant(e, V("et"))
-                order("g", [V("q" + e), V("z" + e)], [])
-                rid, pid = topo.addr(nxt)[:2]
-                m = topo.mask(core, nxt)
-                g.remote_dma(T["ql%d" % t][:, 0:128].bitcast(dt.uint8), T["q" + e][:, 0:128].bitcast(dt.uint8), T.sem["ar%d" % t], T.sem["left"], pid, rid, m)
-                g.remote_dma(T["zl%d" % t][:, 0:128], T["z" + e][:, 0:128], T.sem["ar%d" % t], T.sem["left"], pid, rid, m)
-                total["left"] = total.get("left", 0) + 2 * len(topo.engines(core, nxt))
-        ts(V("l32"), V("lt"), 32.0, None, A.mult)
+                quant("e%d" % t, V("et"))
+                send(t)
         for b in range(4):
             act(V("v32", 256 * b, 256 * b + 128), V("et", b, 512, 4), 32.0)
+            act(V("l32", 128 * b, 128 * b + 128), V("lt", 128 * b, 128 * b + 128), 32.0)
+        scatter(V("orow", 0, 256), V("rku"), V("irow"))
+        act(V("orow", 256, 384), V("orow", 0, 128))
+        act(V("sg", 0, 256), V("orow", 128, 384), lst=V("rku"))
         if last:
-            quant("v", V("vt"))
+            act(V("cop"), V("sg", 0, 256), lst=V("cu"))
+            dma("y", T.op[:, :], T["cop"][0:128:16, :], [V("cop")], [])
         else:
+            act(V("crow", 16, 272), V("sg", 0, 256), F["csg"], V("cu"))
+            act(V("vc"), V("sg"), lst=V("cd"))
             turn(V("tc"), V("vc"))
-            add_halves(V("cl"), "tc")
-        n = 2 * len(topo.engines(prv, core))
-        total["ar%d" % t] = n
-        for z in ("ql%d" % t, "zl%d" % t):
-            acc.setdefault(z, []).append((V(z), True, "r", "ar%d" % t, n, {}))
+            tt(V("cl"), V("tc", 0, 512, 32), V("tc", 16, 512, 32), A.add)
+            copy(V("cd"), V("tc", 0, 512, 16))
+            ts(V("cu"), V("cl"), -float(ZC), None, A.add)
         for b, bank in enumerate(("p0", "p1", "p7", "p3")):
             mm(bank, 128, ("w", 128 * b), ("l%d" % t, 0))
             tt(V("v32", 256 * b + 128, 256 * b + 256), V(bank, 0, 128), V("l32", 128 * b, 128 * b + 128), A.add)
@@ -401,9 +406,40 @@ def rank_program(g, core, T, topo):
     quant("x", V("xn"))
     mm("p4", 256, ("v", 0), ("x", 0))
     copy(V("ys"), V("p4", 0, 256))
+    dma("y", T.y[:, :], T["ys"][:, :], [V("ys")], [])
     dma("y", T.oc[:, :], T["qx"][:, :].bitcast(dt.uint8), [V("qx")], [])
     for i in range(4):
         dma("y" if i % 2 else "s", T.osc[4 * i:4 * i + 4, :], T["zx"][32 * i:32 * i + 4, :], [V("zx")], [])
-    dma("y", T.y[:, :], T["ys"][:, :], [V("ys")], [])
+
+    total = {}
+    know = {q: {} for q in Q}
+    seen = {}
+    for i in arrange(calls):
+        c = calls[i]
+        q, kind = c["q"], c["kind"]
+        if kind == "arrives":
+            total[c["call"]] = 2 * len(topo.engines(prv, core))
+            remember(seen, q, [], c["writes"], (c["call"], total[c["call"]], {}))
+            continue
+        need = {}
+        for e in follows(seen, q, c["reads"], c["writes"] if kind != "adds" else []):
+            sem, n, theirs = e[3]
+            if need.get(sem, (0, 0))[0] < n:
+                need[sem] = (n, theirs)
+        if q == "g" and "cg" in total:
+            need["cg"] = (total["cg"], {})
+        for sem, (n, theirs) in need.items():
+            if know[q].get(sem, 0) < n:
+                Q[q].wait_ge(T.sem[sem], n)
+                for s, k in list(theirs.items()) + [(sem, n)]:
+                    know[q][s] = max(know[q].get(s, 0), k)
+        if kind == "send":
+            c["call"]()
+            total["left"] = total.get("left", 0) + 2 * len(topo.engines(core, nxt))
+            continue
+        sem, n = ("d%d" % len([s for s in total if s[0] == "d"]), 16) if kind == "dma" else ("c" + q, 1)
+        c["call"]().then_inc(T.sem[sem], n)
+        total[sem] = total.get(sem, 0) + n
+        remember(seen, q, c["reads"], c["writes"], (sem, total[sem], dict(know[q])))
     for sem, n in total.items():
         g.wait_ge(T.sem[sem], n)

@@ -4,9 +4,12 @@ ROUNDS = 3
 ZC = 384
 WIN = 400
 XS = (0, 1)
-SL, SR = 7, 3
+VQ = (15, 14, 13)
+WIDE = (256, 192, 128, 128)
+FIRST = ("p0", "p3", "p4", "p2", "p1")
+BIG = 2.0 ** 90
 TINY = 2.0 ** -17
-HOP, FAR, LOAD = 200, 2200, 1800
+HOP, FAR, NEAR, LOAD = 180, 4000, 1600, 1800
 
 SLACK, PASSES = 150, 4
 
@@ -14,24 +17,24 @@ SCRATCH = {}
 PSUM = ["p%d" % i for i in range(8)]
 for _n in PSUM:
     SCRATCH[_n] = ("psum", [128, 512], "float32")
-for _n, _c in [("u", 128), ("v", 128), ("w", 512), ("us", 256), ("x", 256), ("eb", 512), ("k", 128), ("hs", 128), ("hn", 130), ("h", 256), ("al", 256),
-               ("e0", 128), ("e1", 128), ("e2", 128), ("l0", 128), ("l1", 128), ("l2", 128)]:
+for _n, _c in [("u", 128), ("v", 128), ("w", 512), ("us", 256), ("x", 1024), ("eb", 512), ("k", 128), ("hs", 128), ("gs", 128), ("w0", 256), ("w1", 192), ("w2", 128), ("w3", 128), ("h", 256), ("al", 256),
+               ("e", 128), ("n", 768)]:
     SCRATCH["q" + _n] = ("sbuf", [128, _c], "float8_e4m3fn_x4")
     SCRATCH["z" + _n] = ("sbuf", [128, _c], "uint8")
-for _d, _l in [("bfloat16", [("ut", 512), ("vt", 512), ("xt", 1024), ("xn", 1024), ("ebt", 528), ("half", 528), ("kt", 512), ("hst", 512), ("hnt", 520),
-                             ("ht", 1024), ("alt", 1024), ("rho", 256), ("gg", 512), ("ll", 512), ("nf", 384), ("lt1", 256), ("le1", 256),
-                             ("j16", 256), ("m16", 256), ("ka", 256), ("ke", 256), ("eye", 256), ("irow", 256), ("eq", 256), ("es", 256),
-                             ("cmp", 4096), ("cs", 4096), ("jk", 4096), ("f", 1024), ("orow", WIN), ("sg", WIN), ("crow", 272), ("dc", 256), ("up", 256),
+for _d, _l in [("bfloat16", [("ut", 512), ("vt", 512), ("xt", 1024), ("xn", 1024), ("ebt", 528), ("half", 528), ("kt", 512), ("hst", 512), ("gst", 512),
+                             ("ht", 1024), ("alt", 1024), ("rho", 256), ("gg", 512), ("ll", 512), ("nf", 384), ("ex", 256), ("ey", 256),
+                             ("j16", 256), ("m16", 256), ("ka", 256), ("ke", 256), ("eye", 256), ("irow", 256), ("mb", 256), ("es", 256),
+                             ("w0t", 1024), ("w1t", 768), ("w2t", 512), ("w3t", 512), ("cs", 4096), ("jk", 4096), ("f", 1024), ("orow", WIN), ("sg", WIN), ("crow", 272), ("dc", 256), ("up", 256),
                              ("nn", 256), ("mm", 256), ("cc", 256), ("cw", 256), ("vf", 512), ("tf", 512), ("sm", 512), ("vc", 512), ("tc", 512),
-                             ("ta", 1024), ("et", 512), ("lt", 512), ("l32", 512), ("v32", 1024)]),
-               ("float32", [("sm16", 256), ("own", 256), ("key", 256), ("tiny", 256), ("cop", 256), ("ys", 256), ("fc", 32), ("hb", 8), ("neg", 16),
-                            ("kq", 16), ("acc", 16), ("ru", 16), ("rv", 16), ("cl", 16)]),
-               ("int32", [("ci", 16), ("cfi", 16), ("uli", 16), ("ri", 16), ("ra", 16), ("rp", 16)]),
-               ("uint16", [("ul", 16), ("cd", 32), ("cu", 16), ("rku", 16), ("pu", 16), ("lab", 32)])]:
+                             ("ta", 1024), ("et", 512), ("tb", 512), ("fn", 1024), ("v32", 1024)]),
+               ("float32", [("sm16", 256), ("own", 256), ("key", 256), ("tiny", 256), ("cop", 256), ("ys", 256), ("fc", 32), ("hb", 8), ("rw", 16),
+                            ("kq", 16), ("kr", 16), ("acc", 16), ("ru", 16), ("rv", 16), ("cl", 16)]),
+               ("int32", [("ci", 16), ("cfi", 16), ("ri", 16), ("ra", 16), ("rp", 16)]),
+               ("uint16", [("ul", 16), ("cd", 32), ("cu", 16), ("rku", 16), ("pu", 16), ("lab", 32), ("lo", 48), ("li", 48)])]:
     for _n, _c in _l:
         SCRATCH[_n] = ("sbuf", [128, _c], _d)
 
-SEMAPHORES = ["cv", "cs", "ct", "cg", "left"] + ["ar%d" % t for t in range(ROUNDS)] + ["d%d" % i for i in range(20)]
+SEMAPHORES = ["cv", "cs", "ct", "cg", "left"] + [a + str(t) for a in ("ax", "al") for t in range(ROUNDS)] + ["d%d" % i for i in range(20)]
 
 
 def meet(a, b):
@@ -207,16 +210,17 @@ def rank_program(g, core, T, topo):
         k = {"allow_small_or_imprecise_dtypes": True} if small else {}
         put("g", lambda: g.iota(ap(out), pattern, base, cm, **k), [], [out], 130 + 1.66 * size(out))
 
-    def send(t):
-        e = "e%d" % t
+    def send(pairs, sem, ns):
         rid, pid = topo.addr(nxt)[:2]
-        m = topo.mask(core, nxt)
+
+        def raw(v):
+            return ap(v).bitcast(dt.uint8) if v[0][0] == "q" else ap(v)
 
         def call():
-            g.remote_dma(T["ql%d" % t][:, 0:128].bitcast(dt.uint8), T["q" + e][:, 0:128].bitcast(dt.uint8), T.sem["ar%d" % t], T.sem["left"], pid, rid, m)
-            g.remote_dma(T["zl%d" % t][:, 0:128], T["z" + e][:, 0:128], T.sem["ar%d" % t], T.sem["left"], pid, rid, m)
-        sent = put("g", call, [V("q" + e), V("z" + e)], [], FAR, "send", 200)
-        put("r", "ar%d" % t, [], [V("ql%d" % t), V("zl%d" % t)], 0, "arrives", after=[sent])
+            for there, here in pairs:
+                g.remote_dma(raw(there), raw(here), T.sem[sem], T.sem["left"], pid, rid, topo.mask(core, nxt))
+        sent = put("g", call, [p[1] for p in pairs], [], ns, "send", 200)
+        put("r", sem, [], [p[0] for p in pairs], 0, "arrives", after=[sent])
 
     I = {n: one("ci", i) for i, n in enumerate(("p", "r", "m", "s", "g", "h"))}
     F = {n: one("fc", i) for i, n in enumerate(("r", "m", "s", "g", "h", "p", "gs", "m7", "thr", "val", "lo", "csg", "h16", "lw",
@@ -230,31 +234,28 @@ def rank_program(g, core, T, topo):
     dma("y", T["zw"][:, :], T.ws[:, :], [V("ut"), V("xt")], [V("zw")])
     dma("y", T["vt"][:, :], T.v[:, :], [V("ut"), V("xt")], [V("vt")])
 
-    iota(V("uli", 0, 8), [[16, 8]], 0, 0)
-    iota(V("uli", 8, 16), [[0, 8]], 1, 0)
     iota(I["p"], [[0, 1]], 0, 1)
     iota(V("j16"), [[0, 16], [1, 16]], 0, 0, True)
     iota(V("irow"), [[1, 256]], 0, 0, True)
-    iota(V("kq"), [[16, 16]], 16, 0, True)
+    iota(V("kr"), [[16, 16]], 15, 0, True)
     fill(V("half"), 0.5)
     put("g", lambda: g.affine_select(T["ebt"][:, :], T["half"][:, :], [[1, 528]], A.is_equal, 0.0, -4, -4), [V("half")], [V("ebt")], 1050)
     for b in range(4):
         quant("eb", V("ebt", 4 - b, 516 - b), 128 * b, 128 * b + 128)
     fill(V("hst"), 1.0 / 512)
     quant("hs", V("hst"))
-    fill(V("hnt"), 0.0)
-    fill(V("hnt", 8, 12), -1.0 / 512)
-    quant("hn", V("hnt"))
     fill(V("kt"), 2.0)
-    fill(V("kt", 2, 512, 4), 1.0 / 128)
-    fill(V("kt", 3, 512, 4), 0.0)
+    fill(V("kt", 2, 512, 4), -1.0)
     quant("k", V("kt"))
-    for v in (V("ht", 2, 1024, 4), V("ht", 3, 1024, 4), V("alt"), V("acc"), one("cs", 4095), V("kq", 0, SL), V("crow", 0, 16), V("vf")):
+    for v in (V("ht", 2, 1024, 4), V("ht", 3, 1024, 4), V("alt", 0, 4), V("alt", 1, 512, 4), V("alt", 3, 1024, 4), V("acc"), V("cs", 255, 4096, 256),
+              V("crow", 0, 16), V("vf"), V("w0t", 832), V("w1t", 576), V("w2t", 320), V("w3t", 64)):
         fill(v, 0.0)
     fill(V("orow", 256, WIN), float(ZC))
     fill(V("sg", 256, WIN), float(ZC))
-    fill(F["nine"], 9.0)
-    copy(V("ul"), V("uli"))
+    fill(F["nine"], 8.0)
+    iota(V("gst"), [[1, 8], [0, 64]], 0, 0, True)
+    ts(V("ul", 0, 8), V("kr", 0, 8), -15.0, None, A.add)
+    fill(V("ul", 8, 16), 1)
     ts(I["r"], I["p"], 15, None, A.bitwise_and)
     ts(I["m"], I["p"], 1, 7, A.arith_shift_right, A.bitwise_and)
     ts(I["s"], I["p"], 1, None, A.bitwise_and)
@@ -265,7 +266,12 @@ def rank_program(g, core, T, topo):
     copy(V("fc", 1, 5), V("ci", 2, 6))
     ts(V("m16"), V("j16"), F["r"], None, A.is_equal)
     ts(V("ka"), V("j16"), 0.0, None, A.is_gt)
-    ts(V("ke"), V("j16"), F["r"], None, A.is_gt)
+    ts(V("ke"), V("j16"), F["r"], 2 * BIG, A.is_gt, A.mult)
+    ts(V("ke"), V("ke"), -BIG, None, A.add)
+    ts(V("mb"), V("m16"), 2 * BIG, -BIG, A.mult, A.add)
+    ts(V("kq"), V("kr"), F["r"], None, A.subtract)
+    ts(V("gst"), V("gst"), F["g"], None, A.is_equal)
+    quant("gs", V("gst"))
     ts(V("eye"), V("irow"), F["p"], None, A.is_equal)
     act(V("tiny"), V("irow"), TINY)
     ts(F["k0"], F["p"], -TINY, -TINY / 2, A.mult, A.add)
@@ -296,33 +302,32 @@ def rank_program(g, core, T, topo):
     for t in range(ROUNDS):
         last = t == ROUNDS - 1
         tt(V("dc"), V("crow", 15, 271), V("crow", 16, 272), A.subtract)
-        quant("x", V("xt") if t == 0 else V("xn"))
-        mm("p0", 256, ("us", 0), ("x", 0))
-        mm("p1", 256, ("us", 0), ("x", 0))
-        mm("p3", 128, ("x", 0), ("u", 0))
-        mm("p4", 128, ("x", 128), ("u", 0))
-        mm("p2", 256, ("us", 128), ("x", 0))
+        X = 256 * t
+        quant("x", V("xt") if t == 0 else V("xn"), X, X + 256)
+        send([(V("qn", X, X + 256), V("qx", X, X + 256)), (V("zn", X, X + 256), V("zx", X, X + 256))], "ax%d" % t, FAR)
+        first = {"p0": (256, ("us", 0), ("x", X)), "p1": (256, ("us", 0), ("x", X)), "p2": (256, ("us", 128), ("x", X)),
+                 "p3": (128, ("x", X), ("u", 0)), "p4": (128, ("x", X + 128), ("u", 0))}
+        for i, bank in enumerate(FIRST):
+            mm(bank, *first[bank])
+            calls[-1]["after"] = [len(calls) - 2] if i else []
         for h, bank in enumerate(("p3", "p4")):
             act(one("hb", h), one(bank, 1), -1.0)
-            act(V("ht", h, 1024, 4), row("p2"), func=AF.Sign, bias=one("hb", h))
+            act(V("ht", h, 1024, 4), row("p2"), func=AF.Sign, bias=one("hb", h), total_to=one("hb", 4 + h))
         quant("h", V("ht"))
         mm("p5", 256, ("hs", 0), ("h", 0))
-        mm("p3", 128, ("h", 0), ("hn", 2), True, False)
-        mm("p3", 128, ("h", 128), ("hn", 0), False, True)
         mm("p2", 256, ("hs", 0), ("h", 0))
         tt(V("key"), row("p5"), V("tiny"), A.add)
         act(V("rho"), row("p2"))
         for h in (0, 1):
-            act(one("hb", 2 + h), one("p3", 2 * h), func=AF.Identity, bias=F["k%d" % h])
+            act(one("hb", 2 + h), one("hb", 4 + h), 1.0 / 512, func=AF.Identity, bias=F["k%d" % h])
             act(quarter("gg", h), V("key"), func=AF.Sign, bias=one("hb", 2 + h))
             scan(quarter("ll", h), quarter("gg", h), V("rho"), A.max, A.min, -0.75)
         tt(V("nf", 0, 256), row("p5"), V("ll", 0, 256), A.not_equal)
         tt(V("nf", 256, 384), row("p5", 128, 256), V("ll", 384, 512), A.not_equal)
         scan(V("alt", 4, 1024, 4), V("eye", 1, 256), V("nf", 1, 256), A.max, A.min, one("eye", 0))
         scan(V("alt", 513, 1024, 4), V("eye", 0, 128), V("nf", 256, 384), A.max, A.min)
-        tt(V("lt1", 1, 256), row("p5", 1, 256), V("rho", 0, 255), A.is_lt)
-        tt(V("le1", 1, 256), row("p5", 1, 256), V("rho", 0, 255), A.is_le)
-        scan(V("alt", 6, 1024, 4), V("le1", 1, 256), V("lt1", 1, 256), A.min, A.max)
+        tt(V("alt", 6, 512, 4), V("eye", 1, 128), V("nf", 1, 128), A.min)
+        tt(V("alt", 514, 1024, 4), V("eye", 0, 128), V("nf", 256, 384), A.min)
         quant("al", V("alt"))
         mm("p2", 256, ("k", 0), ("al", 0))
         act(V("up"), row("p2"), -1.0, func=AF.Relu, bias=F["nine"])
@@ -331,55 +336,59 @@ def rank_program(g, core, T, topo):
         scan(V("cc"), V("dc"), V("nn"), A.add, A.mult)
         tt(V("cw"), V("cc"), V("mm"), A.mult)
         for b, bank in enumerate(("p6", "p7", "p4", "p3")):
-            mm(bank, 256, ("eb", 128 * b), ("x", 0))
-            act(quarter("f", b), row(bank))
-        tt(V("sm16"), row("p0"), V("m16"), A.mult)
-        scan(V("own"), V("ka"), V("sm16"), A.mult, A.add)
-        tt(V("eq"), row("p0"), V("own"), A.is_equal)
-        scan(V("es"), V("ke"), V("eq"), A.mult, A.add)
+            mm(bank, 256, ("eb", 128 * b), ("x", X))
+            act(quarter("f", b), row(bank), 32.0)
+        tt(V("sm16"), row("p0"), V("mb"), A.min)
+        scan(V("own"), V("ke"), V("sm16"), A.min, A.max)
+        tt(V("w0t", 0, 1024, 4), row("p0"), V("own"), A.is_le)
+        scan(V("es"), V("ka"), V("w0t", 0, 1024, 4), A.mult, A.add)
+        for i, wide in enumerate(WIDE):
+            for c in range(4):
+                q = 16 - 4 * i - c
+                if q == 16:
+                    continue
+                own, e, o = one("own", 16 * q + 15), 16 * q, 256 * q
+                w = V("w%dt" % i, c, 4 * e, 4)
+                if q in VQ:
+                    ts(w, row("p0", 0, e), own, None, A.is_lt)
+                    scan(V("cs", o + 256 - e, o + 256), w, w, A.add, A.max)
+                else:
+                    act(V("jk", o, o + e), row("p1", 0, e), -1.0, func=AF.Relu, bias=own)
+                    act(w, V("jk", o, o + e), func=AF.Sign, total_to=one("acc", q))
+            quant("w%d" % i, V("w%dt" % i))
+            mm("p6", wide, ("gs", 0), ("w%d" % i, 0), i == 0, i == 3)
+        tt(V("ex"), row("p6"), V("m16"), A.mult)
+        scan(V("ey"), V("ka"), V("ex"), A.mult, A.add)
         tt(V("ru"), V("kq"), V("es", 15, 256, 16), A.subtract)
-        if SR:
-            act(V("neg", 0, SR), V("own", 15, 16 * SR, 16), -1.0)
-        for q in range(16):
-            own, e, o = one("own", 16 * q + 15), 16 * q + 16, 256 * q
-            a, z = o if q < SL else o + e, o + 256 if q >= SR else o + e
-            if q < SL:
-                ts(V("cmp", o, o + e), row("p0", 0, e), own, None, A.is_ge)
-            else:
-                j = V("jk", o, o + e)
-                act(j, row("p1", 0, e), -1.0, func=AF.Relu, bias=own)
-                act(j, j, func=AF.Sign, total_to=one("acc", q))
-            if q < SR:
-                j = V("jk", o + e, o + 256)
-                act(j, row("p1", e, 256), func=AF.Relu, bias=one("neg", q))
-                act(j, j, -1.0, func=AF.Sign, total_to=one("acc", q))
-            elif q < 15:
-                ts(V("cmp", o + e, o + 256), row("p0", e, 256), own, None, A.is_gt)
-            if z > a:
-                scan(V("cs", o + 256 - (z - a), o + 256), V("cmp", a, z), V("cmp", a, z), A.add, A.max)
-        tt(V("rv"), V("ru"), V("cs", 255, 4096, 256), A.add)
-        tt(V("ri"), V("rv"), V("acc"), A.subtract)
+        tt(V("rv"), V("ru"), V("cs", 255, 4096, 256), A.subtract)
+        tt(V("rw"), V("rv"), V("acc"), A.subtract)
+        tt(V("ri"), V("rw"), V("ey", 15, 256, 16), A.add)
         ts(V("ra"), V("ri"), 240, None, A.bitwise_and)
         tt(V("rp"), V("ri"), V("ra"), A.add)
         ts(V("pu"), V("rp"), F["h16"], None, A.add)
         copy(V("rku"), V("ri"))
         scatter(V("vf"), V("pu"), V("cw"))
         for half in (0, 1):
-            a, p = 256 * half, 16 * half
+            a = 256 * half
             turn(V("tf", a, a + 256), V("vf", a, a + 256))
             for s in (0, 1):
-                scan(V("sm", a + 128 * s, a + 128 * s + 128), V("ka", 0, 128), V("tf", a + s, a + 256, 2), A.mult, A.add)
-            copy(V("lab", p, p + 16), V("sm", a + 15, a + 256, 16))
-            for b in range(4):
-                tmp = V("ta", 512 * half + 128 * b, 512 * half + 128 * b + 128)
-                act(tmp, quarter("f", b), lst=V("lab", p, p + 8))
-                tt(V("et", b, 512, 4) if half == 0 else V("lt", 128 * b, 128 * b + 128), quarter("f", b), tmp, A.add, lst=V("lab", p + 8, p + 16))
-            if half == 0:
-                quant("e%d" % t, V("et"))
-                send(t)
+                o = 256 * s + 128 * half
+                scan(V("sm", o, o + 128), V("ka", 0, 128), V("tf", a + s, a + 256, 2), A.mult, A.add)
+                if half == 0:
+                    copy(V("lo", 16 * t + 8 * s, 16 * t + 8 * s + 8), V("sm", o + 15, o + 128, 16))
+        send([(V("li", 16 * t, 16 * t + 16), V("lo", 16 * t, 16 * t + 16))], "al%d" % t, NEAR)
+        copy(V("lab"), V("sm", 15, 512, 16))
         for b in range(4):
-            act(V("v32", 256 * b, 256 * b + 128), V("et", b, 512, 4), 32.0)
-            act(V("l32", 128 * b, 128 * b + 128), V("lt", 128 * b, 128 * b + 128), 32.0)
+            act(quarter("ta", b), quarter("f", b), lst=V("lab", 0, 16))
+            tt(quarter("v32", b), quarter("f", b), quarter("ta", b), A.add, lst=V("lab", 16, 32))
+        for b, bank in enumerate(("p7", "p4", "p3", "p5")):
+            mm(bank, 256, ("eb", 128 * b), ("n", X))
+            act(quarter("fn", b), row(bank))
+        for b in range(4):
+            tmp = V("tb", 128 * b, 128 * b + 128)
+            act(tmp, quarter("fn", b), lst=V("li", 16 * t, 16 * t + 8))
+            tt(V("et", b, 512, 4), quarter("fn", b), tmp, A.add, lst=V("li", 16 * t + 8, 16 * t + 16))
+        quant("e", V("et"))
         scatter(V("orow", 0, 256), V("rku"), V("irow"))
         act(V("orow", 256, 384), V("orow", 0, 128))
         act(V("sg", 0, 256), V("orow", 128, 384), lst=V("rku"))
@@ -394,8 +403,9 @@ def rank_program(g, core, T, topo):
             copy(V("cd"), V("tc", 0, 512, 16))
             ts(V("cu"), V("cl"), -float(ZC), None, A.add)
         for b, bank in enumerate(("p0", "p1", "p7", "p3")):
-            mm(bank, 128, ("w", 128 * b), ("l%d" % t, 0))
-            tt(V("v32", 256 * b + 128, 256 * b + 256), V(bank, 0, 128), V("l32", 128 * b, 128 * b + 128), A.add)
+            low = V("v32", 256 * b + 128, 256 * b + 256)
+            mm(bank, 128, ("w", 128 * b), ("e", 0))
+            tt(low, V(bank, 0, 128), low, A.add)
         for b in range(4):
             out, win, lst = V("xn", b, 1024, 4), quarter("v32", b), V("rku")
             if b in XS:
@@ -403,13 +413,14 @@ def rank_program(g, core, T, topo):
             else:
                 ts(out, win, 0.03125, None, A.mult, lst=lst)
 
-    quant("x", V("xn"))
-    mm("p4", 256, ("v", 0), ("x", 0))
+    X = 256 * ROUNDS
+    quant("x", V("xn"), X, X + 256)
+    mm("p4", 256, ("v", 0), ("x", X))
     copy(V("ys"), V("p4", 0, 256))
     dma("y", T.y[:, :], T["ys"][:, :], [V("ys")], [])
-    dma("y", T.oc[:, :], T["qx"][:, :].bitcast(dt.uint8), [V("qx")], [])
+    dma("y", T.oc[:, :], T["qx"][:, X:X + 256].bitcast(dt.uint8), [V("qx", X)], [])
     for i in range(4):
-        dma("y" if i % 2 else "s", T.osc[4 * i:4 * i + 4, :], T["zx"][32 * i:32 * i + 4, :], [V("zx")], [])
+        dma("y" if i % 2 else "s", T.osc[4 * i:4 * i + 4, :], T["zx"][32 * i:32 * i + 4, X:X + 256], [V("zx", X)], [])
 
     total = {}
     know = {q: {} for q in Q}
@@ -418,7 +429,7 @@ def rank_program(g, core, T, topo):
         c = calls[i]
         q, kind = c["q"], c["kind"]
         if kind == "arrives":
-            total[c["call"]] = 2 * len(topo.engines(prv, core))
+            total[c["call"]] = len(c["writes"]) * len(topo.engines(prv, core))
             remember(seen, q, [], c["writes"], (c["call"], total[c["call"]], {}))
             continue
         need = {}
@@ -435,7 +446,7 @@ def rank_program(g, core, T, topo):
                     know[q][s] = max(know[q].get(s, 0), k)
         if kind == "send":
             c["call"]()
-            total["left"] = total.get("left", 0) + 2 * len(topo.engines(core, nxt))
+            total["left"] = total.get("left", 0) + len(c["reads"]) * len(topo.engines(core, nxt))
             continue
         sem, n = ("d%d" % len([s for s in total if s[0] == "d"]), 16) if kind == "dma" else ("c" + q, 1)
         c["call"]().then_inc(T.sem[sem], n)

@@ -4,30 +4,32 @@ ROUNDS = 3
 ZC = 384
 WIN = 400
 XS = (0, 1)
-VQ = (15, 14, 13)
+VQ = (12, 11, 10, 9)
 WIDE = (256, 192, 128, 128)
 FIRST = ("p0", "p3", "p4", "p2", "p1")
 BIG = 2.0 ** 90
-TINY = 2.0 ** -17
-HOP, FAR, NEAR, LOAD = 180, 4000, 1600, 1800
+RHO = False
+OWN = ((128, 256), (0, 128))
+FB, NB, RB, KB = ("p7", "p4", "p3", "p7"), ("p4", "p3", "p7", "p1"), "p6", ("p5", "p2")
+HOP, FAR, NEAR, LOAD = 200, 4000, 1600, 1800
 
-SLACK, PASSES = 150, 4
+SLACK, PASSES = (30, 90, 150), 4
 
 SCRATCH = {}
 PSUM = ["p%d" % i for i in range(8)]
 for _n in PSUM:
     SCRATCH[_n] = ("psum", [128, 512], "float32")
-for _n, _c in [("u", 128), ("v", 128), ("w", 512), ("us", 256), ("x", 1024), ("eb", 512), ("k", 128), ("hs", 128), ("gs", 128), ("w0", 256), ("w1", 192), ("w2", 128), ("w3", 128), ("h", 256), ("al", 256),
+for _n, _c in [("u", 128), ("v", 128), ("w", 512), ("us", 256), ("x", 1024), ("eb", 512), ("k", 128), ("gs", 128), ("w0", 256), ("w1", 192), ("w2", 128), ("w3", 128), ("h", 256), ("al", 256),
                ("e", 128), ("n", 768)]:
     SCRATCH["q" + _n] = ("sbuf", [128, _c], "float8_e4m3fn_x4")
     SCRATCH["z" + _n] = ("sbuf", [128, _c], "uint8")
-for _d, _l in [("bfloat16", [("ut", 512), ("vt", 512), ("xt", 1024), ("xn", 1024), ("ebt", 528), ("half", 528), ("kt", 512), ("hst", 512), ("gst", 512),
-                             ("ht", 1024), ("alt", 1024), ("rho", 256), ("gg", 512), ("ll", 512), ("nf", 384), ("ex", 256), ("ey", 256),
+for _d, _l in [("bfloat16", [("ut", 512), ("vt", 512), ("xt", 1024), ("xn", 1024), ("ebt", 528), ("half", 528), ("kt", 512), ("gst", 512),
+                             ("ht", 1024), ("alt", 1024), ("rho", 256), ("tri", 128), ("gg", 512), ("ll", 512), ("nf", 384), ("ex", 256), ("ey", 256),
                              ("j16", 256), ("m16", 256), ("ka", 256), ("ke", 256), ("eye", 256), ("irow", 256), ("mb", 256), ("es", 256),
                              ("w0t", 1024), ("w1t", 768), ("w2t", 512), ("w3t", 512), ("cs", 4096), ("jk", 4096), ("f", 1024), ("orow", WIN), ("sg", WIN), ("crow", 272), ("dc", 256), ("up", 256),
                              ("nn", 256), ("mm", 256), ("cc", 256), ("cw", 256), ("vf", 512), ("tf", 512), ("sm", 512), ("vc", 512), ("tc", 512),
                              ("ta", 1024), ("et", 512), ("tb", 512), ("fn", 1024), ("v32", 1024)]),
-               ("float32", [("sm16", 256), ("own", 256), ("key", 256), ("tiny", 256), ("cop", 256), ("ys", 256), ("fc", 32), ("hb", 8), ("rw", 16),
+               ("float32", [("sm16", 256), ("own", 256), ("cop", 256), ("ys", 256), ("fc", 32), ("hb", 8), ("rw", 16),
                             ("kq", 16), ("kr", 16), ("acc", 16), ("ru", 16), ("rv", 16), ("cl", 16)]),
                ("int32", [("ci", 16), ("cfi", 16), ("ri", 16), ("ra", 16), ("rp", 16)]),
                ("uint16", [("ul", 16), ("cd", 32), ("cu", 16), ("rku", 16), ("pu", 16), ("lab", 32), ("lo", 48), ("li", 48)])]:
@@ -76,7 +78,7 @@ def arrange(calls):
     def hop(j, i):
         return 0 if calls[j]["q"] == calls[i]["q"] == "t" else HOP
 
-    def place(first, then, way):
+    def place(first, then, way, slack):
         left = [len(b) for b in first]
         ready, done, free, placed, open_ = [0.0] * n, [0.0] * n, {}, [], {}
         for i in range(n):
@@ -87,7 +89,7 @@ def arrange(calls):
             now = max(free.get(q, 0), min(ready[i] for i in open_[q]))
             i = max(open_[q], key=lambda i: way[i] - max(0, ready[i] - now))
             if ready[i] > now:
-                fits = [j for j in open_[q] if ready[j] <= now and now + calls[j]["hold"] <= ready[i] + SLACK]
+                fits = [j for j in open_[q] if ready[j] <= now and now + calls[j]["hold"] <= ready[i] + slack]
                 if not fits:
                     free[q] = min(ready[j] for j in open_[q] if ready[j] > now)
                     continue
@@ -101,14 +103,16 @@ def arrange(calls):
                 if not left[j]:
                     open_.setdefault(calls[j]["q"], []).append(j)
         return placed, done
-    way = [0.0] * n
+    alone = [0.0] * n
     for i in reversed(range(n)):
-        way[i] = calls[i]["long"] + max([hop(i, j) + way[j] for j in behind[i]], default=0)
+        alone[i] = calls[i]["long"] + max([hop(i, j) + alone[j] for j in behind[i]], default=0)
     tries = []
-    for _ in range(PASSES):
-        placed, done = place(before, behind, way)
-        tries.append((max(done), placed))
-        way = place(behind, before, done)[1]
+    for slack in SLACK:
+        way = alone
+        for _ in range(PASSES):
+            placed, done = place(before, behind, way, slack)
+            tries.append((max(done), placed))
+            way = place(behind, before, done, slack)[1]
     return min(tries)[1]
 
 
@@ -192,6 +196,12 @@ def rank_program(g, core, T, topo):
             k["accum_out"] = ap(total_to)
         put("s", lambda: g.scalar.activation(ap(out), ind(in_, lst), func, **k), some(in_, lst, bias, scale), some(out, total_to), cycles(size(out), 1, lst))
 
+    def lay(v, c):
+        act(v, V("half", 0, size(v)), 2 * c) if c != 0.5 else act(v, V("half", 0, size(v)))
+
+    def pick_diagonal(out, in_, base):
+        put("g", lambda: g.affine_select(ap(out), ap(in_), [[1, size(out)]], A.is_equal, 0.0, base, -1), [in_], [out], 170 + 1.66 * size(out))
+
     def turn(out, in_):
         put("v", lambda: g.vector.transpose(ap(out), ap(in_)), [in_], [out], cycles(size(out), narrow(out)))
 
@@ -219,12 +229,13 @@ def rank_program(g, core, T, topo):
         def call():
             for there, here in pairs:
                 g.remote_dma(raw(there), raw(here), T.sem[sem], T.sem["left"], pid, rid, topo.mask(core, nxt))
-        sent = put("g", call, [p[1] for p in pairs], [], ns, "send", 200)
+        mine = [i for i, c in enumerate(calls) if c["q"] == "g"]
+        sent = put("g", call, [p[1] for p in pairs], [], ns, "send", 200, mine)
         put("r", sem, [], [p[0] for p in pairs], 0, "arrives", after=[sent])
 
     I = {n: one("ci", i) for i, n in enumerate(("p", "r", "m", "s", "g", "h"))}
     F = {n: one("fc", i) for i, n in enumerate(("r", "m", "s", "g", "h", "p", "gs", "m7", "thr", "val", "lo", "csg", "h16", "lw",
-                                                "zl", "zu", "k0", "k1", "t0", "t1", "t2", "nine"))}
+                                                "zl", "zu", "k0", "k1", "t0", "t1", "one", "nine"))}
 
     dma("y", T["ut"][:, :], T.u[:, :], [], [V("ut")])
     dma("s", T["xt"][:, 0:512], T.x[:, 0:512], [], [V("xt", 0, 512)])
@@ -242,17 +253,16 @@ def rank_program(g, core, T, topo):
     put("g", lambda: g.affine_select(T["ebt"][:, :], T["half"][:, :], [[1, 528]], A.is_equal, 0.0, -4, -4), [V("half")], [V("ebt")], 1050)
     for b in range(4):
         quant("eb", V("ebt", 4 - b, 516 - b), 128 * b, 128 * b + 128)
-    fill(V("hst"), 1.0 / 512)
-    quant("hs", V("hst"))
-    fill(V("kt"), 2.0)
-    fill(V("kt", 2, 512, 4), -1.0)
+    fill(V("kt"), 1.0 / 512)
+    fill(V("kt", 2, 512, 4), -1.0 / 1024)
     quant("k", V("kt"))
-    for v in (V("ht", 2, 1024, 4), V("ht", 3, 1024, 4), V("alt", 0, 4), V("alt", 1, 512, 4), V("alt", 3, 1024, 4), V("acc"), V("cs", 255, 4096, 256),
-              V("crow", 0, 16), V("vf"), V("w0t", 832), V("w1t", 576), V("w2t", 320), V("w3t", 64)):
+    for v in (V("ht", 2, 1024, 4), V("ht", 3, 1024, 4), V("w0t", 832), V("w1t", 576), V("w2t", 320)):
         fill(v, 0.0)
-    fill(V("orow", 256, WIN), float(ZC))
-    fill(V("sg", 256, WIN), float(ZC))
-    fill(F["nine"], 8.0)
+    for v in (V("alt", 0, 4), V("alt", 1, 512, 4), V("alt", 3, 1024, 4), V("acc"), V("cs", 255, 4096, 256), V("crow", 0, 16), V("vf"), V("w3t", 64)):
+        lay(v, 0.0)
+    lay(V("orow", 256, WIN), float(ZC))
+    lay(V("sg", 256, WIN), float(ZC))
+    lay(F["nine"], 8.0)
     iota(V("gst"), [[1, 8], [0, 64]], 0, 0, True)
     ts(V("ul", 0, 8), V("kr", 0, 8), -15.0, None, A.add)
     fill(V("ul", 8, 16), 1)
@@ -265,7 +275,7 @@ def rank_program(g, core, T, topo):
     copy(F["p"], I["p"])
     copy(V("fc", 1, 5), V("ci", 2, 6))
     ts(V("m16"), V("j16"), F["r"], None, A.is_equal)
-    ts(V("ka"), V("j16"), 0.0, None, A.is_gt)
+    act(V("ka"), V("j16"), func=AF.Sign)
     ts(V("ke"), V("j16"), F["r"], 2 * BIG, A.is_gt, A.mult)
     ts(V("ke"), V("ke"), -BIG, None, A.add)
     ts(V("mb"), V("m16"), 2 * BIG, -BIG, A.mult, A.add)
@@ -273,22 +283,22 @@ def rank_program(g, core, T, topo):
     ts(V("gst"), V("gst"), F["g"], None, A.is_equal)
     quant("gs", V("gst"))
     ts(V("eye"), V("irow"), F["p"], None, A.is_equal)
-    act(V("tiny"), V("irow"), TINY)
-    ts(F["k0"], F["p"], -TINY, -TINY / 2, A.mult, A.add)
-    ts(F["k1"], F["p"], -TINY, -TINY * 128.5, A.mult, A.add)
+    ts(V("tri"), V("irow", 0, 128), F["p"], -0.5, A.is_gt, A.add)
+    lay(F["k0"], 0.5)
+    lay(F["k1"], -0.5)
+    lay(F["one"], 1.0)
     ts(F["gs"], F["g"], F["s"], 7.0, A.add, A.min)
-    ts(F["m7"], F["m"], 7.0, None, A.is_equal)
-    ts(F["t0"], F["m"], -1.0, 7.0, A.mult, A.add)
-    ts(F["t1"], F["m7"], -100.0, 7.0, A.mult, A.add)
-    ts(F["t2"], F["m7"], 7.0, F["m"], A.mult, A.subtract)
-    ts(F["thr"], F["m7"], 100.0, F["t0"], A.mult, A.add)
-    ts(F["lo"], F["t1"], F["gs"], None, A.subtract)
-    ts(F["val"], F["lo"], F["t2"], None, A.add)
-    ts(F["csg"], F["m7"], -2.0, 1.0, A.mult, A.add)
-    ts(F["lw"], F["h"], -1.0, 1.0, A.mult, A.add)
-    ts(F["h16"], F["h"], 16.0, None, A.mult)
-    ts(F["zl"], F["lw"], float(ZC), None, A.mult)
-    ts(F["zu"], F["h"], float(ZC), None, A.mult)
+    ts(F["m7"], F["m"], 7.0, -128.0, A.is_equal, A.mult)
+    ts(F["t0"], F["m"], F["m7"], 1.0, A.add, A.add)
+    ts(F["t1"], F["m7"], F["gs"], 7.0, A.subtract, A.add)
+    act(F["thr"], F["t0"], 1.0 / 1024)
+    act(F["lo"], F["m7"], 7.0 / 128, func=AF.Identity, bias=F["t1"])
+    act(F["val"], F["m"], -1.0, func=AF.Identity, bias=F["t1"])
+    act(F["csg"], F["m7"], 1.0 / 64, func=AF.Identity, bias=F["one"])
+    act(F["lw"], F["h"], -1.0, func=AF.Identity, bias=F["one"])
+    act(F["h16"], F["h"], 16.0)
+    act(F["zl"], F["lw"], float(ZC))
+    act(F["zu"], F["h"], float(ZC))
     quant("u", V("ut"))
     quant("v", V("vt"))
     put("v", lambda: g.vector.tensor_copy(T["qus"][:, :].bitcast(dt.uint32), T["qu"][:, 0:128].bitcast(dt.uint32).indirect(T["ul"][:, :])),
@@ -312,34 +322,36 @@ def rank_program(g, core, T, topo):
             calls[-1]["after"] = [len(calls) - 2] if i else []
         for h, bank in enumerate(("p3", "p4")):
             act(one("hb", h), one(bank, 1), -1.0)
-            act(V("ht", h, 1024, 4), row("p2"), func=AF.Sign, bias=one("hb", h), total_to=one("hb", 4 + h))
+            act(V("ht", h, 1024, 4), row("p2"), func=AF.Sign, bias=one("hb", h))
         quant("h", V("ht"))
-        mm("p5", 256, ("hs", 0), ("h", 0))
-        mm("p2", 256, ("hs", 0), ("h", 0))
-        tt(V("key"), row("p5"), V("tiny"), A.add)
-        act(V("rho"), row("p2"))
+        mm("p5", 256, ("k", 0), ("h", 0))
+        if RHO:
+            mm("p2", 256, ("k", 0), ("h", 0))
+            act(V("rho"), row("p2"))
         for h in (0, 1):
-            act(one("hb", 2 + h), one("hb", 4 + h), 1.0 / 512, func=AF.Identity, bias=F["k%d" % h])
-            act(quarter("gg", h), V("key"), func=AF.Sign, bias=one("hb", 2 + h))
-            scan(quarter("ll", h), quarter("gg", h), V("rho"), A.max, A.min, -0.75)
+            tt(V("gg", 384 * h, 384 * h + 128), V("ht", 513 * h, 512 * h + 512, 4), V("tri"), A.add)
+            act(V("gg", 128 + 128 * h, 256 + 128 * h), V("ht", 512 - 511 * h, 1024 - 512 * h, 4), func=AF.Identity, bias=F["k%d" % h])
+            scan(quarter("ll", h), quarter("gg", h), V("rho") if RHO else row("p5"), A.max, A.min, -0.75)
         tt(V("nf", 0, 256), row("p5"), V("ll", 0, 256), A.not_equal)
         tt(V("nf", 256, 384), row("p5", 128, 256), V("ll", 384, 512), A.not_equal)
         scan(V("alt", 4, 1024, 4), V("eye", 1, 256), V("nf", 1, 256), A.max, A.min, one("eye", 0))
         scan(V("alt", 513, 1024, 4), V("eye", 0, 128), V("nf", 256, 384), A.max, A.min)
-        tt(V("alt", 6, 512, 4), V("eye", 1, 128), V("nf", 1, 128), A.min)
-        tt(V("alt", 514, 1024, 4), V("eye", 0, 128), V("nf", 256, 384), A.min)
+        pick_diagonal(V("alt", 6, 512, 4), V("nf", 1, 128), 1)
+        pick_diagonal(V("alt", 514, 1024, 4), V("nf", 256, 384), 0)
         quant("al", V("alt"))
-        mm("p2", 256, ("k", 0), ("al", 0))
-        act(V("up"), row("p2"), -1.0, func=AF.Relu, bias=F["nine"])
-        ts(V("nn"), V("up"), F["thr"], None, A.is_lt)
+        for bank in KB:
+            mm(bank, 256, ("k", 0), ("al", 0))
+        act(V("up"), row(KB[-1]), -1024.0, func=AF.Relu, bias=F["nine"])
+        ts(V("nn"), row(KB[0]), F["thr"], None, A.is_gt)
         ts(V("mm"), V("up"), F["lo"], F["val"], A.min, A.is_equal)
         scan(V("cc"), V("dc"), V("nn"), A.add, A.mult)
         tt(V("cw"), V("cc"), V("mm"), A.mult)
-        for b, bank in enumerate(("p6", "p7", "p4", "p3")):
+        for b, bank in enumerate(FB):
             mm(bank, 256, ("eb", 128 * b), ("x", X))
             act(quarter("f", b), row(bank), 32.0)
-        tt(V("sm16"), row("p0"), V("mb"), A.min)
-        scan(V("own"), V("ke"), V("sm16"), A.min, A.max)
+        for a, z in OWN:
+            tt(V("sm16", a, z), row("p0", a, z), V("mb", a, z), A.min)
+            scan(V("own", a, z), V("ke", a, z), V("sm16", a, z), A.min, A.max)
         tt(V("w0t", 0, 1024, 4), row("p0"), V("own"), A.is_le)
         scan(V("es"), V("ka"), V("w0t", 0, 1024, 4), A.mult, A.add)
         for i, wide in enumerate(WIDE):
@@ -356,8 +368,8 @@ def rank_program(g, core, T, topo):
                     act(V("jk", o, o + e), row("p1", 0, e), -1.0, func=AF.Relu, bias=own)
                     act(w, V("jk", o, o + e), func=AF.Sign, total_to=one("acc", q))
             quant("w%d" % i, V("w%dt" % i))
-            mm("p6", wide, ("gs", 0), ("w%d" % i, 0), i == 0, i == 3)
-        tt(V("ex"), row("p6"), V("m16"), A.mult)
+            mm(RB, wide, ("gs", 0), ("w%d" % i, 0), i == 0, i == 3)
+        tt(V("ex"), row(RB), V("m16"), A.mult)
         scan(V("ey"), V("ka"), V("ex"), A.mult, A.add)
         tt(V("ru"), V("kq"), V("es", 15, 256, 16), A.subtract)
         tt(V("rv"), V("ru"), V("cs", 255, 4096, 256), A.subtract)
@@ -381,7 +393,7 @@ def rank_program(g, core, T, topo):
         for b in range(4):
             act(quarter("ta", b), quarter("f", b), lst=V("lab", 0, 16))
             tt(quarter("v32", b), quarter("f", b), quarter("ta", b), A.add, lst=V("lab", 16, 32))
-        for b, bank in enumerate(("p7", "p4", "p3", "p5")):
+        for b, bank in enumerate(NB):
             mm(bank, 256, ("eb", 128 * b), ("n", X))
             act(quarter("fn", b), row(bank))
         for b in range(4):

@@ -1,42 +1,45 @@
 from concourse.mybir import dt, AluOpType as A, ActivationFunctionType as AF
 
 ROUNDS = 3
-ZC = 384
-WIN = 400
-XS = (0, 1)
-VQ = (12, 11, 10, 9)
+XS = (0, 2)
+VQ = (12, 11, 10, 9, 8)
 WIDE = (256, 192, 128, 128)
-FIRST = ("p0", "p3", "p4", "p2", "p1")
+FIRST = ("p0", "p3", "p4", "p2", "p1", "p5")
 BIG = 2.0 ** 90
-RHO = False
+CROSS = False
+TILES = (0, 1, 2, 3)
+DG = ((0, 256),)
+FIRST0 = ("p3", "p4", "p0", "p2", "p1", "p5")
+HALVES = False
 OWN = ((128, 256), (0, 128))
-FB, NB, RB, KB = ("p7", "p4", "p3", "p7"), ("p4", "p3", "p7", "p1"), "p6", ("p5", "p2")
-HOP, FAR, NEAR, LOAD = 200, 4000, 1600, 1800
+FB, NB, RB, KB = ("p4", "p3", "p4", "p3"), ("p7", "p1", "p4", "p3"), ("p6", "p7"), ("p2",)
+HOP, FAR, NEAR, LOAD = 200, 4000, 1200, 1800
 
-SLACK, PASSES = (30, 90, 150), 4
+SLACK, PASSES = (30, 90, 150), 2
+URGE = {}
 
 SCRATCH = {}
 PSUM = ["p%d" % i for i in range(8)]
 for _n in PSUM:
     SCRATCH[_n] = ("psum", [128, 512], "float32")
-for _n, _c in [("u", 128), ("v", 128), ("w", 512), ("us", 256), ("x", 1024), ("eb", 512), ("k", 128), ("gs", 128), ("w0", 256), ("w1", 192), ("w2", 128), ("w3", 128), ("h", 256), ("al", 256),
+for _n, _c in [("u", 128), ("v", 128), ("w", 512), ("us", 256), ("x", 1024), ("eb", 512), ("k", 128), ("gs", 128), ("w0", 256), ("w1", 256), ("w2", 128), ("w3", 128), ("al", 256),
                ("e", 128), ("n", 768)]:
     SCRATCH["q" + _n] = ("sbuf", [128, _c], "float8_e4m3fn_x4")
     SCRATCH["z" + _n] = ("sbuf", [128, _c], "uint8")
 for _d, _l in [("bfloat16", [("ut", 512), ("vt", 512), ("xt", 1024), ("xn", 1024), ("ebt", 528), ("half", 528), ("kt", 512), ("gst", 512),
-                             ("ht", 1024), ("alt", 1024), ("rho", 256), ("tri", 128), ("gg", 512), ("ll", 512), ("nf", 384), ("ex", 256), ("ey", 256),
-                             ("j16", 256), ("m16", 256), ("ka", 256), ("ke", 256), ("eye", 256), ("irow", 256), ("mb", 256), ("es", 256),
-                             ("w0t", 1024), ("w1t", 768), ("w2t", 512), ("w3t", 512), ("cs", 4096), ("jk", 4096), ("f", 1024), ("orow", WIN), ("sg", WIN), ("crow", 272), ("dc", 256), ("up", 256),
-                             ("nn", 256), ("mm", 256), ("cc", 256), ("cw", 256), ("vf", 512), ("tf", 512), ("sm", 512), ("vc", 512), ("tc", 512),
+                             ("ht", 512), ("hu", 256), ("alt", 1024), ("tri", 128), ("tru", 128), ("gg", 512), ("nf", 384), ("ex", 256), ("ey", 256),
+                             ("j16", 256), ("m16", 256), ("ka", 256), ("ke", 256), ("eye", 256), ("irow", 256), ("mb", 256), ("kf", 256), ("es", 256),
+                             ("w0t", 1024), ("w1t", 1024), ("w2t", 512), ("w3t", 512), ("jk", 4096), ("f", 1024), ("orow", 384), ("sg", 256), ("crow", 288), ("dc", 256), ("up", 256),
+                             ("nn", 256), ("mm", 256), ("cc", 256), ("cw", 256), ("vf", 288), ("tf", 576), ("sm", 576), ("k8", 160), ("tc", 544),
                              ("ta", 1024), ("et", 512), ("tb", 512), ("fn", 1024), ("v32", 1024)]),
-               ("float32", [("sm16", 256), ("own", 256), ("cop", 256), ("ys", 256), ("fc", 32), ("hb", 8), ("rw", 16),
-                            ("kq", 16), ("kr", 16), ("acc", 16), ("ru", 16), ("rv", 16), ("cl", 16)]),
-               ("int32", [("ci", 16), ("cfi", 16), ("ri", 16), ("ra", 16), ("rp", 16)]),
-               ("uint16", [("ul", 16), ("cd", 32), ("cu", 16), ("rku", 16), ("pu", 16), ("lab", 32), ("lo", 48), ("li", 48)])]:
+               ("float32", [("sm16", 256), ("own", 256), ("ll", 512), ("cop", 256), ("ys", 256), ("fc", 32), ("hb", 8), ("rw", 16),
+                            ("kq", 16), ("kr", 16), ("acc", 16), ("ru", 16), ("ri", 16)]),
+               ("int32", [("ci", 16), ("cfi", 16)]),
+               ("uint16", [("ul", 16), ("at", 6), ("cu", 16), ("rku", 16), ("lab", 32), ("lo", 48), ("li", 48)])]:
     for _n, _c in _l:
         SCRATCH[_n] = ("sbuf", [128, _c], _d)
 
-SEMAPHORES = ["cv", "cs", "ct", "cg", "left"] + [a + str(t) for a in ("ax", "al") for t in range(ROUNDS)] + ["d%d" % i for i in range(20)]
+SEMAPHORES = ["cv", "cs", "ct", "left"] + ["g%d" % i for i in range(16)] + [a + str(t) for a in ("ax", "al") for t in range(ROUNDS)] + ["d%d" % i for i in range(20)]
 
 
 def meet(a, b):
@@ -89,7 +92,7 @@ def arrange(calls):
             now = max(free.get(q, 0), min(ready[i] for i in open_[q]))
             i = max(open_[q], key=lambda i: way[i] - max(0, ready[i] - now))
             if ready[i] > now:
-                fits = [j for j in open_[q] if ready[j] <= now and now + calls[j]["hold"] <= ready[i] + slack]
+                fits = [j for j in open_[q] if ready[j] <= now and now + calls[j]["hold"] <= ready[i] + (slack if q in "vs" else 0)]
                 if not fits:
                     free[q] = min(ready[j] for j in open_[q] if ready[j] > now)
                     continue
@@ -106,11 +109,12 @@ def arrange(calls):
     alone = [0.0] * n
     for i in reversed(range(n)):
         alone[i] = calls[i]["long"] + max([hop(i, j) + alone[j] for j in behind[i]], default=0)
+    urge = [URGE.get(c["writes"][0][0], 0) if c["writes"] else 0 for c in calls]
     tries = []
     for slack in SLACK:
         way = alone
         for _ in range(PASSES):
-            placed, done = place(before, behind, way, slack)
+            placed, done = place(before, behind, [w + u for w, u in zip(way, urge)], slack)
             tries.append((max(done), placed))
             way = place(behind, before, done, slack)[1]
     return min(tries)[1]
@@ -164,8 +168,8 @@ def rank_program(g, core, T, topo):
     def narrow(*v):
         return 0.5 if all(SCRATCH[x[0]][2] in ("bfloat16", "uint16") for x in v) else 1
 
-    def dma(q, out, in_, reads, writes):
-        put(q, lambda: Q[q].dma_start(out, in_), reads, writes, LOAD, "dma", 60)
+    def dma(q, out, in_, reads, writes, ns=LOAD):
+        put(q, lambda: Q[q].dma_start(out, in_), reads, writes, ns, "dma", 60)
 
     def fill(v, c):
         put("v", lambda: g.vector.memset(ap(v), c), [], [v], cycles(size(v), narrow(v)))
@@ -182,8 +186,8 @@ def rank_program(g, core, T, topo):
         put("v", lambda: g.vector.tensor_tensor_scan(ap(out), ap(d0), ap(d1), col(init), op0, op1), some(d0, d1, init), [out],
             cycles(size(out), narrow(out, d0, d1)))
 
-    def copy(out, in_):
-        put("v", lambda: g.vector.tensor_copy(ap(out), ap(in_)), [in_], [out], cycles(size(out), narrow(out, in_)))
+    def copy(out, in_, lst=None):
+        put("v", lambda: g.vector.tensor_copy(ap(out), ind(in_, lst)), some(in_, lst), [out], cycles(size(out), narrow(out, in_), lst))
 
     def scatter(win, lst, in_):
         put("v", lambda: g.vector.tensor_copy(ind(win, lst), ap(in_)), [in_, lst], [win], 50 + 3 * size(in_))
@@ -194,13 +198,14 @@ def rank_program(g, core, T, topo):
             k["bias"] = col(bias)
         if total_to is not None:
             k["accum_out"] = ap(total_to)
-        put("s", lambda: g.scalar.activation(ap(out), ind(in_, lst), func, **k), some(in_, lst, bias, scale), some(out, total_to), cycles(size(out), 1, lst))
+        put("s", lambda: g.scalar.activation(ap(out), ind(in_, lst), func, **k), some(in_, lst, bias, scale), some(out, total_to),
+            cycles(size(out), 1, lst) + (20 if total_to else 0))
 
     def lay(v, c):
         act(v, V("half", 0, size(v)), 2 * c) if c != 0.5 else act(v, V("half", 0, size(v)))
 
-    def pick_diagonal(out, in_, base):
-        put("g", lambda: g.affine_select(ap(out), ap(in_), [[1, size(out)]], A.is_equal, 0.0, base, -1), [in_], [out], 170 + 1.66 * size(out))
+    def diagonal(out, in_):
+        put("g", lambda: g.affine_select(ap(out), ap(in_), [[0, size(out) // 128], [1, 128]], A.is_equal, 0.0, 0, -1), [in_], [out], 170 + 1.66 * size(out))
 
     def turn(out, in_):
         put("v", lambda: g.vector.transpose(ap(out), ap(in_)), [in_], [out], cycles(size(out), narrow(out)))
@@ -233,14 +238,14 @@ def rank_program(g, core, T, topo):
         sent = put("g", call, [p[1] for p in pairs], [], ns, "send", 200, mine)
         put("r", sem, [], [p[0] for p in pairs], 0, "arrives", after=[sent])
 
-    I = {n: one("ci", i) for i, n in enumerate(("p", "r", "m", "s", "g", "h"))}
-    F = {n: one("fc", i) for i, n in enumerate(("r", "m", "s", "g", "h", "p", "gs", "m7", "thr", "val", "lo", "csg", "h16", "lw",
-                                                "zl", "zu", "k0", "k1", "t0", "t1", "one", "nine"))}
+    I = {n: one("ci", i) for i, n in enumerate(("p", "r", "m", "s", "g", "h", "b"))}
+    F = {n: one("fc", i) for i, n in enumerate(("r", "m", "s", "g", "h", "b", "p", "gs", "m7", "thr", "val", "lo", "csg", "far", "a0",
+                                                "a1", "a2", "k0", "k1", "t0", "t1", "one", "nine", "ths", "low"))}
 
     dma("y", T["ut"][:, :], T.u[:, :], [], [V("ut")])
     dma("s", T["xt"][:, 0:512], T.x[:, 0:512], [], [V("xt", 0, 512)])
-    dma("y", T["xt"][:, 512:1024], T.x[:, 512:1024], [], [V("xt", 512, 1024)])
-    dma("y", T["cfi"][:, :], T.cf[:, :], [], [V("cfi")])
+    dma("y", T["xt"][:, 512:1024], T.x[:, 512:1024], [], [V("xt", 512, 1024)], LOAD + 600)
+    dma("y", T["cfi"][:, :], T.cf[:, :], [V("ut"), V("xt")], [V("cfi")])
     dma("y", T["qw"][:, :].bitcast(dt.uint8), T.wc[:, :], [V("ut"), V("xt")], [V("qw")])
     dma("y", T["zw"][:, :], T.ws[:, :], [V("ut"), V("xt")], [V("zw")])
     dma("y", T["vt"][:, :], T.v[:, :], [V("ut"), V("xt")], [V("vt")])
@@ -256,57 +261,65 @@ def rank_program(g, core, T, topo):
     fill(V("kt"), 1.0 / 512)
     fill(V("kt", 2, 512, 4), -1.0 / 1024)
     quant("k", V("kt"))
-    for v in (V("ht", 2, 1024, 4), V("ht", 3, 1024, 4), V("w0t", 832), V("w1t", 576), V("w2t", 320)):
+    for v in (V("w0t", 832), V("w1t", 576), V("w2t", 320)):
         fill(v, 0.0)
-    for v in (V("alt", 0, 4), V("alt", 1, 512, 4), V("alt", 3, 1024, 4), V("acc"), V("cs", 255, 4096, 256), V("crow", 0, 16), V("vf"), V("w3t", 64)):
+    for v in (one("nf", 0), one("alt", 0), V("alt", 1, 512, 4), V("alt", 3, 1024, 4), one("acc", 0), V("crow", 0, 16), V("crow", 272), V("vf"), V("orow", 0, 256), V("w3t", 64)):
         lay(v, 0.0)
-    lay(V("orow", 256, WIN), float(ZC))
-    lay(V("sg", 256, WIN), float(ZC))
+    lay(V("w1t", 512, 576), 0.0)
+    quant("w1", V("w1t", 512), 128, 256)
     lay(F["nine"], 8.0)
     iota(V("gst"), [[1, 8], [0, 64]], 0, 0, True)
     ts(V("ul", 0, 8), V("kr", 0, 8), -15.0, None, A.add)
     fill(V("ul", 8, 16), 1)
     ts(I["r"], I["p"], 15, None, A.bitwise_and)
-    ts(I["m"], I["p"], 1, 7, A.arith_shift_right, A.bitwise_and)
-    ts(I["s"], I["p"], 1, None, A.bitwise_and)
+    ts(I["m"], I["p"], 7, None, A.bitwise_and)
+    ts(I["s"], I["p"], 3, 1, A.arith_shift_right, A.bitwise_and)
+    ts(I["b"], I["p"], 1, None, A.bitwise_and)
     ts(I["g"], I["p"], 4, None, A.arith_shift_right)
     ts(I["h"], I["p"], 4, 1, A.arith_shift_right, A.bitwise_and)
     copy(F["r"], I["r"])
     copy(F["p"], I["p"])
-    copy(V("fc", 1, 5), V("ci", 2, 6))
+    copy(V("fc", 1, 6), V("ci", 2, 7))
     ts(V("m16"), V("j16"), F["r"], None, A.is_equal)
     act(V("ka"), V("j16"), func=AF.Sign)
-    ts(V("ke"), V("j16"), F["r"], 2 * BIG, A.is_gt, A.mult)
-    ts(V("ke"), V("ke"), -BIG, None, A.add)
-    ts(V("mb"), V("m16"), 2 * BIG, -BIG, A.mult, A.add)
+    lay(F["low"], -BIG)
+    ts(V("kf"), V("j16"), F["r"], None, A.is_gt)
+    act(V("ke"), V("kf"), 2 * BIG, func=AF.Identity, bias=F["low"])
+    act(V("mb"), V("m16"), 2 * BIG, func=AF.Identity, bias=F["low"])
     ts(V("kq"), V("kr"), F["r"], None, A.subtract)
     ts(V("gst"), V("gst"), F["g"], None, A.is_equal)
     quant("gs", V("gst"))
     ts(V("eye"), V("irow"), F["p"], None, A.is_equal)
-    ts(V("tri"), V("irow", 0, 128), F["p"], -0.5, A.is_gt, A.add)
-    lay(F["k0"], 0.5)
-    lay(F["k1"], -0.5)
+    ts(V("tru"), V("irow", 0, 128), F["p"], -0.5, A.is_gt, A.add)
+    act(V("tri"), V("tru"), BIG)
+    lay(F["k0"], 0.5 * BIG)
+    lay(F["k1"], -0.5 * BIG)
     lay(F["one"], 1.0)
     ts(F["gs"], F["g"], F["s"], 7.0, A.add, A.min)
     ts(F["m7"], F["m"], 7.0, -128.0, A.is_equal, A.mult)
     ts(F["t0"], F["m"], F["m7"], 1.0, A.add, A.add)
     ts(F["t1"], F["m7"], F["gs"], 7.0, A.subtract, A.add)
     act(F["thr"], F["t0"], 1.0 / 1024)
+    act(F["ths"], F["t0"], -1.0, func=AF.Identity, bias=F["nine"])
     act(F["lo"], F["m7"], 7.0 / 128, func=AF.Identity, bias=F["t1"])
     act(F["val"], F["m"], -1.0, func=AF.Identity, bias=F["t1"])
     act(F["csg"], F["m7"], 1.0 / 64, func=AF.Identity, bias=F["one"])
-    act(F["lw"], F["h"], -1.0, func=AF.Identity, bias=F["one"])
-    act(F["h16"], F["h"], 16.0)
-    act(F["zl"], F["lw"], float(ZC))
-    act(F["zu"], F["h"], float(ZC))
+    ts(F["far"], F["b"], F["h"], None, A.not_equal)
+    ts(F["a0"], F["m"], 16.0, 7.0, A.mult, A.add)
+    act(F["a1"], F["far"], 144.0, func=AF.Identity, bias=F["a0"])
+    act(F["a2"], F["r"], 16.0)
+    ts(one("at", 0), F["s"], 8.0, F["a1"], A.mult, A.add)
+    ts(one("at", 2), F["s"], 288.0, F["a1"], A.mult, A.add)
+    ts(one("at", 3), one("at", 2), 8.0, None, A.add)
+    ts(one("at", 4), F["far"], 272.0, F["a2"], A.mult, A.add)
+    act(V("k8", 0, 128), V("ka", 0, 256, 2))
+    act(V("k8", 128, 160), V("ka", 0, 64, 2))
     quant("u", V("ut"))
     quant("v", V("vt"))
     put("v", lambda: g.vector.tensor_copy(T["qus"][:, :].bitcast(dt.uint32), T["qu"][:, 0:128].bitcast(dt.uint32).indirect(T["ul"][:, :])),
         [V("qu"), V("ul")], [V("qus")], 380)
     put("s", lambda: g.scalar.activation(T["zus"][:, :], T["zu"][:, 0:128].indirect(T["ul"][:, :]), AF.Copy), [V("zu"), V("ul")], [V("zus")], 380)
     copy(V("cu"), V("cfi"))
-    ts(V("cd", 0, 32, 2), V("cfi"), F["lw"], F["zu"], A.mult, A.add)
-    ts(V("cd", 1, 32, 2), V("cfi"), F["h"], F["zl"], A.mult, A.add)
     act(V("crow", 16, 272), V("irow"), F["csg"], V("cu"))
 
     for t in range(ROUNDS):
@@ -315,34 +328,41 @@ def rank_program(g, core, T, topo):
         X = 256 * t
         quant("x", V("xt") if t == 0 else V("xn"), X, X + 256)
         send([(V("qn", X, X + 256), V("qx", X, X + 256)), (V("zn", X, X + 256), V("zx", X, X + 256))], "ax%d" % t, FAR)
-        first = {"p0": (256, ("us", 0), ("x", X)), "p1": (256, ("us", 0), ("x", X)), "p2": (256, ("us", 128), ("x", X)),
+        first = {"p0": (256, ("us", 0), ("x", X)), "p1": (256, ("us", 0), ("x", X)), "p2": (256, ("us", 128), ("x", X)), "p5": (256, ("us", 128), ("x", X)),
                  "p3": (128, ("x", X), ("u", 0)), "p4": (128, ("x", X + 128), ("u", 0))}
-        for i, bank in enumerate(FIRST):
+        for i, bank in enumerate(FIRST if t else FIRST0):
             mm(bank, *first[bank])
             calls[-1]["after"] = [len(calls) - 2] if i else []
         for h, bank in enumerate(("p3", "p4")):
+            same, other = (128 * h, 128 * h + 128), (128 - 128 * h, 256 - 128 * h)
             act(one("hb", h), one(bank, 1), -1.0)
-            act(V("ht", h, 1024, 4), row("p2"), func=AF.Sign, bias=one("hb", h))
-        quant("h", V("ht"))
-        mm("p5", 256, ("k", 0), ("h", 0))
-        if RHO:
-            mm("p2", 256, ("k", 0), ("h", 0))
-            act(V("rho"), row("p2"))
-        for h in (0, 1):
-            tt(V("gg", 384 * h, 384 * h + 128), V("ht", 513 * h, 512 * h + 512, 4), V("tri"), A.add)
-            act(V("gg", 128 + 128 * h, 256 + 128 * h), V("ht", 512 - 511 * h, 1024 - 512 * h, 4), func=AF.Identity, bias=F["k%d" % h])
-            scan(quarter("ll", h), quarter("gg", h), V("rho") if RHO else row("p5"), A.max, A.min, -0.75)
-        tt(V("nf", 0, 256), row("p5"), V("ll", 0, 256), A.not_equal)
-        tt(V("nf", 256, 384), row("p5", 128, 256), V("ll", 384, 512), A.not_equal)
-        scan(V("alt", 4, 1024, 4), V("eye", 1, 256), V("nf", 1, 256), A.max, A.min, one("eye", 0))
-        scan(V("alt", 513, 1024, 4), V("eye", 0, 128), V("nf", 256, 384), A.max, A.min)
-        pick_diagonal(V("alt", 6, 512, 4), V("nf", 1, 128), 1)
-        pick_diagonal(V("alt", 514, 1024, 4), V("nf", 256, 384), 0)
+            act(V("ht", *same), row("p2", *same), func=AF.Sign, bias=one("hb", h))
+            act(V("hu", *same), V("ht", *same), BIG)
+            tt(V("gg", 384 * h, 384 * h + 128), V("hu", *same), V("tri"), A.add)
+            if CROSS:
+                ts(V("gg", 128 + 128 * h, 256 + 128 * h), row("p5", *other), one(bank, 1), 2 * BIG, (A.is_ge, A.is_gt)[h], A.mult)
+            else:
+                act(V("ht", 256 + 128 * h, 384 + 128 * h), row("p2", *other), func=AF.Sign, bias=one("hb", h))
+                act(V("gg", 128 + 128 * h, 256 + 128 * h), V("ht", 256 + 128 * h, 384 + 128 * h), BIG, func=AF.Identity, bias=F["k%d" % h])
+        for a in (256, 0, 384, 128):
+            scan(V("ll", a, a + 128), V("gg", a, a + 128), row("p5", a % 256, a % 256 + 128), A.add if CROSS and a in (128, 256) else A.max, A.min,
+                 one("ll", a - 1) if a % 256 else -0.75 * BIG)
+        tt(V("nf", 1, 128), row("p5", 1, 128), V("ll", 1, 128), A.not_equal)
+        tt(V("nf", 128, 256), row("p5", 128, 256), V("ll", 384, 512), A.not_equal)
+        tt(V("nf", 256, 384), row("p5", 128, 256), V("ll", 128, 256), A.not_equal)
+        scan(V("alt", 4, 512, 4), V("eye", 1, 128), V("nf", 1, 128), A.max, A.min, one("eye", 0))
+        scan(V("alt", 512, 1024, 4), V("eye", 128, 256), V("nf", 256, 384), A.max, A.min, V("alt", 508, 509, 4))
+        scan(V("alt", 513, 1024, 4), V("eye", 0, 128), V("nf", 128, 256), A.max, A.min)
+        for a, z in DG:
+            diagonal(V("alt", 4 * a + 2, 4 * z, 4), V("nf", a, z))
         quant("al", V("alt"))
         for bank in KB:
             mm(bank, 256, ("k", 0), ("al", 0))
         act(V("up"), row(KB[-1]), -1024.0, func=AF.Relu, bias=F["nine"])
-        ts(V("nn"), row(KB[0]), F["thr"], None, A.is_gt)
+        if len(KB) == 2:
+            ts(V("nn"), row(KB[0]), F["thr"], None, A.is_gt)
+        else:
+            ts(V("nn"), V("up"), F["ths"], None, A.is_lt)
         ts(V("mm"), V("up"), F["lo"], F["val"], A.min, A.is_equal)
         scan(V("cc"), V("dc"), V("nn"), A.add, A.mult)
         tt(V("cw"), V("cc"), V("mm"), A.mult)
@@ -354,7 +374,8 @@ def rank_program(g, core, T, topo):
             scan(V("own", a, z), V("ke", a, z), V("sm16", a, z), A.min, A.max)
         tt(V("w0t", 0, 1024, 4), row("p0"), V("own"), A.is_le)
         scan(V("es"), V("ka"), V("w0t", 0, 1024, 4), A.mult, A.add)
-        for i, wide in enumerate(WIDE):
+        for i in TILES:
+            wide = WIDE[i]
             for c in range(4):
                 q = 16 - 4 * i - c
                 if q == 16:
@@ -363,33 +384,31 @@ def rank_program(g, core, T, topo):
                 w = V("w%dt" % i, c, 4 * e, 4)
                 if q in VQ:
                     ts(w, row("p0", 0, e), own, None, A.is_lt)
-                    scan(V("cs", o + 256 - e, o + 256), w, w, A.add, A.max)
+                    act(V("jk", o, o + e), w, total_to=one("acc", q))
                 else:
                     act(V("jk", o, o + e), row("p1", 0, e), -1.0, func=AF.Relu, bias=own)
                     act(w, V("jk", o, o + e), func=AF.Sign, total_to=one("acc", q))
-            quant("w%d" % i, V("w%dt" % i))
-            mm(RB, wide, ("gs", 0), ("w%d" % i, 0), i == 0, i == 3)
-        tt(V("ex"), row(RB), V("m16"), A.mult)
-        scan(V("ey"), V("ka"), V("ex"), A.mult, A.add)
+            quant("w%d" % i, V("w%dt" % i, 0, 4 * wide), 0, wide)
+            mm(RB[0], 128, ("gs", 0), ("w%d" % i, 0), i == TILES[0], i == TILES[3])
+            if i < 2:
+                mm(RB[1], 128, ("gs", 0), ("w%d" % i, 128), TILES.index(i) < TILES.index(1 - i), TILES.index(i) > TILES.index(1 - i))
+        for a, bank in ((128, RB[1]), (0, RB[0])):
+            tt(V("ex", a, a + 128), row(bank, 0, 128), V("m16", 0, 128), A.mult)
+            scan(V("ey", a, a + 128), V("ka", 0, 128), V("ex", a, a + 128), A.mult, A.add)
         tt(V("ru"), V("kq"), V("es", 15, 256, 16), A.subtract)
-        tt(V("rv"), V("ru"), V("cs", 255, 4096, 256), A.subtract)
-        tt(V("rw"), V("rv"), V("acc"), A.subtract)
+        tt(V("rw"), V("ru"), V("acc"), A.subtract)
         tt(V("ri"), V("rw"), V("ey", 15, 256, 16), A.add)
-        ts(V("ra"), V("ri"), 240, None, A.bitwise_and)
-        tt(V("rp"), V("ri"), V("ra"), A.add)
-        ts(V("pu"), V("rp"), F["h16"], None, A.add)
         copy(V("rku"), V("ri"))
-        scatter(V("vf"), V("pu"), V("cw"))
+        scatter(V("vf", 16, 272), V("rku"), V("cw"))
         for half in (0, 1):
-            a = 256 * half
-            turn(V("tf", a, a + 256), V("vf", a, a + 256))
-            for s in (0, 1):
-                o = 256 * s + 128 * half
-                scan(V("sm", o, o + 128), V("ka", 0, 128), V("tf", a + s, a + 256, 2), A.mult, A.add)
-                if half == 0:
-                    copy(V("lo", 16 * t + 8 * s, 16 * t + 8 * s + 8), V("sm", o + 15, o + 128, 16))
+            a, o = 128 * half, 288 * half
+            for c, z, shift in ((0, 128, 16), (128, 288, 0)):
+                turn(V("tf", o + c, o + z), V("vf", a + shift, a + shift + z - c))
+                scan(V("sm", o + c, o + z), V("k8", 0, z - c), V("tf", o + c, o + z), A.mult, A.add)
+            if half == 0:
+                copy(V("lo", 16 * t, 16 * t + 16), V("sm", 0, 288), V("at", 0, 1))
         send([(V("li", 16 * t, 16 * t + 16), V("lo", 16 * t, 16 * t + 16))], "al%d" % t, NEAR)
-        copy(V("lab"), V("sm", 15, 512, 16))
+        copy(V("lab"), V("sm"), V("at", 2, 4))
         for b in range(4):
             act(quarter("ta", b), quarter("f", b), lst=V("lab", 0, 16))
             tt(quarter("v32", b), quarter("f", b), quarter("ta", b), A.add, lst=V("lab", 16, 32))
@@ -409,27 +428,27 @@ def rank_program(g, core, T, topo):
             dma("y", T.op[:, :], T["cop"][0:128:16, :], [V("cop")], [])
         else:
             act(V("crow", 16, 272), V("sg", 0, 256), F["csg"], V("cu"))
-            act(V("vc"), V("sg"), lst=V("cd"))
-            turn(V("tc"), V("vc"))
-            tt(V("cl"), V("tc", 0, 512, 32), V("tc", 16, 512, 32), A.add)
-            copy(V("cd"), V("tc", 0, 512, 16))
-            ts(V("cu"), V("cl"), -float(ZC), None, A.add)
+            turn(V("tc", 0, 256), V("crow", 16, 272))
+            turn(V("tc", 256, 544), V("crow"))
+            copy(V("cu"), V("tc"), V("at", 4, 5))
         for b, bank in enumerate(("p0", "p1", "p7", "p3")):
             low = V("v32", 256 * b + 128, 256 * b + 256)
             mm(bank, 128, ("w", 128 * b), ("e", 0))
             tt(low, V(bank, 0, 128), low, A.add)
-        for b in range(4):
-            out, win, lst = V("xn", b, 1024, 4), quarter("v32", b), V("rku")
-            if b in XS:
-                act(out, win, scale=0.03125, lst=lst)
-            else:
-                ts(out, win, 0.03125, None, A.mult, lst=lst)
+        for a, z in ((0, 8), (8, 16)) if last and HALVES else ((0, 16),):
+            for b in range(4):
+                out, win, lst = V("xn", 64 * a + b, 64 * z, 4), quarter("v32", b), V("rku", a, z)
+                if b in XS:
+                    act(out, win, scale=0.03125, lst=lst)
+                else:
+                    ts(out, win, 0.03125, None, A.mult, lst=lst)
 
     X = 256 * ROUNDS
-    quant("x", V("xn"), X, X + 256)
-    mm("p4", 256, ("v", 0), ("x", X))
-    copy(V("ys"), V("p4", 0, 256))
-    dma("y", T.y[:, :], T["ys"][:, :], [V("ys")], [])
+    for a, z, bank in ((0, 128, "p4"), (128, 256, "p5")) if HALVES else ((0, 256, "p4"),):
+        quant("x", V("xn", 4 * a, 4 * z), X + a, X + z)
+        mm(bank, z - a, ("v", 0), ("x", X + a))
+        (copy if a else act)(V("ys", a, z), V(bank, 0, z - a))
+        dma("y" if a else "s", T.y[:, a:z], T["ys"][:, a:z], [V("ys", a, z)], [])
     dma("y", T.oc[:, :], T["qx"][:, X:X + 256].bitcast(dt.uint8), [V("qx", X)], [])
     for i in range(4):
         dma("y" if i % 2 else "s", T.osc[4 * i:4 * i + 4, :], T["zx"][32 * i:32 * i + 4, X:X + 256], [V("zx", X)], [])
@@ -449,8 +468,6 @@ def rank_program(g, core, T, topo):
             sem, n, theirs = e[3]
             if need.get(sem, (0, 0))[0] < n:
                 need[sem] = (n, theirs)
-        if q == "g" and "cg" in total:
-            need["cg"] = (total["cg"], {})
         for sem, (n, theirs) in need.items():
             if know[q].get(sem, 0) < n:
                 Q[q].wait_ge(T.sem[sem], n)
@@ -460,7 +477,8 @@ def rank_program(g, core, T, topo):
             c["call"]()
             total["left"] = total.get("left", 0) + len(c["reads"]) * len(topo.engines(core, nxt))
             continue
-        sem, n = ("d%d" % len([s for s in total if s[0] == "d"]), 16) if kind == "dma" else ("c" + q, 1)
+        own = "d" if kind == "dma" else "g" if q == "g" else None
+        sem, n = (own + str(len([s for s in total if s[0] == own])) if own else "c" + q), (16 if kind == "dma" else 1)
         c["call"]().then_inc(T.sem[sem], n)
         total[sem] = total.get(sem, 0) + n
         remember(seen, q, c["reads"], c["writes"], (sem, total[sem], dict(know[q])))

@@ -1,51 +1,99 @@
+import math
+import numpy as np
 from concourse.mybir import dt, AluOpType as A, ActivationFunctionType as AF
 
 ROUNDS = 3
-XS = (0, 2)
-VQ = (12, 11, 10, 9, 8)
-WIDE = (256, 192, 128, 128)
-FIRST = ("p0", "p3", "p4", "p2", "p1", "p5")
+RW, SC = "v", 1
+SCAN, SUM = (1.0, 1.2), 70
+LATE, PARTS = False, False
+ONS = ()
+XQ, YH, OH, ZD = "s", False, False, False
+SPLIT, TWICE, ZH = True, False, ()
+XL = "ss ss sv vv"
+XS = "ss ss sv vv"
+VQ = (12, 11, 4, 3, 2, 1)
+VS = VQ
+TAV, TBV = (0,), (3,)
+WRAP = "v"
+APART = False
 BIG = 2.0 ** 90
-CROSS = False
-TILES = (0, 1, 2, 3)
-DG = ((0, 256),)
-FIRST0 = ("p3", "p4", "p0", "p2", "p1", "p5")
-HALVES = False
-OWN = ((128, 256), (0, 128))
-FB, NB, RB, KB = ("p4", "p3", "p4", "p3"), ("p7", "p1", "p4", "p3"), ("p6", "p7"), ("p2",)
-HOP, FAR, NEAR, LOAD = 200, 4000, 1200, 1800
+WIDE = 2.0 ** 14
+TILES = (2, 1, 0)
+HALVES = True
+OWN = (0, 128)
+DIRECT = False
+SL, SV, SS, DL, DU, CA, CB = 0, 5, 1, 2, 4, 3, 3
+RB, KB, FB, NB, LB = (6, 7), (2, 4), (3, 0, 5, 3), (1, 2, 4, 0), (6, 7, 3, 5)
+FIRST = "sl ca dl s2 sv cb du ss"
+FIRST0 = FIRST
+PACES = [dict(slow=1.0, call=15, wait=180, gather=1.0, pick=110, scatter=1.6, tensor=0.9, far=3500, near=1200, load=1500, first=2000, issue=100),
+         dict(slow=1.0, call=30, wait=110, gather=0.9, pick=90, scatter=2.2, tensor=1.0, far=4200, near=1400, load=1800, first=1000, issue=300),
+         dict(slow=1.3, call=10, wait=220, gather=1.25, pick=80, scatter=3.0, tensor=1.2, far=5000, near=1700, load=1700, first=2000, issue=200)]
+SLACK, PASSES = (30, 90), 2
+MOVES, HEAT = 30000, 0.0001
+ORDER = {}
 
-SLACK, PASSES = (30, 90, 150), 2
-URGE = {}
+SPLIT, OWN, TILES, FIRST, CB, XS, XL, HALVES = False, (128, 0), (1, 0, 2), "sv ca cb df ss", 4, "s v s v", "s v s v", False
+FIRST0, KB, FB, NB, LB, TAV, TBV = FIRST, (2, 3), (4, 5, 4, 5), (1, 2, 3, 0), (6, 7, 4, 5), (0,), ()
+VQ = VS = (8, 7, 6, 5, 4, 3, 2, 1)
+SCAN, SUM = (0.75, 1.0), 40
+PACES = [dict(slow=1.0, call=30, wait=180, gather=1.15, pick=70, scatter=2.4, tensor=1.0, far=3800, near=1300, load=1600, first=1500, issue=100),
+         dict(slow=1.0, call=50, wait=120, gather=0.9, pick=90, scatter=1.6, tensor=0.9, far=3300, near=1100, load=1400, first=1000, issue=300),
+         dict(slow=1.3, call=20, wait=240, gather=1.3, pick=70, scatter=3.2, tensor=1.3, far=4800, near=1700, load=1900, first=2000, issue=200)]
 
-SCRATCH = {}
-PSUM = ["p%d" % i for i in range(8)]
-for _n in PSUM:
-    SCRATCH[_n] = ("psum", [128, 512], "float32")
-for _n, _c in [("u", 128), ("v", 128), ("w", 512), ("us", 256), ("x", 1024), ("eb", 512), ("k", 128), ("gs", 128), ("w0", 256), ("w1", 256), ("w2", 128), ("w3", 128), ("al", 256),
+HB2 = False
+TAIL = "sysysy"
+GG, HOLD, CW = "s", True, True
+GG, HOLD, CW, SCAN, TT, SUM = None, False, False, None, 2, 30
+VQ = VS = (12, 11, 4, 3, 2, 1)
+SPLIT, OWN, TILES, FIRST, CB, XS, XL, HALVES = True, (0, 128), (2, 1, 0), "sl ca dl s2 sv cb du ss", 3, "ss ss sv vv", "ss ss sv vv", True
+FIRST0, KB, FB, NB, LB, TAV, TBV, ZH = FIRST, (2, 4), (3, 0, 5, 3), (1, 2, 4, 0), (6, 7, 3, 5), (), (3,), (0, 1, 2, 3)
+SCAN, SUM = (1.0, 1.1), 50
+VS, XS, TILES, MOVES = (4, 3, 2, 1), "ss sv sv vv", (2, 0, 1), 90000
+SCAN, SUM, XQ, MOVES, TT, CALLS = (0.72, 1.27), 30, "s", 60000, 1.45, "vs"
+PACES = [dict(slow=1.0, call=15, wait=190, s=25, t=60, own=10, gather=0.88, pick=80, scatter=2.5, tensor=0.85, far=2700, near=1150, load=2100, first=800, issue=60),
+         dict(slow=1.0, call=12, wait=172, s=10, t=110, own=35, gather=0.95, pick=85, scatter=2.2, tensor=0.92, far=3200, near=1250, load=1900, first=1500, issue=60),
+         dict(slow=1.35, call=14, wait=210, s=25, t=90, own=25, gather=1.2, pick=80, scatter=2.9, tensor=1.3, far=5400, near=1700, load=2100, first=1500, issue=100)]
+TAIL, YH, OH = "ssyyyy", True, True
+WRAP, RW, ONS, MOVES = "v", "v", (), 70000
+TAIL, YH, OH, SCAN, SUM, TT, CALLS = "sysysy", False, False, (1.0, 1.15), 50, 2, "s"
+PACES = [dict(slow=1.0, call=15, wait=240, own=50, gather=0.9, pick=62, scatter=2.2, tensor=0.85, far=4000, near=1250, load=1650, first=1000, issue=60),
+         dict(slow=1.0, call=25, wait=205, own=80, gather=1.1, pick=62, scatter=1.6, tensor=1.0, far=2800, near=1100, load=1500, first=1500, issue=100),
+         dict(slow=1.35, call=15, wait=270, own=50, gather=1.25, pick=62, scatter=3.2, tensor=1.2, far=5200, near=1600, load=1900, first=1500, issue=100)]
+SCRATCH = {"ps": ("psum", [128, 4096], "float32")}
+for _n, _c in [("u", 128), ("v", 128), ("w", 512), ("us", 256), ("x", 1024), ("eb", 512), ("k", 256), ("gs", 128), ("w0", 256), ("w1", 256), ("w2", 256), ("al", 128),
                ("e", 128), ("n", 768)]:
     SCRATCH["q" + _n] = ("sbuf", [128, _c], "float8_e4m3fn_x4")
     SCRATCH["z" + _n] = ("sbuf", [128, _c], "uint8")
-for _d, _l in [("bfloat16", [("ut", 512), ("vt", 512), ("xt", 1024), ("xn", 1024), ("ebt", 528), ("half", 528), ("kt", 512), ("gst", 512),
-                             ("ht", 512), ("hu", 256), ("alt", 1024), ("tri", 128), ("tru", 128), ("gg", 512), ("nf", 384), ("ex", 256), ("ey", 256),
-                             ("j16", 256), ("m16", 256), ("ka", 256), ("ke", 256), ("eye", 256), ("irow", 256), ("mb", 256), ("kf", 256), ("es", 256),
-                             ("w0t", 1024), ("w1t", 1024), ("w2t", 512), ("w3t", 512), ("jk", 4096), ("f", 1024), ("orow", 384), ("sg", 256), ("crow", 288), ("dc", 256), ("up", 256),
-                             ("nn", 256), ("mm", 256), ("cc", 256), ("cw", 256), ("vf", 288), ("tf", 576), ("sm", 576), ("k8", 160), ("tc", 544),
+for _d, _l in [("bfloat16", [("ut", 512), ("vt", 512), ("xt", 1024), ("xn", 1024), ("ebt", 528), ("kt", 520), ("gst", 512), ("irow", 256), ("k16", 320), ("kq", 256), ("kc", 256),
+                             ("mb", 128), ("kep", 128), ("m14", 128), ("ma", 128), ("mc", 128), ("eye", 128), ("eab", 128), ("tri", 256), ("tru", 128),
+                             ("s2", 512), ("gg", 512), ("go", 128), ("t0", 128), ("t1", 128), ("t2", 128), ("t3", 128), ("sel", 256), ("cs", 256), ("ex", 256), ("ey", 256), ("nf", 256), ("alt", 512), ("up", 256),
+                             ("n2", 512), ("m2", 512), ("c2", 512), ("h2", 512), ("cw", 512), ("es", 256),
+                             ("w0t", 1024), ("w1t", 1024), ("w2t", 1024), ("jk", 4096), ("f", 1024), ("sg", 256), ("cn", 288),
+                             ("vf", 400), ("tf", 576), ("sm", 576), ("tc", 544),
                              ("ta", 1024), ("et", 512), ("tb", 512), ("fn", 1024), ("v32", 1024)]),
-               ("float32", [("sm16", 256), ("own", 256), ("ll", 512), ("cop", 256), ("ys", 256), ("fc", 32), ("hb", 8), ("rw", 16),
-                            ("kq", 16), ("kr", 16), ("acc", 16), ("ru", 16), ("ri", 16)]),
+               ("float32", [("sm16", 256), ("own", 256), ("ll", 384), ("cop", 256), ("ys", 256), ("fc", 32), ("hb", 8), ("rw", 16),
+                            ("acc", 4096), ("r2", 16), ("ri", 16)]),
                ("int32", [("ci", 16), ("cfi", 16)]),
-               ("uint16", [("ul", 16), ("at", 6), ("cu", 16), ("rku", 16), ("lab", 32), ("lo", 48), ("li", 48)])]:
+               ("uint16", [("ul", 16), ("at", 6), ("cu", 16), ("rku", 16), ("lab", 32), ("lal", 16), ("lo", 48), ("li", 48)])]:
     for _n, _c in _l:
         SCRATCH[_n] = ("sbuf", [128, _c], _d)
 
-SEMAPHORES = ["cv", "cs", "ct", "left"] + ["g%d" % i for i in range(16)] + [a + str(t) for a in ("ax", "al") for t in range(ROUNDS)] + ["d%d" % i for i in range(20)]
+SEMAPHORES = ["cv", "cs", "ct", "left"] + ["g%d" % i for i in range(24)] + [a + str(t) for a in ("ax", "ay", "al") for t in range(ROUNDS)] + ["d%d" % i for i in range(20)]
+
+
+def last_of(v):
+    return v[1] + (v[2] - 1 - v[1]) // v[3] * v[3]
 
 
 def meet(a, b):
     if a[4] >= b[5] or b[4] >= a[5] or a[1] >= b[2] or b[1] >= a[2]:
         return False
     return not (a[3] == b[3] and (a[1] - b[1]) % a[3])
+
+
+def one_bank(a, b):
+    return a[1] // 512 <= last_of(b) // 512 and b[1] // 512 <= last_of(a) // 512
 
 
 def covers(v, o):
@@ -55,7 +103,7 @@ def covers(v, o):
 def follows(seen, q, reads, writes):
     for v, w in [(r, False) for r in reads] + [(r, True) for r in writes]:
         for e in seen.get(v[0], []):
-            if (w or e[1] or e[2] != q) if v[0] in PSUM else ((w or e[1]) and meet(v, e[0])):
+            if ((w or e[1] or e[2] != q) and one_bank(v, e[0])) if v[0] == "ps" else ((w or e[1]) and meet(v, e[0])):
                 yield e
 
 
@@ -67,7 +115,117 @@ def remember(seen, q, reads, writes, who):
         L.append((v, w, q, who))
 
 
+def lengths(c, pace, first):
+    what, n = c["cost"]
+    if what == "load":
+        return pace["load"] + n, pace["issue"]
+    if what == "mid":
+        return 0.8 * pace["far"] + first, 200 * n + first
+    if what in ("far", "near"):
+        return pace[what] + first, 200 * n + first
+    ns = pace["slow"] * (n + pace["call"] * (c["q"] in CALLS) if what == "plain" else pace[what] * n + pace["pick"] * (what != "tensor"))
+    return ns, ns
+
+
+def polish(calls, before, behind, order):
+    n = len(calls)
+    above = []
+    for i in range(n):
+        a = 0
+        for j in before[i]:
+            a |= above[j] | 1 << j
+        above.append(a)
+    q = [c["q"] for c in calls]
+    timed = [[j for j in before[i] if not (q[i] == q[j] in "tg")] for i in range(n)]
+    timed = [[j for j in t if not any(above[k] >> j & 1 for k in t)] for t in timed]
+    sent = min(i for i in range(n) if calls[i]["kind"] == "send")
+    paces = []
+    for p in PACES:
+        L = [lengths(calls[i], p, p["first"] if i == sent else 0) for i in range(n)]
+        paces.append(([x[0] + (0 if calls[i]["kind"] == "send" else p["wait"] + p.get(q[i], 0)) for i, x in enumerate(L)], [x[1] for x in L], p.get("own", 0)))
+    cross = [[j for j in timed[i] if q[j] != q[i]] for i in range(n)]
+    same = [[j for j in timed[i] if q[j] == q[i]] for i in range(n)]
+
+    def ahead(order):
+        last, prev = {}, [n] * n
+        for i in order:
+            if q[i] != "r":
+                prev[i], last[q[i]] = last.get(q[i], n), i
+        return prev
+
+    def run(order, prev, start, state):
+        new, total = [], 0.0
+        rest = order[start:]
+        for (long, hold, own), (there, free, unit) in zip(paces, state):
+            there, free = there[:], free[:]
+            for i in rest:
+                t = free[prev[i]]
+                for j in cross[i]:
+                    if there[j] > t:
+                        t = there[j]
+                for j in same[i]:
+                    if there[j] + own > t:
+                        t = there[j] + own
+                free[i], there[i] = t + hold[i], t + long[i]
+            new.append((there, free, unit))
+            total += max(there) / unit
+        return total / len(paces), new
+
+    def chain(order, prev, state, m):
+        there, free, _ = state[m]
+        hold = paces[m][1]
+        i, pairs = there.index(max(there)), []
+        while True:
+            t = free[i] - hold[i]
+            if prev[i] < n and abs(free[prev[i]] - t) < 1e-6:
+                pairs.append((prev[i], i))
+                i = prev[i]
+                continue
+            back = [j for j in timed[i] if abs(there[j] + paces[m][2] * (q[j] == q[i]) - t) < 1e-6]
+            if not back:
+                return pairs
+            i = back[0]
+    dice = np.random.RandomState(1)
+    prev = ahead(order)
+    state = run(order, prev, 0, [([0.0] * n, [0.0] * (n + 1), 1.0) for _ in paces])[1]
+    state = [(a, b, max(a)) for a, b, _ in state]
+    now = best = 1.0
+    kept = list(order)
+    throws = dice.random_sample((MOVES, 5)).tolist()
+    for move, (r0, r1, r2, r3, r4) in enumerate(throws):
+        if move % 8 == 0:
+            m = move // 8 % len(paces)
+            at = {i: a for a, i in enumerate(order)}
+            order.sort(key=lambda i: (state[m][1][i] - paces[m][1][i], at[i]))
+            pairs = chain(order, prev, state, m)
+        step = 1 if r1 < 0.5 else -1
+        a = order.index(pairs[int(r2 * len(pairs))][step < 0]) if r0 < 0.7 else int(r2 * n)
+        i, far, b, to = order[a], (1, 1, 1, 2, 3, 5, 8)[int(r3 * 7)], a, a
+        stop = before[i] if step < 0 else behind[i]
+        while far and 0 <= b + step < n and order[b + step] not in stop:
+            b += step
+            if q[order[b]] == q[i]:
+                far, to = far - 1, b
+        if to == a or q[i] == "r":
+            continue
+        other = order[:a] + order[a + 1:]
+        other.insert(to, i)
+        prev2 = ahead(other)
+        end, state2 = run(other, prev2, min(a, to), state)
+        if end <= now - HEAT * (1.0 - move / MOVES) * math.log(r4 + 1e-12):
+            order, prev, state, now = other, prev2, state2, end
+            if end < best:
+                best, kept = end, list(other)
+    ORDER["best"] = [best] + [best * s[2] for s in state]
+    return kept
+
+
 def arrange(calls):
+    if len(calls) in ORDER:
+        return ORDER[len(calls)]
+    for c in calls:
+        c["long"], c["hold"] = lengths(c, PACES[0], 0)
+    HOP = PACES[0]["wait"]
     seen, before = {}, []
     for i, c in enumerate(calls):
         before.append({e[3] for e in follows(seen, c["q"], c["reads"], c["writes"])} | set(c["after"]))
@@ -79,7 +237,7 @@ def arrange(calls):
             behind[j].append(i)
 
     def hop(j, i):
-        return 0 if calls[j]["q"] == calls[i]["q"] == "t" else HOP
+        return 0 if calls[j]["q"] == calls[i]["q"] in "tg" or calls[i]["q"] == "r" else HOP
 
     def place(first, then, way, slack):
         left = [len(b) for b in first]
@@ -101,23 +259,24 @@ def arrange(calls):
             free[q], done[i] = now + calls[i]["hold"], now + calls[i]["long"]
             placed.append(i)
             for j in then[i]:
-                ready[j] = max(ready[j], done[i] + hop(i, j))
+                ready[j] = max(ready[j], free[q] if q == calls[j]["q"] == "g" else done[i] + hop(i, j))
                 left[j] -= 1
                 if not left[j]:
                     open_.setdefault(calls[j]["q"], []).append(j)
         return placed, done
     alone = [0.0] * n
     for i in reversed(range(n)):
-        alone[i] = calls[i]["long"] + max([hop(i, j) + alone[j] for j in behind[i]], default=0)
-    urge = [URGE.get(c["writes"][0][0], 0) if c["writes"] else 0 for c in calls]
+        c = calls[i]
+        alone[i] = max([(c["hold"] if c["q"] == calls[j]["q"] == "g" else c["long"] + hop(i, j)) + alone[j] for j in behind[i]], default=c["long"])
     tries = []
     for slack in SLACK:
         way = alone
         for _ in range(PASSES):
-            placed, done = place(before, behind, [w + u for w, u in zip(way, urge)], slack)
+            placed, done = place(before, behind, way, slack)
             tries.append((max(done), placed))
             way = place(behind, before, done, slack)[1]
-    return min(tries)[1]
+    ORDER[n] = polish(calls, before, [set(b) for b in behind], min(tries)[1])
+    return ORDER[n]
 
 
 def rank_program(g, core, T, topo):
@@ -147,7 +306,10 @@ def rank_program(g, core, T, topo):
         return V(n, i, i + 1)
 
     def row(bank, a=0, z=256):
-        return V(bank, a, z)
+        return V("ps", 512 * bank + a, 512 * bank + z)
+
+    def every(n, first, count, st=2):
+        return V(n, first, first + st * (count - 1) + 1, st)
 
     def ind(v, lst):
         return ap(v) if lst is None else ap(v).indirect(ap(lst))
@@ -158,18 +320,18 @@ def rank_program(g, core, T, topo):
     def col(s):
         return ap(s) if isinstance(s, tuple) else s
 
-    def put(q, call, reads, writes, ns, kind="call", hold=None, after=()):
-        calls.append({"q": q, "call": call, "reads": reads, "writes": writes, "long": ns, "hold": ns if hold is None else hold, "kind": kind, "after": after})
+    def put(q, call, reads, writes, cost, kind="call", after=()):
+        calls.append({"q": q, "call": call, "reads": reads, "writes": writes, "cost": cost, "kind": kind, "after": after})
         return len(calls) - 1
 
-    def cycles(n, each, lst=None):
-        return 60 + 1.25 * n if lst is not None else 0.83 * max(64, n * each)
+    def cycles(n, each, lst=None, more=0):
+        return ("gather", n) if lst is not None else ("plain", 0.83 * max(64, n * each) + more)
 
     def narrow(*v):
-        return 0.5 if all(SCRATCH[x[0]][2] in ("bfloat16", "uint16") for x in v) else 1
+        return 0.5 if all(x[0] != "ps" and SCRATCH[x[0]][2] in ("bfloat16", "uint16") for x in v) else 1
 
-    def dma(q, out, in_, reads, writes, ns=LOAD):
-        put(q, lambda: Q[q].dma_start(out, in_), reads, writes, ns, "dma", 60)
+    def dma(q, out, in_, reads, writes, later=0):
+        put(q, lambda: Q[q].dma_start(out, in_), reads, writes, ("load", later), "dma")
 
     def fill(v, c):
         put("v", lambda: g.vector.memset(ap(v), c), [], [v], cycles(size(v), narrow(v)))
@@ -180,17 +342,17 @@ def rank_program(g, core, T, topo):
 
     def tt(out, in0, in1, op, lst=None):
         put("v", lambda: g.vector.tensor_tensor(ap(out), ind(in0, lst), ap(in1), op), some(in0, in1, lst), [out],
-            cycles(size(out), 1 if in0[0] in PSUM else 2, lst))
+            cycles(size(out), 1 if in0[0] == "ps" else TT, lst))
 
     def scan(out, d0, d1, op0, op1, init=0.0):
         put("v", lambda: g.vector.tensor_tensor_scan(ap(out), ap(d0), ap(d1), col(init), op0, op1), some(d0, d1, init), [out],
-            cycles(size(out), narrow(out, d0, d1)))
+            cycles(size(out), SCAN[narrow(out, d0, d1) == 1] if SCAN else SC * narrow(out, d0, d1)))
 
     def copy(out, in_, lst=None):
         put("v", lambda: g.vector.tensor_copy(ap(out), ind(in_, lst)), some(in_, lst), [out], cycles(size(out), narrow(out, in_), lst))
 
     def scatter(win, lst, in_):
-        put("v", lambda: g.vector.tensor_copy(ind(win, lst), ap(in_)), [in_, lst], [win], 50 + 3 * size(in_))
+        put("v", lambda: g.vector.tensor_copy(ind(win, lst), ap(in_)), [in_, lst], [win], ("scatter", size(in_)))
 
     def act(out, in_, scale=1.0, lst=None, func=AF.Copy, bias=None, total_to=None):
         k = {} if scale == 1.0 else {"scale": col(scale)}
@@ -199,33 +361,40 @@ def rank_program(g, core, T, topo):
         if total_to is not None:
             k["accum_out"] = ap(total_to)
         put("s", lambda: g.scalar.activation(ap(out), ind(in_, lst), func, **k), some(in_, lst, bias, scale), some(out, total_to),
-            cycles(size(out), 1, lst) + (20 if total_to else 0))
+            cycles(size(out), 1, lst, SUM if total_to else 0))
 
-    def lay(v, c):
-        act(v, V("half", 0, size(v)), 2 * c) if c != 0.5 else act(v, V("half", 0, size(v)))
+    def pick(out, in_, lst):
+        act(out, in_, lst=lst)
 
-    def diagonal(out, in_):
-        put("g", lambda: g.affine_select(ap(out), ap(in_), [[0, size(out) // 128], [1, 128]], A.is_equal, 0.0, 0, -1), [in_], [out], 170 + 1.66 * size(out))
+    def line(out, in_, scale, bias):
+        act(out, in_, scale, func=AF.Identity, bias=bias)
+
+    def lay(v, c=0.0):
+        zero = V("w2t", 768, 768 + size(v))
+        line(v, zero, 0.0, c) if c else act(v, zero)
+
+    def carry(out, in_, after):
+        put("g", lambda: g.affine_select(ap(out), ap(in_), [[0, size(out)]], A.is_gt, 0.0, 1, 0), [in_], [out], ("plain", 170 + 1.66 * size(out)), after=[after])
 
     def turn(out, in_):
         put("v", lambda: g.vector.transpose(ap(out), ap(in_)), [in_], [out], cycles(size(out), narrow(out)))
 
     def quant(n, tile, lo=0, hi=None):
         c, z = V("q" + n, lo, hi), V("z" + n, lo, hi)
-        put("v", lambda: g.vector.quantize_mx(ap(c), ap(z), ap(tile)), [tile], [c, z], 12 + 0.22 * size(tile))
+        put("v", lambda: g.vector.quantize_mx(ap(c), ap(z), ap(tile)), [tile], [c, z], ("plain", 12 + 0.22 * size(tile)))
 
     def mm(bank, cols, L, R, start=True, stop=True):
         lc, lz = V("q" + L[0], L[1], L[1] + 128), V("z" + L[0], L[1], L[1] + 128)
         rc, rz = V("q" + R[0], R[1], R[1] + cols), V("z" + R[0], R[1], R[1] + cols)
-        out = V(bank, 0, cols)
-        put("t", lambda: g.tensor.matmul_mx(ap(out), ap(lc), ap(lz), ap(rc), ap(rz), start, stop), [lc, lz, rc, rz], [out], 0.83 * (cols + 16),
+        out = row(bank, 0, cols)
+        put("t", lambda: g.tensor.matmul_mx(ap(out), ap(lc), ap(lz), ap(rc), ap(rz), start, stop), [lc, lz, rc, rz], [out], ("tensor", cols + 16),
             "call" if start else "adds")
 
-    def iota(out, pattern, base, cm, small=False):
+    def iota(out, pattern, base, cm, small=True):
         k = {"allow_small_or_imprecise_dtypes": True} if small else {}
-        put("g", lambda: g.iota(ap(out), pattern, base, cm, **k), [], [out], 130 + 1.66 * size(out))
+        return put("g", lambda: g.iota(ap(out), pattern, base, cm, **k), [], [out], ("plain", 130 + 1.66 * size(out)))
 
-    def send(pairs, sem, ns):
+    def send(pairs, sem, ns, after):
         rid, pid = topo.addr(nxt)[:2]
 
         def raw(v):
@@ -234,229 +403,334 @@ def rank_program(g, core, T, topo):
         def call():
             for there, here in pairs:
                 g.remote_dma(raw(there), raw(here), T.sem[sem], T.sem["left"], pid, rid, topo.mask(core, nxt))
-        mine = [i for i, c in enumerate(calls) if c["q"] == "g"]
-        sent = put("g", call, [p[1] for p in pairs], [], ns, "send", 200, mine)
-        put("r", sem, [], [p[0] for p in pairs], 0, "arrives", after=[sent])
+        sent = put("g", call, [p[1] for p in pairs], [], (ns, len(pairs)), "send", after)
+        put("r", sem, [], [p[0] for p in pairs], ("plain", 0), "arrives", after=[sent])
+        return sent
 
-    I = {n: one("ci", i) for i, n in enumerate(("p", "r", "m", "s", "g", "h", "b"))}
-    F = {n: one("fc", i) for i, n in enumerate(("r", "m", "s", "g", "h", "b", "p", "gs", "m7", "thr", "val", "lo", "csg", "far", "a0",
-                                                "a1", "a2", "k0", "k1", "t0", "t1", "one", "nine", "ths", "low"))}
+    I = {n: one("ci", i) for i, n in enumerate(("p", "p17", "r", "g", "far"))}
+    F = {n: one("fc", i) for i, n in enumerate(("p", "p17", "r", "g", "far", "odd", "s", "m", "sp", "nsp", "msp", "spm", "up", "down", "t", "lo", "val",
+                                                "r256", "r257", "a0", "a1", "a2", "g16", "up8", "mn", "m1", "m2"))}
 
     dma("y", T["ut"][:, :], T.u[:, :], [], [V("ut")])
-    dma("s", T["xt"][:, 0:512], T.x[:, 0:512], [], [V("xt", 0, 512)])
-    dma("y", T["xt"][:, 512:1024], T.x[:, 512:1024], [], [V("xt", 512, 1024)], LOAD + 600)
-    dma("y", T["cfi"][:, :], T.cf[:, :], [V("ut"), V("xt")], [V("cfi")])
-    dma("y", T["qw"][:, :].bitcast(dt.uint8), T.wc[:, :], [V("ut"), V("xt")], [V("qw")])
-    dma("y", T["zw"][:, :], T.ws[:, :], [V("ut"), V("xt")], [V("zw")])
-    dma("y", T["vt"][:, :], T.v[:, :], [V("ut"), V("xt")], [V("vt")])
+    dma(XQ, T["xt"][:, 0:512], T.x[:, 0:512], [], [V("xt", 0, 512)], 300)
+    dma("y", T["xt"][:, 512:1024], T.x[:, 512:1024], [], [V("xt", 512, 1024)], 800)
+    dma("y", T["cfi"][:, :], T.cf[:, :], [], [V("cfi")], 1100)
 
-    iota(I["p"], [[0, 1]], 0, 1)
-    iota(V("j16"), [[0, 16], [1, 16]], 0, 0, True)
-    iota(V("irow"), [[1, 256]], 0, 0, True)
-    iota(V("kr"), [[16, 16]], 15, 0, True)
-    fill(V("half"), 0.5)
-    put("g", lambda: g.affine_select(T["ebt"][:, :], T["half"][:, :], [[1, 528]], A.is_equal, 0.0, -4, -4), [V("half")], [V("ebt")], 1050)
+    def later(behind):
+        dma("y", T["qw"][:, :].bitcast(dt.uint8), T.wc[:, :], behind, [V("qw")], 600)
+        dma("y", T["zw"][:, :], T.ws[:, :], behind, [V("zw")], 800)
+        dma("y", T["vt"][:, :], T.v[:, :], behind, [V("vt")], 1200)
+        quant("v", V("vt"))
+    if not LATE:
+        later([V("ut"), V("xt")])
+
+    iota(I["p"], [[0, 1]], 0, 1, False)
+    iota(I["p17"], [[0, 1]], 0, 17, False)
+    iota(V("irow", 0, 128), [[1, 128]], 0, 0)
+    iota(V("k16", 0, 128), [[0, 8], [256, 16]], 0, 0)
+    iota(V("kq"), [[16, 16], [0, 16]], 0, 0)
+    iota(V("kt"), [[0, 130], [-1, 2], [0, 2]], 1, 0)
+    mine = []
+    low = V("irow", 0, 128)
+    line(V("irow", 128), low, 1.0, 128.0)
+    act(V("k16", 128, 256), V("k16", 0, 128))
+    act(V("k16", 256), V("k16", 0, 64))
+    ts(I["r"], I["p"], 15, None, A.bitwise_and)
+    ts(I["g"], I["p"], 4, None, A.arith_shift_right)
+    ts(I["far"], I["p17"], 4, 1, A.arith_shift_right, A.bitwise_and)
+    copy(V("fc", 0, 5), V("ci", 0, 5))
+    line(F["odd"], F["p"], -2.0, -1.0)
+    act(F["g16"], F["g"], 16.0)
+    fill(V("ebt"), 0.0)
+    fill(V("w2t", 512), 0.0)
+    for v in (V("w0t", 832), V("w1t", 576, 768), V("w2t", 320, 512)) + (() if GG else (every("s2", 0, 256),)) + (every("alt", 1, 128, 4), one("alt", 0), one("acc", 255),
+              V("vf", 0, 16), V("vf", 272, 288), V("cn", 0, 16), V("cn", 272)):
+        lay(v)
+    if not GG:
+        lay(every("tri", 0, 128), -BIG)
+    if not HOLD:
+        lay(every("n2", 1, 256), 1.0)
+    ts(every("ebt", 4, 128, 4), low, F["p"], 0.5, A.is_equal, A.mult)
     for b in range(4):
         quant("eb", V("ebt", 4 - b, 516 - b), 128 * b, 128 * b + 128)
-    fill(V("kt"), 1.0 / 512)
-    fill(V("kt", 2, 512, 4), -1.0 / 1024)
-    quant("k", V("kt"))
-    for v in (V("w0t", 832), V("w1t", 576), V("w2t", 320)):
-        fill(v, 0.0)
-    for v in (one("nf", 0), one("alt", 0), V("alt", 1, 512, 4), V("alt", 3, 1024, 4), one("acc", 0), V("crow", 0, 16), V("crow", 272), V("vf"), V("orow", 0, 256), V("w3t", 64)):
-        lay(v, 0.0)
-    lay(V("w1t", 512, 576), 0.0)
-    quant("w1", V("w1t", 512), 128, 256)
-    lay(F["nine"], 8.0)
-    iota(V("gst"), [[1, 8], [0, 64]], 0, 0, True)
-    ts(V("ul", 0, 8), V("kr", 0, 8), -15.0, None, A.add)
-    fill(V("ul", 8, 16), 1)
-    ts(I["r"], I["p"], 15, None, A.bitwise_and)
-    ts(I["m"], I["p"], 7, None, A.bitwise_and)
-    ts(I["s"], I["p"], 3, 1, A.arith_shift_right, A.bitwise_and)
-    ts(I["b"], I["p"], 1, None, A.bitwise_and)
-    ts(I["g"], I["p"], 4, None, A.arith_shift_right)
-    ts(I["h"], I["p"], 4, 1, A.arith_shift_right, A.bitwise_and)
-    copy(F["r"], I["r"])
-    copy(F["p"], I["p"])
-    copy(V("fc", 1, 6), V("ci", 2, 7))
-    ts(V("m16"), V("j16"), F["r"], None, A.is_equal)
-    act(V("ka"), V("j16"), func=AF.Sign)
-    lay(F["low"], -BIG)
-    ts(V("kf"), V("j16"), F["r"], None, A.is_gt)
-    act(V("ke"), V("kf"), 2 * BIG, func=AF.Identity, bias=F["low"])
-    act(V("mb"), V("m16"), 2 * BIG, func=AF.Identity, bias=F["low"])
-    ts(V("kq"), V("kr"), F["r"], None, A.subtract)
-    ts(V("gst"), V("gst"), F["g"], None, A.is_equal)
+    quant("w2", V("w2t", 512), 128, 256)
+    if ZD:
+        dma("y", T["qw1"][:, 192:256].bitcast(dt.uint8), T["qw2"][:, 192:256].bitcast(dt.uint8), [V("qw2", 192)], [V("qw1", 192)])
+        dma("y", T["zw1"][:, 192:256], T["zw2"][:, 192:256], [V("zw2", 192)], [V("zw1", 192)])
+    else:
+        quant("w1", V("w2t", 512), 128, 256)
+    quant("k", V("kt", 0, 512), 0, 128)
+    quant("k", V("kt", 2, 514), 128, 256)
+    for c in range(4):
+        ts(every("gst", c, 128, 4), V("kq", 0, 128), F["g16"], -1.0, A.is_equal, A.mult)
     quant("gs", V("gst"))
-    ts(V("eye"), V("irow"), F["p"], None, A.is_equal)
-    ts(V("tru"), V("irow", 0, 128), F["p"], -0.5, A.is_gt, A.add)
-    act(V("tri"), V("tru"), BIG)
-    lay(F["k0"], 0.5 * BIG)
-    lay(F["k1"], -0.5 * BIG)
-    lay(F["one"], 1.0)
-    ts(F["gs"], F["g"], F["s"], 7.0, A.add, A.min)
-    ts(F["m7"], F["m"], 7.0, -128.0, A.is_equal, A.mult)
-    ts(F["t0"], F["m"], F["m7"], 1.0, A.add, A.add)
-    ts(F["t1"], F["m7"], F["gs"], 7.0, A.subtract, A.add)
-    act(F["thr"], F["t0"], 1.0 / 1024)
-    act(F["ths"], F["t0"], -1.0, func=AF.Identity, bias=F["nine"])
-    act(F["lo"], F["m7"], 7.0 / 128, func=AF.Identity, bias=F["t1"])
-    act(F["val"], F["m"], -1.0, func=AF.Identity, bias=F["t1"])
-    act(F["csg"], F["m7"], 1.0 / 64, func=AF.Identity, bias=F["one"])
-    ts(F["far"], F["b"], F["h"], None, A.not_equal)
-    ts(F["a0"], F["m"], 16.0, 7.0, A.mult, A.add)
-    act(F["a1"], F["far"], 144.0, func=AF.Identity, bias=F["a0"])
-    act(F["a2"], F["r"], 16.0)
-    ts(one("at", 0), F["s"], 8.0, F["a1"], A.mult, A.add)
-    ts(one("at", 2), F["s"], 288.0, F["a1"], A.mult, A.add)
-    ts(one("at", 3), one("at", 2), 8.0, None, A.add)
+    copy(V("ul", 0, 8), every("irow", 0, 8, 16))
+    fill(V("ul", 8, 16), 1)
+    run = V("k16", 0, 128)
+    act(F["r256"], F["r"], 256.0)
+    line(F["r257"], F["r"], 256.0, 256.0)
+    ts(V("mb"), run, F["r256"], 2 * BIG, A.not_equal, A.mult)
+    ts(V("kep"), run, 0.0, 2 * BIG, A.is_equal, A.mult)
+    ts(V("ma"), run, F["r257"], WIDE, A.is_equal, A.mult)
+    ts(V("mc"), run, F["r256"], None, A.not_equal)
+    tt(V("m14"), V("ma"), V("mc"), A.max)
+    act(V("eab"), low, 2.0, func=AF.Abs, bias=F["odd"])
+    act(V("eye"), V("eab"), -0.5, func=AF.Relu, bias=1.5)
+    ts(V("tru"), low, F["p"], -0.5, A.is_gt, A.add)
+    act(every("tri", 1, 128), V("tru"), BIG)
+    line(V("kc"), V("kq"), 1.0, F["r"])
+    ts(F["s"], F["r"], 8.0, None, A.is_ge)
+    ts(F["m"], F["s"], -8.0, F["r"], A.mult, A.add)
+    ts(F["sp"], F["r"], 15.0, None, A.is_equal)
+    line(F["nsp"], F["sp"], -1.0, 1.0)
+    line(F["spm"], F["sp"], 1.0, -1.0)
+    act(F["msp"], F["sp"], -1.0)
+    line(F["up"], F["sp"], 1.0 - WIDE, WIDE)
+    if RW == "s":
+        line(F["up8"], F["sp"], (1.0 - WIDE) / 8, WIDE / 8)
+    line(F["down"], F["sp"], 1.0 - 1.0 / WIDE, 1.0 / WIDE)
+    line(F["t"], F["sp"], -100.0, 7.0)
+    ts(F["lo"], F["t"], F["g"], F["s"], A.subtract, A.subtract)
+    ts(F["val"], F["m"], F["spm"], F["lo"], A.mult, A.add)
+    if not CW:
+        lay(every("m2", 0, 256), F["sp"])
+    if HOLD:
+        line(F["mn"], F["sp"], -100.0, F["m"])
+    if "n0" in ONS or "n1" in ONS:
+        ts(F["m2"], F["m"], 7.0, -1000.0, A.is_equal, A.mult)
+        ts(F["m1"], F["m2"], F["m"], 1.0, A.subtract, A.subtract)
+    line(F["a0"], F["m"], 16.0, 7.0)
+    line(F["a1"], F["far"], 144.0, F["a0"])
+    line(F["a2"], F["r"], 16.0, 15.0)
+    ts(one("at", 0), F["s"], 7.0, F["a1"], A.mult, A.add)
+    if len(ZH) < 4:
+        ts(one("at", 2), F["s"], 288.0, F["a1"], A.mult, A.add)
+        ts(one("at", 3), one("at", 2), 7.0, None, A.add)
     ts(one("at", 4), F["far"], 272.0, F["a2"], A.mult, A.add)
-    act(V("k8", 0, 128), V("ka", 0, 256, 2))
-    act(V("k8", 128, 160), V("ka", 0, 64, 2))
     quant("u", V("ut"))
-    quant("v", V("vt"))
-    put("v", lambda: g.vector.tensor_copy(T["qus"][:, :].bitcast(dt.uint32), T["qu"][:, 0:128].bitcast(dt.uint32).indirect(T["ul"][:, :])),
-        [V("qu"), V("ul")], [V("qus")], 380)
-    put("s", lambda: g.scalar.activation(T["zus"][:, :], T["zu"][:, 0:128].indirect(T["ul"][:, :]), AF.Copy), [V("zu"), V("ul")], [V("zus")], 380)
+    for a in (0, 128):
+        def codes(a=a):
+            return g.vector.tensor_copy(T["qus"][:, a:a + 128].bitcast(dt.uint32), T["qu"][:, 0:128].bitcast(dt.uint32).indirect(T["ul"][:, a // 16:a // 16 + 8]))
+
+        def scales(a=a):
+            return g.scalar.activation(T["zus"][:, a:a + 128], T["zu"][:, 0:128].indirect(T["ul"][:, a // 16:a // 16 + 8]), AF.Copy)
+        put("v", codes, [V("qu"), V("ul")], [V("qus", a, a + 128)], cycles(128, 1, 1))
+        put("s", scales, [V("zu"), V("ul")], [V("zus", a, a + 128)], cycles(128, 1, 1))
     copy(V("cu"), V("cfi"))
-    act(V("crow", 16, 272), V("irow"), F["csg"], V("cu"))
 
     for t in range(ROUNDS):
         last = t == ROUNDS - 1
-        tt(V("dc"), V("crow", 15, 271), V("crow", 16, 272), A.subtract)
         X = 256 * t
-        quant("x", V("xt") if t == 0 else V("xn"), X, X + 256)
-        send([(V("qn", X, X + 256), V("qx", X, X + 256)), (V("zn", X, X + 256), V("zx", X, X + 256))], "ax%d" % t, FAR)
-        first = {"p0": (256, ("us", 0), ("x", X)), "p1": (256, ("us", 0), ("x", X)), "p2": (256, ("us", 128), ("x", X)), "p5": (256, ("us", 128), ("x", X)),
-                 "p3": (128, ("x", X), ("u", 0)), "p4": (128, ("x", X + 128), ("u", 0))}
-        for i, bank in enumerate(FIRST if t else FIRST0):
-            mm(bank, *first[bank])
-            calls[-1]["after"] = [len(calls) - 2] if i else []
-        for h, bank in enumerate(("p3", "p4")):
-            same, other = (128 * h, 128 * h + 128), (128 - 128 * h, 256 - 128 * h)
-            act(one("hb", h), one(bank, 1), -1.0)
-            act(V("ht", *same), row("p2", *same), func=AF.Sign, bias=one("hb", h))
-            act(V("hu", *same), V("ht", *same), BIG)
-            tt(V("gg", 384 * h, 384 * h + 128), V("hu", *same), V("tri"), A.add)
-            if CROSS:
-                ts(V("gg", 128 + 128 * h, 256 + 128 * h), row("p5", *other), one(bank, 1), 2 * BIG, (A.is_ge, A.is_gt)[h], A.mult)
-            else:
-                act(V("ht", 256 + 128 * h, 384 + 128 * h), row("p2", *other), func=AF.Sign, bias=one("hb", h))
-                act(V("gg", 128 + 128 * h, 256 + 128 * h), V("ht", 256 + 128 * h, 384 + 128 * h), BIG, func=AF.Identity, bias=F["k%d" % h])
-        for a in (256, 0, 384, 128):
-            scan(V("ll", a, a + 128), V("gg", a, a + 128), row("p5", a % 256, a % 256 + 128), A.add if CROSS and a in (128, 256) else A.max, A.min,
-                 one("ll", a - 1) if a % 256 else -0.75 * BIG)
-        tt(V("nf", 1, 128), row("p5", 1, 128), V("ll", 1, 128), A.not_equal)
-        tt(V("nf", 128, 256), row("p5", 128, 256), V("ll", 384, 512), A.not_equal)
-        tt(V("nf", 256, 384), row("p5", 128, 256), V("ll", 128, 256), A.not_equal)
-        scan(V("alt", 4, 512, 4), V("eye", 1, 128), V("nf", 1, 128), A.max, A.min, one("eye", 0))
-        scan(V("alt", 512, 1024, 4), V("eye", 128, 256), V("nf", 256, 384), A.max, A.min, V("alt", 508, 509, 4))
-        scan(V("alt", 513, 1024, 4), V("eye", 0, 128), V("nf", 128, 256), A.max, A.min)
-        for a, z in DG:
-            diagonal(V("alt", 4 * a + 2, 4 * z, 4), V("nf", a, z))
-        quant("al", V("alt"))
-        for bank in KB:
-            mm(bank, 256, ("k", 0), ("al", 0))
-        act(V("up"), row(KB[-1]), -1024.0, func=AF.Relu, bias=F["nine"])
-        if len(KB) == 2:
-            ts(V("nn"), row(KB[0]), F["thr"], None, A.is_gt)
+        for a, z in ((0, 128), (128, 256)) if SPLIT else ((0, 256),):
+            quant("x", V("xn" if t else "xt", 4 * a, 4 * z), X + a, X + z)
+        if PARTS:
+            send([(V("qn", X, X + 128), V("qx", X, X + 128))], "ay%d" % t, "mid", mine)
+            sent = send([(V("qn", X + 128, X + 256), V("qx", X + 128, X + 256)), (V("zn", X, X + 256), V("zx", X, X + 256))], "ax%d" % t, "mid", [len(calls) - 2])
         else:
-            ts(V("nn"), V("up"), F["ths"], None, A.is_lt)
-        ts(V("mm"), V("up"), F["lo"], F["val"], A.min, A.is_equal)
-        scan(V("cc"), V("dc"), V("nn"), A.add, A.mult)
-        tt(V("cw"), V("cc"), V("mm"), A.mult)
+            sent = send([(V("qn", X, X + 256), V("qx", X, X + 256)), (V("zn", X, X + 256), V("zx", X, X + 256))], "ax%d" % t, "far", mine)
+        if LATE and not t:
+            later([V("zn", 0, 256)])
+        act(every("c2", 0, 256), V("irow"), F["nsp"], V("cu"), AF.Identity, F["sp"])
+        if not HOLD:
+            carry(every("c2", 1, 256), every("c2", 0, 256), sent)
+        first = {"sl": (SL, 128, ("us", 0), ("x", X)), "s2": (RB[0], 128, ("us", 0), ("x", X)), "sv": (SV, 256, ("us", 0), ("x", X)), "ss": (SS, 256, ("us", 0), ("x", X)),
+                 "dl": (DL, 128, ("us", 128), ("x", X)), "du": (DU, 128, ("us", 128), ("x", X + 128)), "df": (DL, 256, ("us", 128), ("x", X)),
+                 "ca": (CA, 128, ("x", X), ("u", 0)), "cb": (CB, 128, ("x", X + 128), ("u", 0))}
+        order = (FIRST if t else FIRST0).split()
+        for i, name in enumerate(order):
+            mm(*first[name])
+            calls[-1]["after"] = [made] if i else []
+            made = len(calls) - 1
+            if name[0] == "c" and (CA == CB or HB2):
+                act(one("hb", int(name == "cb")), one("ps", 512 * first[name][0] + 1))
+        if CA != CB and not HB2:
+            act(V("hb", 0, 2), every("ps", 512 * CA + 1, 2, 512 * (CB - CA)))
+        drive = [row(DL, 0, 128), row(DU, 0, 128) if "du" in order else row(DL, 128, 256)]
+        for h in (0, 1):
+            act(every("s2", 256 * h + 1, 128), drive[h], -1.0, func=AF.Sign, bias=one("hb", h))
+        for h in (0, 1):
+            if GG:
+                big = every("s2", 256 * h, 128)
+                if GG == "s":
+                    act(big, every("s2", 256 * h + 1, 128), -BIG)
+                else:
+                    ts(big, every("s2", 256 * h + 1, 128), -BIG, None, A.mult)
+                tt(every("gg", 256 * h + 1, 128), big, every("tri", 1, 128), A.add)
+            else:
+                scan(V("gg", 256 * h, 256 * h + 256), V("s2", 256 * h, 256 * h + 256), V("tri"), A.mult, A.add)
+        if "go" in ONS:
+            act(V("t2"), drive[0], -1.0, func=AF.Sign, bias=one("hb", 1))
+            act(V("go"), V("t2"), -2 * BIG, func=AF.Relu)
+        else:
+            ts(V("go"), drive[0], one("hb", 1), 2 * BIG, A.is_gt, A.mult)
+        if "t0" in ONS:
+            act(V("t3"), drive[1], -1.0, func=AF.Sign, bias=one("hb", 0))
+            act(V("t0"), V("t3"), 2.0, func=AF.Relu)
+        scan(V("ll", 128, 256), V("go"), drive[0], A.add, A.min, -0.75 * BIG)
+        scan(V("ll", 256, 384), every("gg", 257, 128), drive[1], A.max, A.min, one("ll", 255))
+        scan(V("ll", 0, 128), every("gg", 1, 128), drive[0], A.max, A.min, -0.75 * BIG)
+        tt(V("nf", 0, 128), drive[0], V("ll", 0, 128), A.not_equal)
+        tt(V("nf", 128, 256), drive[1], V("ll", 256, 384), A.not_equal)
+        if "t0" not in ONS:
+            ts(V("t0"), drive[1], one("hb", 0), 2.0, A.is_lt, A.mult)
+        ts(V("t1"), drive[1], one("ll", 127), 2.0, A.is_gt, A.mult)
+        scan(every("alt", 4, 127, 4), V("eye", 1), V("nf", 1, 128), A.add, A.mult, one("eye", 0))
+        scan(every("alt", 3, 128, 4), V("eye"), V("nf", 128, 256), A.add, A.mult)
+        scan(every("alt", 2, 128, 4), V("t0"), V("t1"), A.mult, A.min, one("alt", 508))
+        quant("al", V("alt"))
+        early = SL if "sl" in order else SV
+        for a in OWN:
+            tt(V("sm16", a, a + 128), row(SV if a else early, a, a + 128), V("mb"), A.add)
+            scan(V("own", a, a + 128), V("kep"), V("sm16", a, a + 128), A.add, A.min)
+        tt(V("w0t", 0, 1024, 4), row(SV), V("own"), A.is_gt)
+        scan(V("es"), V("kc"), V("w0t", 0, 1024, 4), A.max, A.add)
+
+        def compare(q, w):
+            own, e, o = one("own", 16 * q + 15), 16 * q, 256 * q
+            if q in VQ:
+                ts(w, row(RB[0] if q <= 8 and "s2" in order else SV, 0, e), own, -1.0, A.is_lt, A.mult)
+                if q in VS:
+                    scan(V("acc", o + 256 - e, o + 256), w, V("k16", 0, e), A.add, A.min)
+                else:
+                    act(V("jk", o, o + e), w, total_to=one("acc", o + 255))
+            else:
+                act(V("jk", o, o + e), row(SL if q <= 8 and "sl" in order else SS, 0, e), -1.0, func=AF.Relu, bias=own)
+                act(w, V("jk", o, o + e), -1.0, func=AF.Sign, total_to=one("acc", o + 255))
+        for i in TILES if APART else ():
+            name, at = "w%d" % min(i, 2), 128 * (i == 3)
+            for q in range(min(15, 16 - 4 * i), 12 - 4 * i, -1):
+                compare(q, every(name + "t", (16 - q) % 4 + 4 * at, 16 * q, 4))
+            wide = (256, 192, 128, 128)[i]
+            quant(name, V(name + "t", 4 * at, 4 * (at + wide)), at, at + wide)
+            mm(RB[0], 128, ("gs", 0), (name, at), i == TILES[0], i == TILES[3])
+            if i < 2:
+                mm(RB[1], 128, ("gs", 0), (name, 128), TILES.index(i) < TILES.index(1 - i), TILES.index(i) > TILES.index(1 - i))
+        for i in () if APART else TILES:
+            name = "w%d" % i
+            for q in ((15, 14, 13), (12, 11, 10, 9), (8, 7, 6, 5, 4, 3, 2, 1))[i]:
+                compare(q, every(name + "t", (16 - q) % 4 + (512 if q < 5 else 0), 16 * q, 4))
+            wide = 192 if i else 256
+            quant(name, V(name + "t", 0, 4 * wide), 0, wide)
+            mm(RB[0], 128, ("gs", 0), (name, 0), i == TILES[0], i == TILES[2] and i < 2)
+            if i < 2:
+                mm(RB[1], 128, ("gs", 0), (name, 128), TILES.index(i) < TILES.index(1 - i), TILES.index(i) > TILES.index(1 - i))
+            else:
+                mm(RB[0], 128, ("gs", 0), (name, 128), False, i == TILES[2])
+        for h in (0, 1):
+            a, o = 128 * h, 256 * h
+            mm(KB[h], 128, ("k", a), ("al", 0))
+            act(V("up", a, a + 128), row(KB[h], 0, 128), -1.0, func=AF.Relu, bias=8.0)
+            if "n%d" % h in ONS:
+                act(V("sel", a, a + 128), row(KB[h], 0, 128), func=AF.Relu, bias=F["m1"])
+                act(every("n2", o, 128), V("sel", a, a + 128), func=AF.Sign)
+            else:
+                ts(every("n2", o, 128), V("up", a, a + 128), F["mn" if HOLD else "m"], 7.0, A.add, A.is_lt)
+            ts(every("m2", o + 1, 128), V("up", a, a + 128), F["lo"], F["val"], A.min, A.is_equal)
+            if HOLD:
+                ts(V("sel", a, a + 128), V("up", a, a + 128), F["m"], 7.0, A.add, A.is_ge)
+                tt(V("cs", a, a + 128), every("c2", o, 128), V("sel", a, a + 128), A.mult)
+                scan(every("h2", o + 1, 128), every("n2", o, 128), V("cs", a, a + 128), A.mult, A.add, one("h2", o - 1) if h else F["msp"])
+            else:
+                scan(V("h2", o, o + 256), V("c2", o, o + 256), V("n2", o, o + 256), A.subtract, A.mult, one("h2", o - 1) if h else 0.0)
+            if CW:
+                tt(every("cw", o + 1, 128), every("h2", o + 1, 128), every("m2", o + 1, 128), A.mult)
+            else:
+                scan(V("cw", o, o + 256), V("h2", o, o + 256), V("m2", o, o + 256), A.add, A.mult, one("cw", o - 1) if h else F["msp"])
         for b, bank in enumerate(FB):
             mm(bank, 256, ("eb", 128 * b), ("x", X))
             act(quarter("f", b), row(bank), 32.0)
-        for a, z in OWN:
-            tt(V("sm16", a, z), row("p0", a, z), V("mb", a, z), A.min)
-            scan(V("own", a, z), V("ke", a, z), V("sm16", a, z), A.min, A.max)
-        tt(V("w0t", 0, 1024, 4), row("p0"), V("own"), A.is_le)
-        scan(V("es"), V("ka"), V("w0t", 0, 1024, 4), A.mult, A.add)
-        for i in TILES:
-            wide = WIDE[i]
-            for c in range(4):
-                q = 16 - 4 * i - c
-                if q == 16:
-                    continue
-                own, e, o = one("own", 16 * q + 15), 16 * q, 256 * q
-                w = V("w%dt" % i, c, 4 * e, 4)
-                if q in VQ:
-                    ts(w, row("p0", 0, e), own, None, A.is_lt)
-                    act(V("jk", o, o + e), w, total_to=one("acc", q))
-                else:
-                    act(V("jk", o, o + e), row("p1", 0, e), -1.0, func=AF.Relu, bias=own)
-                    act(w, V("jk", o, o + e), func=AF.Sign, total_to=one("acc", q))
-            quant("w%d" % i, V("w%dt" % i, 0, 4 * wide), 0, wide)
-            mm(RB[0], 128, ("gs", 0), ("w%d" % i, 0), i == TILES[0], i == TILES[3])
-            if i < 2:
-                mm(RB[1], 128, ("gs", 0), ("w%d" % i, 128), TILES.index(i) < TILES.index(1 - i), TILES.index(i) > TILES.index(1 - i))
         for a, bank in ((128, RB[1]), (0, RB[0])):
-            tt(V("ex", a, a + 128), row(bank, 0, 128), V("m16", 0, 128), A.mult)
-            scan(V("ey", a, a + 128), V("ka", 0, 128), V("ex", a, a + 128), A.mult, A.add)
-        tt(V("ru"), V("kq"), V("es", 15, 256, 16), A.subtract)
-        tt(V("rw"), V("ru"), V("acc"), A.subtract)
-        tt(V("ri"), V("rw"), V("ey", 15, 256, 16), A.add)
-        copy(V("rku"), V("ri"))
-        scatter(V("vf", 16, 272), V("rku"), V("cw"))
+            if "e%d" % (a // 128) in ONS:
+                act(V("ex", a, a + 128), row(bank, 0, 128))
+                scan(V("ey", a, a + 128), V("m14"), V("ex", a, a + 128), A.mult, A.add)
+            else:
+                scan(V("ey", a, a + 128), V("m14"), row(bank, 0, 128), A.mult, A.add)
+        for a, z in ((8, 16), (0, 8)) if TWICE else ((0, 16),):
+            tt(V("r2", a, z), every("es", 16 * a + 15, z - a, 16), every("acc", 256 * a + 255, z - a, 256), A.add)
+            if RW == "s":
+                line(V("rw", a, z), V("r2", a, z), F["up"], F["up8"])
+            else:
+                ts(V("rw", a, z), V("r2", a, z), 0.125, F["up"], A.add, A.mult)
+            tt(V("ri", a, z), V("rw", a, z), every("ey", 16 * a + 15, z - a, 16), A.add)
+            ts(V("rku", a, z), V("ri", a, z), F["down"], None, A.mult)
+            scatter(V("vf", 16, 272), V("rku", a, z), every("cw", 32 * a + 1, 16 * (z - a)))
+        if WRAP == "v":
+            copy(V("vf", 272, 400), V("vf", 16, 144))
+        if WRAP == "g":
+            carry(V("vf", 272, 400), V("vf", 16, 144), sent)
         for half in (0, 1):
             a, o = 128 * half, 288 * half
             for c, z, shift in ((0, 128, 16), (128, 288, 0)):
                 turn(V("tf", o + c, o + z), V("vf", a + shift, a + shift + z - c))
-                scan(V("sm", o + c, o + z), V("k8", 0, z - c), V("tf", o + c, o + z), A.mult, A.add)
+                scan(V("sm", o + c, o + z), every("k16", 0, z - c), V("tf", o + c, o + z), A.min, A.add)
             if half == 0:
                 copy(V("lo", 16 * t, 16 * t + 16), V("sm", 0, 288), V("at", 0, 1))
-        send([(V("li", 16 * t, 16 * t + 16), V("lo", 16 * t, 16 * t + 16))], "al%d" % t, NEAR)
-        copy(V("lab"), V("sm"), V("at", 2, 4))
+        sent = send([(V("li", 16 * t, 16 * t + 16), V("lo", 16 * t, 16 * t + 16))], "al%d" % t, "near", mine)
+        if len(ZH) < 4:
+            copy(V("lab"), V("sm"), V("at", 2, 4))
+        if ZH:
+            copy(V("lal"), V("sm", 288), V("at", 0, 1))
+        for b in ZH:
+            tmp = V("ta", 256 * b, 256 * b + 128)
+            pick(tmp, quarter("f", b), V("lo", 16 * t, 16 * t + 8))
+            tt(V("v32", 256 * b, 256 * b + 128), quarter("f", b), tmp, A.add, lst=V("lo", 16 * t + 8, 16 * t + 16))
         for b in range(4):
-            act(quarter("ta", b), quarter("f", b), lst=V("lab", 0, 16))
-            tt(quarter("v32", b), quarter("f", b), quarter("ta", b), A.add, lst=V("lab", 16, 32))
+            if b in ZH:
+                tmp = V("ta", 256 * b + 128, 256 * b + 256)
+                (copy if b in TAV else pick)(tmp, quarter("f", b), V("lal", 0, 8))
+                tt(V("v32", 256 * b + 128, 256 * b + 256), quarter("f", b), tmp, A.add, lst=V("lal", 8, 16))
+            else:
+                (copy if b in TAV else pick)(quarter("ta", b), quarter("f", b), V("lab", 0, 16))
+                tt(quarter("v32", b), quarter("f", b), quarter("ta", b), A.add, lst=V("lab", 16, 32))
         for b, bank in enumerate(NB):
             mm(bank, 256, ("eb", 128 * b), ("n", X))
             act(quarter("fn", b), row(bank))
         for b in range(4):
             tmp = V("tb", 128 * b, 128 * b + 128)
-            act(tmp, quarter("fn", b), lst=V("li", 16 * t, 16 * t + 8))
+            (copy if b in TBV else pick)(tmp, quarter("fn", b), V("li", 16 * t, 16 * t + 8))
             tt(V("et", b, 512, 4), quarter("fn", b), tmp, A.add, lst=V("li", 16 * t + 8, 16 * t + 16))
         quant("e", V("et"))
-        scatter(V("orow", 0, 256), V("rku"), V("irow"))
-        act(V("orow", 256, 384), V("orow", 0, 128))
-        act(V("sg", 0, 256), V("orow", 128, 384), lst=V("rku"))
+        if WRAP == "s":
+            act(V("vf", 272, 400), V("vf", 16, 144))
+        act(V("sg"), V("vf", 144, 400), lst=V("rku"))
         if last:
-            act(V("cop"), V("sg", 0, 256), lst=V("cu"))
-            dma("y", T.op[:, :], T["cop"][0:128:16, :], [V("cop")], [])
+            act(V("cop"), V("sg"), lst=V("cu"))
+            dma("y", T.op[:, :], T["cop"][15:128:16, :], [V("cop")], [])
         else:
-            act(V("crow", 16, 272), V("sg", 0, 256), F["csg"], V("cu"))
-            turn(V("tc", 0, 256), V("crow", 16, 272))
-            turn(V("tc", 256, 544), V("crow"))
+            act(V("cn", 16, 272), V("sg"), lst=V("cu"))
+            turn(V("tc", 0, 256), V("cn", 16, 272))
+            turn(V("tc", 256, 544), V("cn"))
             copy(V("cu"), V("tc"), V("at", 4, 5))
-        for b, bank in enumerate(("p0", "p1", "p7", "p3")):
+        for b, bank in enumerate(LB):
             low = V("v32", 256 * b + 128, 256 * b + 256)
             mm(bank, 128, ("w", 128 * b), ("e", 0))
-            tt(low, V(bank, 0, 128), low, A.add)
-        for a, z in ((0, 8), (8, 16)) if last and HALVES else ((0, 16),):
-            for b in range(4):
-                out, win, lst = V("xn", 64 * a + b, 64 * z, 4), quarter("v32", b), V("rku", a, z)
-                if b in XS:
+            tt(low, row(bank, 0, 128), low, A.add)
+        for b, who in enumerate((XL if last else XS).split()):
+            for c, d in ((0, 8), (8, 16)) if len(who) == 2 else ((0, 16),):
+                out, win, lst = V("xn", 64 * c + b, 64 * d, 4), quarter("v32", b), V("rku", c, d)
+                if who[c // 8] == "s":
                     act(out, win, scale=0.03125, lst=lst)
                 else:
                     ts(out, win, 0.03125, None, A.mult, lst=lst)
 
     X = 256 * ROUNDS
-    for a, z, bank in ((0, 128, "p4"), (128, 256, "p5")) if HALVES else ((0, 256, "p4"),):
+    for a, z, bank in ((0, 128, 0), (128, 256, 1)) if HALVES else ((0, 256, 0),):
         quant("x", V("xn", 4 * a, 4 * z), X + a, X + z)
         mm(bank, z - a, ("v", 0), ("x", X + a))
-        (copy if a else act)(V("ys", a, z), V(bank, 0, z - a))
-        dma("y" if a else "s", T.y[:, a:z], T["ys"][:, a:z], [V("ys", a, z)], [])
-    dma("y", T.oc[:, :], T["qx"][:, X:X + 256].bitcast(dt.uint8), [V("qx", X)], [])
+        calls[-1]["after"] = [len(calls) - 4] if a else []
+        (copy if a else act)(V("ys", a, z), row(bank, 0, z - a))
+    for a, z in ((0, 128), (128, 256)) if YH else ((0, 256),):
+        dma(TAIL[int(a > 0)], T.y[:, a:z], T["ys"][:, a:z], [V("ys", a, z)], [], 400 if a or not YH else 900)
+    for a, z in ((0, 128), (128, 256)) if OH else ((0, 256),):
+        dma("y", T.oc[:, 4 * a:4 * z], T["qx"][:, X + a:X + z].bitcast(dt.uint8), [V("qx", X + a, X + z)], [], 1000)
     for i in range(4):
-        dma("y" if i % 2 else "s", T.osc[4 * i:4 * i + 4, :], T["zx"][32 * i:32 * i + 4, X:X + 256], [V("zx", X)], [])
+        dma(TAIL[2 + i], T.osc[4 * i:4 * i + 4, :], T["zx"][32 * i:32 * i + 4, X:X + 256], [V("zx", X)], [])
 
     total = {}
     know = {q: {} for q in Q}
     seen = {}
-    for i in arrange(calls):
+    loads = [i for i, c in enumerate(calls) if c["kind"] == "dma" and not c["reads"]]
+    for i in loads + [i for i in arrange(calls) if i not in loads]:
         c = calls[i]
         q, kind = c["q"], c["kind"]
         if kind == "arrives":

import math
import numpy as np
from concourse.mybir import dt, AluOpType as A, ActivationFunctionType as AF

ROUNDS = 3
RW, SC = "v", 1
SCAN, SUM = (1.0, 1.2), 70
LATE, PARTS = False, False
ONS = ()
XQ, YH, OH, ZD = "s", False, False, False
SPLIT, TWICE, ZH = True, False, ()
XL = "ss ss sv vv"
XS = "ss ss sv vv"
VQ = (12, 11, 4, 3, 2, 1)
VS = VQ
TAV, TBV = (0,), (3,)
WRAP = "v"
APART = False
BIG = 2.0 ** 90
WIDE = 2.0 ** 14
TILES = (2, 1, 0)
HALVES = True
OWN = (0, 128)
DIRECT = False
SL, SV, SS, DL, DU, CA, CB = 0, 5, 1, 2, 4, 3, 3
RB, KB, FB, NB, LB = (6, 7), (2, 4), (3, 0, 5, 3), (1, 2, 4, 0), (6, 7, 3, 5)
FIRST = "sl ca dl s2 sv cb du ss"
FIRST0 = FIRST
PACES = [dict(slow=1.0, call=15, wait=180, gather=1.0, pick=110, scatter=1.6, tensor=0.9, far=3500, near=1200, load=1500, first=2000, issue=100),
         dict(slow=1.0, call=30, wait=110, gather=0.9, pick=90, scatter=2.2, tensor=1.0, far=4200, near=1400, load=1800, first=1000, issue=300),
         dict(slow=1.3, call=10, wait=220, gather=1.25, pick=80, scatter=3.0, tensor=1.2, far=5000, near=1700, load=1700, first=2000, issue=200)]
SLACK, PASSES = (30, 90), 2
MOVES, HEAT = 30000, 0.0001
ORDER = {}

SPLIT, OWN, TILES, FIRST, CB, XS, XL, HALVES = False, (128, 0), (1, 0, 2), "sv ca cb df ss", 4, "s v s v", "s v s v", False
FIRST0, KB, FB, NB, LB, TAV, TBV = FIRST, (2, 3), (4, 5, 4, 5), (1, 2, 3, 0), (6, 7, 4, 5), (0,), ()
VQ = VS = (8, 7, 6, 5, 4, 3, 2, 1)
SCAN, SUM = (0.75, 1.0), 40
PACES = [dict(slow=1.0, call=30, wait=180, gather=1.15, pick=70, scatter=2.4, tensor=1.0, far=3800, near=1300, load=1600, first=1500, issue=100),
         dict(slow=1.0, call=50, wait=120, gather=0.9, pick=90, scatter=1.6, tensor=0.9, far=3300, near=1100, load=1400, first=1000, issue=300),
         dict(slow=1.3, call=20, wait=240, gather=1.3, pick=70, scatter=3.2, tensor=1.3, far=4800, near=1700, load=1900, first=2000, issue=200)]

HB2 = False
TAIL = "sysysy"
GG, HOLD, CW = "s", True, True
GG, HOLD, CW, SCAN, TT, SUM = None, False, False, None, 2, 30
VQ = VS = (12, 11, 4, 3, 2, 1)
SPLIT, OWN, TILES, FIRST, CB, XS, XL, HALVES = True, (0, 128), (2, 1, 0), "sl ca dl s2 sv cb du ss", 3, "ss ss sv vv", "ss ss sv vv", True
FIRST0, KB, FB, NB, LB, TAV, TBV, ZH = FIRST, (2, 4), (3, 0, 5, 3), (1, 2, 4, 0), (6, 7, 3, 5), (), (3,), (0, 1, 2, 3)
SCAN, SUM = (1.0, 1.1), 50
VS, XS, TILES, MOVES = (4, 3, 2, 1), "ss sv sv vv", (2, 0, 1), 90000
SCAN, SUM, XQ, MOVES, TT, CALLS = (0.72, 1.27), 30, "s", 60000, 1.45, "vs"
PACES = [dict(slow=1.0, call=15, wait=190, s=25, t=60, own=10, gather=0.88, pick=80, scatter=2.5, tensor=0.85, far=2700, near=1150, load=2100, first=800, issue=60),
         dict(slow=1.0, call=12, wait=172, s=10, t=110, own=35, gather=0.95, pick=85, scatter=2.2, tensor=0.92, far=3200, near=1250, load=1900, first=1500, issue=60),
         dict(slow=1.35, call=14, wait=210, s=25, t=90, own=25, gather=1.2, pick=80, scatter=2.9, tensor=1.3, far=5400, near=1700, load=2100, first=1500, issue=100)]
TAIL, YH, OH = "ssyyyy", True, True
WRAP, RW, ONS, MOVES = "v", "v", (), 70000
TAIL, YH, OH, SCAN, SUM, TT, CALLS = "sysysy", False, False, (1.0, 1.15), 50, 2, "s"
PACES = [dict(slow=1.0, call=15, wait=240, own=50, gather=0.9, pick=62, scatter=2.2, tensor=0.85, far=4000, near=1250, load=1650, first=1000, issue=60),
         dict(slow=1.0, call=25, wait=205, own=80, gather=1.1, pick=62, scatter=1.6, tensor=1.0, far=2800, near=1100, load=1500, first=1500, issue=100),
         dict(slow=1.35, call=15, wait=270, own=50, gather=1.25, pick=62, scatter=3.2, tensor=1.2, far=5200, near=1600, load=1900, first=1500, issue=100)]
SCRATCH = {"ps": ("psum", [128, 4096], "float32")}
for _n, _c in [("u", 128), ("v", 128), ("w", 512), ("us", 256), ("x", 1024), ("eb", 512), ("k", 256), ("gs", 128), ("w0", 256), ("w1", 256), ("w2", 256), ("al", 128),
               ("e", 128), ("n", 768)]:
    SCRATCH["q" + _n] = ("sbuf", [128, _c], "float8_e4m3fn_x4")
    SCRATCH["z" + _n] = ("sbuf", [128, _c], "uint8")
for _d, _l in [("bfloat16", [("ut", 512), ("vt", 512), ("xt", 1024), ("xn", 1024), ("ebt", 528), ("kt", 520), ("gst", 512), ("irow", 256), ("k16", 320), ("kq", 256), ("kc", 256),
                             ("mb", 128), ("kep", 128), ("m14", 128), ("ma", 128), ("mc", 128), ("eye", 128), ("eab", 128), ("tri", 256), ("tru", 128),
                             ("s2", 512), ("gg", 512), ("go", 128), ("t0", 128), ("t1", 128), ("t2", 128), ("t3", 128), ("sel", 256), ("cs", 256), ("ex", 256), ("ey", 256), ("nf", 256), ("alt", 512), ("up", 256),
                             ("n2", 512), ("m2", 512), ("c2", 512), ("h2", 512), ("cw", 512), ("es", 256),
                             ("w0t", 1024), ("w1t", 1024), ("w2t", 1024), ("jk", 4096), ("f", 1024), ("sg", 256), ("cn", 288),
                             ("vf", 400), ("tf", 576), ("sm", 576), ("tc", 544),
                             ("ta", 1024), ("et", 512), ("tb", 512), ("fn", 1024), ("v32", 1024)]),
               ("float32", [("sm16", 256), ("own", 256), ("ll", 384), ("cop", 256), ("ys", 256), ("fc", 32), ("hb", 8), ("rw", 16),
                            ("acc", 4096), ("r2", 16), ("ri", 16)]),
               ("int32", [("ci", 16), ("cfi", 16)]),
               ("uint16", [("ul", 16), ("at", 6), ("cu", 16), ("rku", 16), ("lab", 32), ("lal", 16), ("lo", 48), ("li", 48)])]:
    for _n, _c in _l:
        SCRATCH[_n] = ("sbuf", [128, _c], _d)

SEMAPHORES = ["cv", "cs", "ct", "left"] + ["g%d" % i for i in range(24)] + [a + str(t) for a in ("ax", "ay", "al") for t in range(ROUNDS)] + ["d%d" % i for i in range(20)]


def last_of(v):
    return v[1] + (v[2] - 1 - v[1]) // v[3] * v[3]


def meet(a, b):
    if a[4] >= b[5] or b[4] >= a[5] or a[1] >= b[2] or b[1] >= a[2]:
        return False
    return not (a[3] == b[3] and (a[1] - b[1]) % a[3])


def one_bank(a, b):
    return a[1] // 512 <= last_of(b) // 512 and b[1] // 512 <= last_of(a) // 512


def covers(v, o):
    return o[1] >= v[1] and o[2] <= v[2] and o[4] >= v[4] and o[5] <= v[5] and (v[3] == 1 or (v[3] == o[3] and (v[1] - o[1]) % v[3] == 0))


def follows(seen, q, reads, writes):
    for v, w in [(r, False) for r in reads] + [(r, True) for r in writes]:
        for e in seen.get(v[0], []):
            if ((w or e[1] or e[2] != q) and one_bank(v, e[0])) if v[0] == "ps" else ((w or e[1]) and meet(v, e[0])):
                yield e


def remember(seen, q, reads, writes, who):
    for v, w in [(r, False) for r in reads] + [(r, True) for r in writes]:
        L = seen.setdefault(v[0], [])
        if w:
            L[:] = [e for e in L if not covers(v, e[0])]
        L.append((v, w, q, who))


def lengths(c, pace, first):
    what, n = c["cost"]
    if what == "load":
        return pace["load"] + n, pace["issue"]
    if what == "mid":
        return 0.8 * pace["far"] + first, 200 * n + first
    if what in ("far", "near"):
        return pace[what] + first, 200 * n + first
    ns = pace["slow"] * (n + pace["call"] * (c["q"] in CALLS) if what == "plain" else pace[what] * n + pace["pick"] * (what != "tensor"))
    return ns, ns


def polish(calls, before, behind, order):
    n = len(calls)
    above = []
    for i in range(n):
        a = 0
        for j in before[i]:
            a |= above[j] | 1 << j
        above.append(a)
    q = [c["q"] for c in calls]
    timed = [[j for j in before[i] if not (q[i] == q[j] in "tg")] for i in range(n)]
    timed = [[j for j in t if not any(above[k] >> j & 1 for k in t)] for t in timed]
    sent = min(i for i in range(n) if calls[i]["kind"] == "send")
    paces = []
    for p in PACES:
        L = [lengths(calls[i], p, p["first"] if i == sent else 0) for i in range(n)]
        paces.append(([x[0] + (0 if calls[i]["kind"] == "send" else p["wait"] + p.get(q[i], 0)) for i, x in enumerate(L)], [x[1] for x in L], p.get("own", 0)))
    cross = [[j for j in timed[i] if q[j] != q[i]] for i in range(n)]
    same = [[j for j in timed[i] if q[j] == q[i]] for i in range(n)]

    def ahead(order):
        last, prev = {}, [n] * n
        for i in order:
            if q[i] != "r":
                prev[i], last[q[i]] = last.get(q[i], n), i
        return prev

    def run(order, prev, start, state):
        new, total = [], 0.0
        rest = order[start:]
        for (long, hold, own), (there, free, unit) in zip(paces, state):
            there, free = there[:], free[:]
            for i in rest:
                t = free[prev[i]]
                for j in cross[i]:
                    if there[j] > t:
                        t = there[j]
                for j in same[i]:
                    if there[j] + own > t:
                        t = there[j] + own
                free[i], there[i] = t + hold[i], t + long[i]
            new.append((there, free, unit))
            total += max(there) / unit
        return total / len(paces), new

    def chain(order, prev, state, m):
        there, free, _ = state[m]
        hold = paces[m][1]
        i, pairs = there.index(max(there)), []
        while True:
            t = free[i] - hold[i]
            if prev[i] < n and abs(free[prev[i]] - t) < 1e-6:
                pairs.append((prev[i], i))
                i = prev[i]
                continue
            back = [j for j in timed[i] if abs(there[j] + paces[m][2] * (q[j] == q[i]) - t) < 1e-6]
            if not back:
                return pairs
            i = back[0]
    dice = np.random.RandomState(1)
    prev = ahead(order)
    state = run(order, prev, 0, [([0.0] * n, [0.0] * (n + 1), 1.0) for _ in paces])[1]
    state = [(a, b, max(a)) for a, b, _ in state]
    now = best = 1.0
    kept = list(order)
    throws = dice.random_sample((MOVES, 5)).tolist()
    for move, (r0, r1, r2, r3, r4) in enumerate(throws):
        if move % 8 == 0:
            m = move // 8 % len(paces)
            at = {i: a for a, i in enumerate(order)}
            order.sort(key=lambda i: (state[m][1][i] - paces[m][1][i], at[i]))
            pairs = chain(order, prev, state, m)
        step = 1 if r1 < 0.5 else -1
        a = order.index(pairs[int(r2 * len(pairs))][step < 0]) if r0 < 0.7 else int(r2 * n)
        i, far, b, to = order[a], (1, 1, 1, 2, 3, 5, 8)[int(r3 * 7)], a, a
        stop = before[i] if step < 0 else behind[i]
        while far and 0 <= b + step < n and order[b + step] not in stop:
            b += step
            if q[order[b]] == q[i]:
                far, to = far - 1, b
        if to == a or q[i] == "r":
            continue
        other = order[:a] + order[a + 1:]
        other.insert(to, i)
        prev2 = ahead(other)
        end, state2 = run(other, prev2, min(a, to), state)
        if end <= now - HEAT * (1.0 - move / MOVES) * math.log(r4 + 1e-12):
            order, prev, state, now = other, prev2, state2, end
            if end < best:
                best, kept = end, list(other)
    ORDER["best"] = [best] + [best * s[2] for s in state]
    return kept


def arrange(calls):
    if len(calls) in ORDER:
        return ORDER[len(calls)]
    for c in calls:
        c["long"], c["hold"] = lengths(c, PACES[0], 0)
    HOP = PACES[0]["wait"]
    seen, before = {}, []
    for i, c in enumerate(calls):
        before.append({e[3] for e in follows(seen, c["q"], c["reads"], c["writes"])} | set(c["after"]))
        remember(seen, c["q"], c["reads"], c["writes"], i)
    n = len(calls)
    behind = [[] for _ in range(n)]
    for i in range(n):
        for j in before[i]:
            behind[j].append(i)

    def hop(j, i):
        return 0 if calls[j]["q"] == calls[i]["q"] in "tg" or calls[i]["q"] == "r" else HOP

    def place(first, then, way, slack):
        left = [len(b) for b in first]
        ready, done, free, placed, open_ = [0.0] * n, [0.0] * n, {}, [], {}
        for i in range(n):
            if not left[i]:
                open_.setdefault(calls[i]["q"], []).append(i)
        while len(placed) < n:
            q = min((k for k in open_ if open_[k]), key=lambda k: max(free.get(k, 0), min(ready[i] for i in open_[k])))
            now = max(free.get(q, 0), min(ready[i] for i in open_[q]))
            i = max(open_[q], key=lambda i: way[i] - max(0, ready[i] - now))
            if ready[i] > now:
                fits = [j for j in open_[q] if ready[j] <= now and now + calls[j]["hold"] <= ready[i] + (slack if q in "vs" else 0)]
                if not fits:
                    free[q] = min(ready[j] for j in open_[q] if ready[j] > now)
                    continue
                i = max(fits, key=lambda j: way[j])
            open_[q].remove(i)
            free[q], done[i] = now + calls[i]["hold"], now + calls[i]["long"]
            placed.append(i)
            for j in then[i]:
                ready[j] = max(ready[j], free[q] if q == calls[j]["q"] == "g" else done[i] + hop(i, j))
                left[j] -= 1
                if not left[j]:
                    open_.setdefault(calls[j]["q"], []).append(j)
        return placed, done
    alone = [0.0] * n
    for i in reversed(range(n)):
        c = calls[i]
        alone[i] = max([(c["hold"] if c["q"] == calls[j]["q"] == "g" else c["long"] + hop(i, j)) + alone[j] for j in behind[i]], default=c["long"])
    tries = []
    for slack in SLACK:
        way = alone
        for _ in range(PASSES):
            placed, done = place(before, behind, way, slack)
            tries.append((max(done), placed))
            way = place(behind, before, done, slack)[1]
    ORDER[n] = polish(calls, before, [set(b) for b in behind], min(tries)[1])
    return ORDER[n]


def rank_program(g, core, T, topo):
    rank = T.rank_of(core)
    if rank is None:
        return
    nxt = T.cores[(rank + 1) % len(T.cores)]
    prv = T.cores[(rank - 1) % len(T.cores)]
    Q = {"v": g.vector, "s": g.scalar, "t": g.tensor, "g": g, "y": g.sync}
    calls = []

    def V(name, lo=0, hi=None, st=1, p0=0, p1=128):
        return (name, lo, SCRATCH[name][1][1] if hi is None else hi, st, p0, p1)

    def ap(v):
        name, lo, hi, st, p0, p1 = v
        c = slice(lo, hi) if st == 1 else slice(lo, hi, st)
        return T[name][:, c] if (p0, p1) == (0, 128) else T[name][p0:p1, c]

    def size(v):
        return len(range(v[1], v[2], v[3]))

    def quarter(n, b):
        return V(n, 256 * b, 256 * b + 256)

    def one(n, i):
        return V(n, i, i + 1)

    def row(bank, a=0, z=256):
        return V("ps", 512 * bank + a, 512 * bank + z)

    def every(n, first, count, st=2):
        return V(n, first, first + st * (count - 1) + 1, st)

    def ind(v, lst):
        return ap(v) if lst is None else ap(v).indirect(ap(lst))

    def some(*v):
        return [x for x in v if isinstance(x, tuple)]

    def col(s):
        return ap(s) if isinstance(s, tuple) else s

    def put(q, call, reads, writes, cost, kind="call", after=()):
        calls.append({"q": q, "call": call, "reads": reads, "writes": writes, "cost": cost, "kind": kind, "after": after})
        return len(calls) - 1

    def cycles(n, each, lst=None, more=0):
        return ("gather", n) if lst is not None else ("plain", 0.83 * max(64, n * each) + more)

    def narrow(*v):
        return 0.5 if all(x[0] != "ps" and SCRATCH[x[0]][2] in ("bfloat16", "uint16") for x in v) else 1

    def dma(q, out, in_, reads, writes, later=0):
        put(q, lambda: Q[q].dma_start(out, in_), reads, writes, ("load", later), "dma")

    def fill(v, c):
        put("v", lambda: g.vector.memset(ap(v), c), [], [v], cycles(size(v), narrow(v)))

    def ts(out, in0, s1, s2, op0, op1=None, lst=None):
        a = [col(s1), col(s2), op0] + ([] if op1 is None else [op1])
        put("v", lambda: g.vector.tensor_scalar(ap(out), ind(in0, lst), *a), some(in0, s1, s2, lst), [out], cycles(size(out), narrow(out, in0), lst))

    def tt(out, in0, in1, op, lst=None):
        put("v", lambda: g.vector.tensor_tensor(ap(out), ind(in0, lst), ap(in1), op), some(in0, in1, lst), [out],
            cycles(size(out), 1 if in0[0] == "ps" else TT, lst))

    def scan(out, d0, d1, op0, op1, init=0.0):
        put("v", lambda: g.vector.tensor_tensor_scan(ap(out), ap(d0), ap(d1), col(init), op0, op1), some(d0, d1, init), [out],
            cycles(size(out), SCAN[narrow(out, d0, d1) == 1] if SCAN else SC * narrow(out, d0, d1)))

    def copy(out, in_, lst=None):
        put("v", lambda: g.vector.tensor_copy(ap(out), ind(in_, lst)), some(in_, lst), [out], cycles(size(out), narrow(out, in_), lst))

    def scatter(win, lst, in_):
        put("v", lambda: g.vector.tensor_copy(ind(win, lst), ap(in_)), [in_, lst], [win], ("scatter", size(in_)))

    def act(out, in_, scale=1.0, lst=None, func=AF.Copy, bias=None, total_to=None):
        k = {} if scale == 1.0 else {"scale": col(scale)}
        if bias is not None:
            k["bias"] = col(bias)
        if total_to is not None:
            k["accum_out"] = ap(total_to)
        put("s", lambda: g.scalar.activation(ap(out), ind(in_, lst), func, **k), some(in_, lst, bias, scale), some(out, total_to),
            cycles(size(out), 1, lst, SUM if total_to else 0))

    def pick(out, in_, lst):
        act(out, in_, lst=lst)

    def line(out, in_, scale, bias):
        act(out, in_, scale, func=AF.Identity, bias=bias)

    def lay(v, c=0.0):
        zero = V("w2t", 768, 768 + size(v))
        line(v, zero, 0.0, c) if c else act(v, zero)

    def carry(out, in_, after):
        put("g", lambda: g.affine_select(ap(out), ap(in_), [[0, size(out)]], A.is_gt, 0.0, 1, 0), [in_], [out], ("plain", 170 + 1.66 * size(out)), after=[after])

    def turn(out, in_):
        put("v", lambda: g.vector.transpose(ap(out), ap(in_)), [in_], [out], cycles(size(out), narrow(out)))

    def quant(n, tile, lo=0, hi=None):
        c, z = V("q" + n, lo, hi), V("z" + n, lo, hi)
        put("v", lambda: g.vector.quantize_mx(ap(c), ap(z), ap(tile)), [tile], [c, z], ("plain", 12 + 0.22 * size(tile)))

    def mm(bank, cols, L, R, start=True, stop=True):
        lc, lz = V("q" + L[0], L[1], L[1] + 128), V("z" + L[0], L[1], L[1] + 128)
        rc, rz = V("q" + R[0], R[1], R[1] + cols), V("z" + R[0], R[1], R[1] + cols)
        out = row(bank, 0, cols)
        put("t", lambda: g.tensor.matmul_mx(ap(out), ap(lc), ap(lz), ap(rc), ap(rz), start, stop), [lc, lz, rc, rz], [out], ("tensor", cols + 16),
            "call" if start else "adds")

    def iota(out, pattern, base, cm, small=True):
        k = {"allow_small_or_imprecise_dtypes": True} if small else {}
        return put("g", lambda: g.iota(ap(out), pattern, base, cm, **k), [], [out], ("plain", 130 + 1.66 * size(out)))

    def send(pairs, sem, ns, after):
        rid, pid = topo.addr(nxt)[:2]

        def raw(v):
            return ap(v).bitcast(dt.uint8) if v[0][0] == "q" else ap(v)

        def call():
            for there, here in pairs:
                g.remote_dma(raw(there), raw(here), T.sem[sem], T.sem["left"], pid, rid, topo.mask(core, nxt))
        sent = put("g", call, [p[1] for p in pairs], [], (ns, len(pairs)), "send", after)
        put("r", sem, [], [p[0] for p in pairs], ("plain", 0), "arrives", after=[sent])
        return sent

    I = {n: one("ci", i) for i, n in enumerate(("p", "p17", "r", "g", "far"))}
    F = {n: one("fc", i) for i, n in enumerate(("p", "p17", "r", "g", "far", "odd", "s", "m", "sp", "nsp", "msp", "spm", "up", "down", "t", "lo", "val",
                                                "r256", "r257", "a0", "a1", "a2", "g16", "up8", "mn", "m1", "m2"))}

    dma("y", T["ut"][:, :], T.u[:, :], [], [V("ut")])
    dma(XQ, T["xt"][:, 0:512], T.x[:, 0:512], [], [V("xt", 0, 512)], 300)
    dma("y", T["xt"][:, 512:1024], T.x[:, 512:1024], [], [V("xt", 512, 1024)], 800)
    dma("y", T["cfi"][:, :], T.cf[:, :], [], [V("cfi")], 1100)

    def later(behind):
        dma("y", T["qw"][:, :].bitcast(dt.uint8), T.wc[:, :], behind, [V("qw")], 600)
        dma("y", T["zw"][:, :], T.ws[:, :], behind, [V("zw")], 800)
        dma("y", T["vt"][:, :], T.v[:, :], behind, [V("vt")], 1200)
        quant("v", V("vt"))
    if not LATE:
        later([V("ut"), V("xt")])

    iota(I["p"], [[0, 1]], 0, 1, False)
    iota(I["p17"], [[0, 1]], 0, 17, False)
    iota(V("irow", 0, 128), [[1, 128]], 0, 0)
    iota(V("k16", 0, 128), [[0, 8], [256, 16]], 0, 0)
    iota(V("kq"), [[16, 16], [0, 16]], 0, 0)
    iota(V("kt"), [[0, 130], [-1, 2], [0, 2]], 1, 0)
    mine = []
    low = V("irow", 0, 128)
    line(V("irow", 128), low, 1.0, 128.0)
    act(V("k16", 128, 256), V("k16", 0, 128))
    act(V("k16", 256), V("k16", 0, 64))
    ts(I["r"], I["p"], 15, None, A.bitwise_and)
    ts(I["g"], I["p"], 4, None, A.arith_shift_right)
    ts(I["far"], I["p17"], 4, 1, A.arith_shift_right, A.bitwise_and)
    copy(V("fc", 0, 5), V("ci", 0, 5))
    line(F["odd"], F["p"], -2.0, -1.0)
    act(F["g16"], F["g"], 16.0)
    fill(V("ebt"), 0.0)
    fill(V("w2t", 512), 0.0)
    for v in (V("w0t", 832), V("w1t", 576, 768), V("w2t", 320, 512)) + (() if GG else (every("s2", 0, 256),)) + (every("alt", 1, 128, 4), one("alt", 0), one("acc", 255),
              V("vf", 0, 16), V("vf", 272, 288), V("cn", 0, 16), V("cn", 272)):
        lay(v)
    if not GG:
        lay(every("tri", 0, 128), -BIG)
    if not HOLD:
        lay(every("n2", 1, 256), 1.0)
    ts(every("ebt", 4, 128, 4), low, F["p"], 0.5, A.is_equal, A.mult)
    for b in range(4):
        quant("eb", V("ebt", 4 - b, 516 - b), 128 * b, 128 * b + 128)
    quant("w2", V("w2t", 512), 128, 256)
    if ZD:
        dma("y", T["qw1"][:, 192:256].bitcast(dt.uint8), T["qw2"][:, 192:256].bitcast(dt.uint8), [V("qw2", 192)], [V("qw1", 192)])
        dma("y", T["zw1"][:, 192:256], T["zw2"][:, 192:256], [V("zw2", 192)], [V("zw1", 192)])
    else:
        quant("w1", V("w2t", 512), 128, 256)
    quant("k", V("kt", 0, 512), 0, 128)
    quant("k", V("kt", 2, 514), 128, 256)
    for c in range(4):
        ts(every("gst", c, 128, 4), V("kq", 0, 128), F["g16"], -1.0, A.is_equal, A.mult)
    quant("gs", V("gst"))
    copy(V("ul", 0, 8), every("irow", 0, 8, 16))
    fill(V("ul", 8, 16), 1)
    run = V("k16", 0, 128)
    act(F["r256"], F["r"], 256.0)
    line(F["r257"], F["r"], 256.0, 256.0)
    ts(V("mb"), run, F["r256"], 2 * BIG, A.not_equal, A.mult)
    ts(V("kep"), run, 0.0, 2 * BIG, A.is_equal, A.mult)
    ts(V("ma"), run, F["r257"], WIDE, A.is_equal, A.mult)
    ts(V("mc"), run, F["r256"], None, A.not_equal)
    tt(V("m14"), V("ma"), V("mc"), A.max)
    act(V("eab"), low, 2.0, func=AF.Abs, bias=F["odd"])
    act(V("eye"), V("eab"), -0.5, func=AF.Relu, bias=1.5)
    ts(V("tru"), low, F["p"], -0.5, A.is_gt, A.add)
    act(every("tri", 1, 128), V("tru"), BIG)
    line(V("kc"), V("kq"), 1.0, F["r"])
    ts(F["s"], F["r"], 8.0, None, A.is_ge)
    ts(F["m"], F["s"], -8.0, F["r"], A.mult, A.add)
    ts(F["sp"], F["r"], 15.0, None, A.is_equal)
    line(F["nsp"], F["sp"], -1.0, 1.0)
    line(F["spm"], F["sp"], 1.0, -1.0)
    act(F["msp"], F["sp"], -1.0)
    line(F["up"], F["sp"], 1.0 - WIDE, WIDE)
    if RW == "s":
        line(F["up8"], F["sp"], (1.0 - WIDE) / 8, WIDE / 8)
    line(F["down"], F["sp"], 1.0 - 1.0 / WIDE, 1.0 / WIDE)
    line(F["t"], F["sp"], -100.0, 7.0)
    ts(F["lo"], F["t"], F["g"], F["s"], A.subtract, A.subtract)
    ts(F["val"], F["m"], F["spm"], F["lo"], A.mult, A.add)
    if not CW:
        lay(every("m2", 0, 256), F["sp"])
    if HOLD:
        line(F["mn"], F["sp"], -100.0, F["m"])
    if "n0" in ONS or "n1" in ONS:
        ts(F["m2"], F["m"], 7.0, -1000.0, A.is_equal, A.mult)
        ts(F["m1"], F["m2"], F["m"], 1.0, A.subtract, A.subtract)
    line(F["a0"], F["m"], 16.0, 7.0)
    line(F["a1"], F["far"], 144.0, F["a0"])
    line(F["a2"], F["r"], 16.0, 15.0)
    ts(one("at", 0), F["s"], 7.0, F["a1"], A.mult, A.add)
    if len(ZH) < 4:
        ts(one("at", 2), F["s"], 288.0, F["a1"], A.mult, A.add)
        ts(one("at", 3), one("at", 2), 7.0, None, A.add)
    ts(one("at", 4), F["far"], 272.0, F["a2"], A.mult, A.add)
    quant("u", V("ut"))
    for a in (0, 128):
        def codes(a=a):
            return g.vector.tensor_copy(T["qus"][:, a:a + 128].bitcast(dt.uint32), T["qu"][:, 0:128].bitcast(dt.uint32).indirect(T["ul"][:, a // 16:a // 16 + 8]))

        def scales(a=a):
            return g.scalar.activation(T["zus"][:, a:a + 128], T["zu"][:, 0:128].indirect(T["ul"][:, a // 16:a // 16 + 8]), AF.Copy)
        put("v", codes, [V("qu"), V("ul")], [V("qus", a, a + 128)], cycles(128, 1, 1))
        put("s", scales, [V("zu"), V("ul")], [V("zus", a, a + 128)], cycles(128, 1, 1))
    copy(V("cu"), V("cfi"))

    for t in range(ROUNDS):
        last = t == ROUNDS - 1
        X = 256 * t
        for a, z in ((0, 128), (128, 256)) if SPLIT else ((0, 256),):
            quant("x", V("xn" if t else "xt", 4 * a, 4 * z), X + a, X + z)
        if PARTS:
            send([(V("qn", X, X + 128), V("qx", X, X + 128))], "ay%d" % t, "mid", mine)
            sent = send([(V("qn", X + 128, X + 256), V("qx", X + 128, X + 256)), (V("zn", X, X + 256), V("zx", X, X + 256))], "ax%d" % t, "mid", [len(calls) - 2])
        else:
            sent = send([(V("qn", X, X + 256), V("qx", X, X + 256)), (V("zn", X, X + 256), V("zx", X, X + 256))], "ax%d" % t, "far", mine)
        if LATE and not t:
            later([V("zn", 0, 256)])
        act(every("c2", 0, 256), V("irow"), F["nsp"], V("cu"), AF.Identity, F["sp"])
        if not HOLD:
            carry(every("c2", 1, 256), every("c2", 0, 256), sent)
        first = {"sl": (SL, 128, ("us", 0), ("x", X)), "s2": (RB[0], 128, ("us", 0), ("x", X)), "sv": (SV, 256, ("us", 0), ("x", X)), "ss": (SS, 256, ("us", 0), ("x", X)),
                 "dl": (DL, 128, ("us", 128), ("x", X)), "du": (DU, 128, ("us", 128), ("x", X + 128)), "df": (DL, 256, ("us", 128), ("x", X)),
                 "ca": (CA, 128, ("x", X), ("u", 0)), "cb": (CB, 128, ("x", X + 128), ("u", 0))}
        order = (FIRST if t else FIRST0).split()
        for i, name in enumerate(order):
            mm(*first[name])
            calls[-1]["after"] = [made] if i else []
            made = len(calls) - 1
            if name[0] == "c" and (CA == CB or HB2):
                act(one("hb", int(name == "cb")), one("ps", 512 * first[name][0] + 1))
        if CA != CB and not HB2:
            act(V("hb", 0, 2), every("ps", 512 * CA + 1, 2, 512 * (CB - CA)))
        drive = [row(DL, 0, 128), row(DU, 0, 128) if "du" in order else row(DL, 128, 256)]
        for h in (0, 1):
            act(every("s2", 256 * h + 1, 128), drive[h], -1.0, func=AF.Sign, bias=one("hb", h))
        for h in (0, 1):
            if GG:
                big = every("s2", 256 * h, 128)
                if GG == "s":
                    act(big, every("s2", 256 * h + 1, 128), -BIG)
                else:
                    ts(big, every("s2", 256 * h + 1, 128), -BIG, None, A.mult)
                tt(every("gg", 256 * h + 1, 128), big, every("tri", 1, 128), A.add)
            else:
                scan(V("gg", 256 * h, 256 * h + 256), V("s2", 256 * h, 256 * h + 256), V("tri"), A.mult, A.add)
        if "go" in ONS:
            act(V("t2"), drive[0], -1.0, func=AF.Sign, bias=one("hb", 1))
            act(V("go"), V("t2"), -2 * BIG, func=AF.Relu)
        else:
            ts(V("go"), drive[0], one("hb", 1), 2 * BIG, A.is_gt, A.mult)
        if "t0" in ONS:
            act(V("t3"), drive[1], -1.0, func=AF.Sign, bias=one("hb", 0))
            act(V("t0"), V("t3"), 2.0, func=AF.Relu)
        scan(V("ll", 128, 256), V("go"), drive[0], A.add, A.min, -0.75 * BIG)
        scan(V("ll", 256, 384), every("gg", 257, 128), drive[1], A.max, A.min, one("ll", 255))
        scan(V("ll", 0, 128), every("gg", 1, 128), drive[0], A.max, A.min, -0.75 * BIG)
        tt(V("nf", 0, 128), drive[0], V("ll", 0, 128), A.not_equal)
        tt(V("nf", 128, 256), drive[1], V("ll", 256, 384), A.not_equal)
        if "t0" not in ONS:
            ts(V("t0"), drive[1], one("hb", 0), 2.0, A.is_lt, A.mult)
        ts(V("t1"), drive[1], one("ll", 127), 2.0, A.is_gt, A.mult)
        scan(every("alt", 4, 127, 4), V("eye", 1), V("nf", 1, 128), A.add, A.mult, one("eye", 0))
        scan(every("alt", 3, 128, 4), V("eye"), V("nf", 128, 256), A.add, A.mult)
        scan(every("alt", 2, 128, 4), V("t0"), V("t1"), A.mult, A.min, one("alt", 508))
        quant("al", V("alt"))
        early = SL if "sl" in order else SV
        for a in OWN:
            tt(V("sm16", a, a + 128), row(SV if a else early, a, a + 128), V("mb"), A.add)
            scan(V("own", a, a + 128), V("kep"), V("sm16", a, a + 128), A.add, A.min)
        tt(V("w0t", 0, 1024, 4), row(SV), V("own"), A.is_gt)
        scan(V("es"), V("kc"), V("w0t", 0, 1024, 4), A.max, A.add)

        def compare(q, w):
            own, e, o = one("own", 16 * q + 15), 16 * q, 256 * q
            if q in VQ:
                ts(w, row(RB[0] if q <= 8 and "s2" in order else SV, 0, e), own, -1.0, A.is_lt, A.mult)
                if q in VS:
                    scan(V("acc", o + 256 - e, o + 256), w, V("k16", 0, e), A.add, A.min)
                else:
                    act(V("jk", o, o + e), w, total_to=one("acc", o + 255))
            else:
                act(V("jk", o, o + e), row(SL if q <= 8 and "sl" in order else SS, 0, e), -1.0, func=AF.Relu, bias=own)
                act(w, V("jk", o, o + e), -1.0, func=AF.Sign, total_to=one("acc", o + 255))
        for i in TILES if APART else ():
            name, at = "w%d" % min(i, 2), 128 * (i == 3)
            for q in range(min(15, 16 - 4 * i), 12 - 4 * i, -1):
                compare(q, every(name + "t", (16 - q) % 4 + 4 * at, 16 * q, 4))
            wide = (256, 192, 128, 128)[i]
            quant(name, V(name + "t", 4 * at, 4 * (at + wide)), at, at + wide)
            mm(RB[0], 128, ("gs", 0), (name, at), i == TILES[0], i == TILES[3])
            if i < 2:
                mm(RB[1], 128, ("gs", 0), (name, 128), TILES.index(i) < TILES.index(1 - i), TILES.index(i) > TILES.index(1 - i))
        for i in () if APART else TILES:
            name = "w%d" % i
            for q in ((15, 14, 13), (12, 11, 10, 9), (8, 7, 6, 5, 4, 3, 2, 1))[i]:
                compare(q, every(name + "t", (16 - q) % 4 + (512 if q < 5 else 0), 16 * q, 4))
            wide = 192 if i else 256
            quant(name, V(name + "t", 0, 4 * wide), 0, wide)
            mm(RB[0], 128, ("gs", 0), (name, 0), i == TILES[0], i == TILES[2] and i < 2)
            if i < 2:
                mm(RB[1], 128, ("gs", 0), (name, 128), TILES.index(i) < TILES.index(1 - i), TILES.index(i) > TILES.index(1 - i))
            else:
                mm(RB[0], 128, ("gs", 0), (name, 128), False, i == TILES[2])
        for h in (0, 1):
            a, o = 128 * h, 256 * h
            mm(KB[h], 128, ("k", a), ("al", 0))
            act(V("up", a, a + 128), row(KB[h], 0, 128), -1.0, func=AF.Relu, bias=8.0)
            if "n%d" % h in ONS:
                act(V("sel", a, a + 128), row(KB[h], 0, 128), func=AF.Relu, bias=F["m1"])
                act(every("n2", o, 128), V("sel", a, a + 128), func=AF.Sign)
            else:
                ts(every("n2", o, 128), V("up", a, a + 128), F["mn" if HOLD else "m"], 7.0, A.add, A.is_lt)
            ts(every("m2", o + 1, 128), V("up", a, a + 128), F["lo"], F["val"], A.min, A.is_equal)
            if HOLD:
                ts(V("sel", a, a + 128), V("up", a, a + 128), F["m"], 7.0, A.add, A.is_ge)
                tt(V("cs", a, a + 128), every("c2", o, 128), V("sel", a, a + 128), A.mult)
                scan(every("h2", o + 1, 128), every("n2", o, 128), V("cs", a, a + 128), A.mult, A.add, one("h2", o - 1) if h else F["msp"])
            else:
                scan(V("h2", o, o + 256), V("c2", o, o + 256), V("n2", o, o + 256), A.subtract, A.mult, one("h2", o - 1) if h else 0.0)
            if CW:
                tt(every("cw", o + 1, 128), every("h2", o + 1, 128), every("m2", o + 1, 128), A.mult)
            else:
                scan(V("cw", o, o + 256), V("h2", o, o + 256), V("m2", o, o + 256), A.add, A.mult, one("cw", o - 1) if h else F["msp"])
        for b, bank in enumerate(FB):
            mm(bank, 256, ("eb", 128 * b), ("x", X))
            act(quarter("f", b), row(bank), 32.0)
        for a, bank in ((128, RB[1]), (0, RB[0])):
            if "e%d" % (a // 128) in ONS:
                act(V("ex", a, a + 128), row(bank, 0, 128))
                scan(V("ey", a, a + 128), V("m14"), V("ex", a, a + 128), A.mult, A.add)
            else:
                scan(V("ey", a, a + 128), V("m14"), row(bank, 0, 128), A.mult, A.add)
        for a, z in ((8, 16), (0, 8)) if TWICE else ((0, 16),):
            tt(V("r2", a, z), every("es", 16 * a + 15, z - a, 16), every("acc", 256 * a + 255, z - a, 256), A.add)
            if RW == "s":
                line(V("rw", a, z), V("r2", a, z), F["up"], F["up8"])
            else:
                ts(V("rw", a, z), V("r2", a, z), 0.125, F["up"], A.add, A.mult)
            tt(V("ri", a, z), V("rw", a, z), every("ey", 16 * a + 15, z - a, 16), A.add)
            ts(V("rku", a, z), V("ri", a, z), F["down"], None, A.mult)
            scatter(V("vf", 16, 272), V("rku", a, z), every("cw", 32 * a + 1, 16 * (z - a)))
        if WRAP == "v":
            copy(V("vf", 272, 400), V("vf", 16, 144))
        if WRAP == "g":
            carry(V("vf", 272, 400), V("vf", 16, 144), sent)
        for half in (0, 1):
            a, o = 128 * half, 288 * half
            for c, z, shift in ((0, 128, 16), (128, 288, 0)):
                turn(V("tf", o + c, o + z), V("vf", a + shift, a + shift + z - c))
                scan(V("sm", o + c, o + z), every("k16", 0, z - c), V("tf", o + c, o + z), A.min, A.add)
            if half == 0:
                copy(V("lo", 16 * t, 16 * t + 16), V("sm", 0, 288), V("at", 0, 1))
        sent = send([(V("li", 16 * t, 16 * t + 16), V("lo", 16 * t, 16 * t + 16))], "al%d" % t, "near", mine)
        if len(ZH) < 4:
            copy(V("lab"), V("sm"), V("at", 2, 4))
        if ZH:
            copy(V("lal"), V("sm", 288), V("at", 0, 1))
        for b in ZH:
            tmp = V("ta", 256 * b, 256 * b + 128)
            pick(tmp, quarter("f", b), V("lo", 16 * t, 16 * t + 8))
            tt(V("v32", 256 * b, 256 * b + 128), quarter("f", b), tmp, A.add, lst=V("lo", 16 * t + 8, 16 * t + 16))
        for b in range(4):
            if b in ZH:
                tmp = V("ta", 256 * b + 128, 256 * b + 256)
                (copy if b in TAV else pick)(tmp, quarter("f", b), V("lal", 0, 8))
                tt(V("v32", 256 * b + 128, 256 * b + 256), quarter("f", b), tmp, A.add, lst=V("lal", 8, 16))
            else:
                (copy if b in TAV else pick)(quarter("ta", b), quarter("f", b), V("lab", 0, 16))
                tt(quarter("v32", b), quarter("f", b), quarter("ta", b), A.add, lst=V("lab", 16, 32))
        for b, bank in enumerate(NB):
            mm(bank, 256, ("eb", 128 * b), ("n", X))
            act(quarter("fn", b), row(bank))
        for b in range(4):
            tmp = V("tb", 128 * b, 128 * b + 128)
            (copy if b in TBV else pick)(tmp, quarter("fn", b), V("li", 16 * t, 16 * t + 8))
            tt(V("et", b, 512, 4), quarter("fn", b), tmp, A.add, lst=V("li", 16 * t + 8, 16 * t + 16))
        quant("e", V("et"))
        if WRAP == "s":
            act(V("vf", 272, 400), V("vf", 16, 144))
        act(V("sg"), V("vf", 144, 400), lst=V("rku"))
        if last:
            act(V("cop"), V("sg"), lst=V("cu"))
            dma("y", T.op[:, :], T["cop"][15:128:16, :], [V("cop")], [])
        else:
            act(V("cn", 16, 272), V("sg"), lst=V("cu"))
            turn(V("tc", 0, 256), V("cn", 16, 272))
            turn(V("tc", 256, 544), V("cn"))
            copy(V("cu"), V("tc"), V("at", 4, 5))
        for b, bank in enumerate(LB):
            low = V("v32", 256 * b + 128, 256 * b + 256)
            mm(bank, 128, ("w", 128 * b), ("e", 0))
            tt(low, row(bank, 0, 128), low, A.add)
        for b, who in enumerate((XL if last else XS).split()):
            for c, d in ((0, 8), (8, 16)) if len(who) == 2 else ((0, 16),):
                out, win, lst = V("xn", 64 * c + b, 64 * d, 4), quarter("v32", b), V("rku", c, d)
                if who[c // 8] == "s":
                    act(out, win, scale=0.03125, lst=lst)
                else:
                    ts(out, win, 0.03125, None, A.mult, lst=lst)

    X = 256 * ROUNDS
    for a, z, bank in ((0, 128, 0), (128, 256, 1)) if HALVES else ((0, 256, 0),):
        quant("x", V("xn", 4 * a, 4 * z), X + a, X + z)
        mm(bank, z - a, ("v", 0), ("x", X + a))
        calls[-1]["after"] = [len(calls) - 4] if a else []
        (copy if a else act)(V("ys", a, z), row(bank, 0, z - a))
    for a, z in ((0, 128), (128, 256)) if YH else ((0, 256),):
        dma(TAIL[int(a > 0)], T.y[:, a:z], T["ys"][:, a:z], [V("ys", a, z)], [], 400 if a or not YH else 900)
    for a, z in ((0, 128), (128, 256)) if OH else ((0, 256),):
        dma("y", T.oc[:, 4 * a:4 * z], T["qx"][:, X + a:X + z].bitcast(dt.uint8), [V("qx", X + a, X + z)], [], 1000)
    for i in range(4):
        dma(TAIL[2 + i], T.osc[4 * i:4 * i + 4, :], T["zx"][32 * i:32 * i + 4, X:X + 256], [V("zx", X)], [])

    total = {}
    know = {q: {} for q in Q}
    seen = {}
    loads = [i for i, c in enumerate(calls) if c["kind"] == "dma" and not c["reads"]]
    for i in loads + [i for i in arrange(calls) if i not in loads]:
        c = calls[i]
        q, kind = c["q"], c["kind"]
        if kind == "arrives":
            total[c["call"]] = len(c["writes"]) * len(topo.engines(prv, core))
            remember(seen, q, [], c["writes"], (c["call"], total[c["call"]], {}))
            continue
        need = {}
        for e in follows(seen, q, c["reads"], c["writes"] if kind != "adds" else []):
            sem, n, theirs = e[3]
            if need.get(sem, (0, 0))[0] < n:
                need[sem] = (n, theirs)
        for sem, (n, theirs) in need.items():
            if know[q].get(sem, 0) < n:
                Q[q].wait_ge(T.sem[sem], n)
                for s, k in list(theirs.items()) + [(sem, n)]:
                    know[q][s] = max(know[q].get(s, 0), k)
        if kind == "send":
            c["call"]()
            total["left"] = total.get("left", 0) + len(c["reads"]) * len(topo.engines(core, nxt))
            continue
        own = "d" if kind == "dma" else "g" if q == "g" else None
        sem, n = (own + str(len([s for s in total if s[0] == own])) if own else "c" + q), (16 if kind == "dma" else 1)
        c["call"]().then_inc(T.sem[sem], n)
        total[sem] = total.get(sem, 0) + n
        remember(seen, q, c["reads"], c["writes"], (sem, total[sem], dict(know[q])))
    for sem, n in total.items():
        g.wait_ge(T.sem[sem], n)
